import numpy as np, ml_dtypes
CORES = [48,51,52,55]
N = 4
import mx_ref
BF = ml_dtypes.bfloat16
def gentries(a):
    return np.ascontiguousarray(a.reshape(8, 16, -1).transpose(0, 2, 1)).reshape(8, -1)
def gtable(e):
    e = np.asarray(e); return np.ascontiguousarray(e.reshape(8, -1, 16).transpose(0, 2, 1)).reshape(128, -1).astype(np.int32)
def gcols(t, e):
    v = np.concatenate([t.reshape(8, 16, -1, 4), np.zeros((8, 16, 1, 4), BF)], axis=2)
    return np.ascontiguousarray(np.stack([v[g][:, e[g]] for g in range(8)])).reshape(128, -1)
def tile(rs):
    return np.stack(rs, axis=2).reshape(128, -1).astype(BF)
def pick(q, e):
    c = np.concatenate([q[0].reshape(128, -1, 4), np.zeros((128, 1, 4), np.uint8)], axis=1); s = np.concatenate([q[1], np.ones((16, 1), np.uint8)], axis=1)
    return (np.ascontiguousarray(c[:, e].reshape(128, -1)), np.ascontiguousarray(s[:, e]))
def join(*qs):
    return (np.concatenate([q[0] for q in qs], axis=1), np.concatenate([q[1] for q in qs], axis=1))
def put(q, e, v):
    c, s = q[0].reshape(128, -1, 4).copy(), q[1].copy(); c[:, e] = v[0].reshape(128, -1, 4); s[:, e] = v[1]
    return (c.reshape(128, -1), s)
def pk(c, s):
    return (np.ascontiguousarray(c), mx_ref.live(s))
def emit(q):
    return q[0], q[1]
def packed(v, rng):
    q = [mx_ref.quantize(np.ascontiguousarray(v[r])) for r in range(N)]
    return np.stack([a for a, b in q]), np.stack([mx_ref.plane(b, rng) for a, b in q])
def values_of_codes():
    e, c = np.zeros((128, 128, 4), np.float32), np.zeros((128, 2, 4), np.uint8)
    e[np.arange(128), np.arange(128), 0] = 1
    c[:127, :, 0] = np.arange(256).reshape(2, 128).T[:127]
    return mx_ref.matmul(mx_ref.quantize(e.reshape(128, 512).astype(BF)), (c.reshape(128, 8), np.full((16, 2), 127, np.uint8))).T.reshape(-1).astype(np.float64)
CODE_VALUE, SCALE_VALUE = values_of_codes(), 2.0 ** (np.arange(256) - 127.0)
def decode(q):
    return (CODE_VALUE[q[0]].reshape(16, 8, -1, 4) * SCALE_VALUE[q[1]][:, None, :, None] + 0.0).reshape(128, -1).astype(np.float32)
def f(rng, *shape):
    return mx_ref.flush((rng.standard_normal(shape, dtype=np.float32) * np.exp2(rng.integers(-2, 3, shape[:-1] + (1,)))).astype(BF))
def wide(rng, *shape, cols=0):
    v = rng.standard_normal(shape, dtype=np.float32) * np.exp2(rng.integers(-12, 13, shape)).astype(np.float32)
    if cols: v *= np.repeat(np.exp2(rng.integers(-cols, cols + 1, shape[:-2] + (1, shape[-1] // 4))) * (rng.random(shape[:-2] + (1, shape[-1] // 4)) > 0.0625), 4, axis=-1).astype(np.float32)
    return mx_ref.flush(v.astype(BF))
C, STAGES = 480, 5
STEP = [1, 2, 3]
def numbers_of(rng):
    return {"x": np.array(f(rng, N, 128, 4 * C)), "u": np.array(f(rng, N, 128, 512)), "v": np.array(f(rng, N, 128, 512))}
def stored(a, b, s):
    return {"ta": np.stack([gtable(a[r]) for r in range(N)]), "tb": np.stack([gtable(b[r]) for r in range(N)]), "st": np.stack([gtable(s[r]) for r in range(N)])}
def lists(rng):
    e = np.tile(np.arange(C), (N, 8, 1))
    return stored(rng.permuted(e, axis=2), rng.permuted(e, axis=2), rng.permuted(e, axis=2))
def layers(rng):
    return np.array(f(rng, N, 128, 2048)).reshape(N, 8, 16, 4, 8, 16, 4)
def weights(rng, w):
    c, p = packed(np.ascontiguousarray(w).reshape(N, 128, 2048), rng)
    return {"wc": c, "ws": p}
def setup_inputs(rng):
    return {**numbers_of(rng), **lists(rng), **weights(rng, layers(rng))}
def setup_inputs_ties(rng):
    d = numbers_of(rng)
    o = rng.permutation(N)
    k = rng.integers(-1, 2, (2, N, 8, C)).astype(np.float32)
    k[0, o[1]] = 1
    x = d["x"].reshape(N, 8, 16, C, 4)
    x[:, :, [0, 1, 8]] = 0
    x[:, :, 0, :, 0] = k[0].astype(BF)
    x[:, :, 1, :, 0] = k[1].astype(BF)
    c = np.ones(N, np.float32)
    c[o[0]] = 0
    c[o[2]] = -1
    u = d["u"].reshape(N, 128, 128, 4)
    u[:, :, ::16] = 0
    for h in range(0, 128, 16):
        u[:, h, h, 0] = c.astype(BF)
        u[:, h + 8, h, 0] = c.astype(BF)
    w = layers(rng)
    w[:, :, :, :, :, [0, 1, 8]] = 0
    for g in range(8): w[:, g, 1, 0, g, 8, 0] = 32.0
    return {"x": x.reshape(N, 128, 4 * C), "u": u.reshape(N, 128, 512), "v": d["v"], **lists(rng), **weights(rng, w)}
def setup_inputs_near(rng):
    d = numbers_of(rng)
    o = rng.permutation(N) % 2
    k = np.where(o == 0, 2.0 ** -30, 1.0).astype(np.float32)
    x = np.zeros((N, 8, 16, C, 4), np.float32)
    s = rng.integers(-1, 2, (N, 8, C)) * k[:, None, None]
    x[:, :, 0, :, 0] = 1.125 * s
    x[:, :, 1, :, 0] = -1.25 * s
    for r in range(N):
        for g in rng.permutation(8)[:4]: x[r, g, 0, rng.integers(C), 0] = 2.0 ** 30 * rng.choice([-1.0, 1.0])
    x[:, :, 10, :, 0] = rng.integers(-1, 2, (N, 8, C)) * 2.0 ** -30
    x[:, :, 11, :, 0] = 2.0 ** -30
    u = d["u"].reshape(N, 128, 128, 4)
    u[:, :, ::16] = 0
    for h in range(0, 128, 16):
        u[:, h, h, 0] = (1.125 * k).astype(BF)
        u[:, h + 1, h, 0] = k.astype(BF)
        u[:, h + 8, h, 0] = k.astype(BF)
    w = np.zeros((N, 8, 16, 4, 8, 16, 4), np.float32)
    for g in range(8):
        w[:, g, 10, 0, g, 8, 0] = 2.0 ** -7
        w[:, g, 11, 0, g, 9, 0] = 2.0 ** 7
    for r in range(N):
        for g in rng.permutation(8)[:4]:
            w[r, g, 10, 0, g, 8, 0] = 2.0 ** -11
            w[r, g, 10, 0, g, 13, 0] = -2.0 ** -11
            w[r, g, 12, 0, g, 8, 0] = 2.0 ** -8
            w[r, g, 12, 0, g, 13, 0] = 2.0 ** -8
            w[r, g, 11, 0, g, 9, 0] = 2.0 ** 5
            u[r, 16 * g + 8, 16 * g, 0] = 1.125 * float(k[r])
            u[r, 16 * g + 13, 16 * g, 0] = float(k[r])
    return {"x": x.reshape(N, 128, 4 * C).astype(BF), "u": u.reshape(N, 128, 512), "v": d["v"], **lists(rng), **weights(rng, w.astype(BF))}
def setup_inputs_odd(rng):
    d = numbers_of(rng)
    x = (1.0 + (2 * rng.integers(0, 64, (N, 8, 16, C, 4)) + 1) * 2.0 ** -7) * np.exp2(-rng.integers(0, 7, (N, 8, 16, C, 4)).astype(np.float64)) * rng.choice([-1.0, 1.0], (N, 8, 16, C, 4))
    x[:, :, 0, :, 0] = 1.96875 * 2.0 ** 8 * rng.choice([-1.0, 1.0], (N, 8, C))
    x[:, :, 1:3] = 0
    x[:, :, 1, :, 0] = (8 + rng.integers(0, 2, (N, 8, C))) * 2.0 ** -8
    x[:, :, 2, :, 0] = -2.0 ** -5
    a = np.exp2(rng.integers(-3, 4, (N, 8, C)).astype(np.float64))
    x[:, :, 8:] = 0
    x[:, :, 8, :, 0] = 1.125 * a
    x[:, :, 11, :, 0] = (8 + rng.integers(0, 2, (N, 8, C))) * 2.0 ** -7 * a
    x[:, :, 12, :, 0] = 2.0 ** -4 * a
    u = d["u"].reshape(N, 128, 128, 4)
    u[:, :, ::16] = 0
    for h in range(0, 128, 16):
        for i in (1, 2, 9, 10): u[:, h + i, h, 0] = 1.0
    w = layers(rng)
    w[:, :, :3] = 0
    w[:, :, :, :, :, :3] = 0
    w[:, :, :, :, :, 8:] = 0
    for g in range(8):
        w[:, g, 8, 0, g, 8, 0] = 28.0
        w[:, g, 11, 0, g, 9, 0] = 2.0 ** -5
        w[:, g, 12, 0, g, 10, 0] = -2.0 ** -5
    return {"x": x.astype(np.float32).reshape(N, 128, 4 * C).astype(BF), "u": u.reshape(N, 128, 512), "v": d["v"], **lists(rng), **weights(rng, w)}
def setup_inputs_ends(rng):
    d = numbers_of(rng)
    o, e, h = rng.permutation(N) % 4, rng.permutation(N) % 4, rng.permutation(N) % 2
    s = rng.choice([-1.0, 1.0], (N, 8, 8, C, 4))
    s[o == 0] = -1
    s[o == 1] = rng.choice([-1.0, 1.0], (N, 1, 1, C, 1))[o == 1]
    low = s * (0.9 + 0.1 * rng.random((N, 8, 8, C, 4))) * 2.0 ** 30
    low[o == 3] = s[o == 3] * 2.0 ** -30
    x = d["x"].astype(np.float32).reshape(N, 8, 16, C, 4)
    x[:, :, :8] = low
    size = np.where(o == 3, 2.0 ** -30, 2.0 ** 30)
    c = np.stack([rng.permutation(8) % 2 * 2.0 - 1.0 for r in range(N)]) * size[:, None]
    u = d["u"].reshape(N, 128, 128, 4)
    u[:, :, ::16] = c.astype(np.float32).astype(BF)[:, None, :, None]
    v = rng.choice([-1.0, 1.0], (N, 128, 512)) * size[:, None, None]
    a, b, t = [rng.integers(0, C, (N, 8, C)) for i in range(3)]
    a[e == 0], b[e == 0], t[e == 0] = C - 1, C - 1, C - 1
    a[e == 1], b[e == 1], t[e == 1] = 0, C - 1, 0
    a[e == 2], b[e == 2], t[e == 2] = C - 1 - np.arange(C), np.arange(C), (np.arange(C) + 1) % 2 * (C - 1)
    w = np.zeros((N, 128, 4, 128, 4), np.float32)
    i = np.flatnonzero(np.arange(128) % 16 >= 8)
    for k in range(4): w[:, i, k, i, k] = np.where(h == 0, 2.0 ** 8, 2.0 ** -8)[:, None] * rng.choice([-1.0, 1.0], (N, 64))
    return {"x": x.reshape(N, 128, 4 * C).astype(BF), "u": u.reshape(N, 128, 512), "v": v.astype(np.float32).astype(BF), **stored(a, b, t), **weights(rng, w.astype(BF))}
def setup_inputs_spread(rng):
    d = setup_inputs(rng)
    d["x"] = wide(rng, N, 128, 4 * C, cols=6)
    return d
def check_inputs(d):
    b = []
    for k in ("x", "u", "v"):
        a = np.abs(d[k].astype(np.float32))
        if not (np.isfinite(a).all() and ((a == 0) | (a >= 2.0 ** -30) & (a <= 2.0 ** 30)).all()): b.append("a value of " + k)
    for k in ("ta", "tb", "st"):
        if not ((d[k] >= 0) & (d[k] < C)).all(): b.append("an entry of " + k)
    none, least, most = [emit(mx_ref.quantize(np.full((128, 16), k, np.float32).astype(BF)))[1][0, 0] for k in (0.0, 2.0 ** -8, 2.0 ** 8)]
    for r in range(N):
        if ((d["wc"][r] == 0x7F) | (d["wc"][r] == 0xFF)).any(): b.append("wc: a code that is no number")
        s = mx_ref.live(d["ws"][r])
        if ((s != none) & ((s < least) | (s > most))).any(): b.append("ws: a scale out of range")
    return b
def at(t, s):
    return np.take_along_axis(t, s, axis=2)
def reference(x, u, v, ta, tb, st, wc, ws):
    qu = [mx_ref.quantize(u[r]) for r in range(N)]
    lay = [pk(wc[r], ws[r]) for r in range(N)]
    a, b, s = [np.stack([gentries(k[r]) for r in range(N)]).astype(np.int64) for k in (ta, tb, st)]
    now = [x[r] for r in range(N)]
    for step in STEP:
        q = [mx_ref.quantize(now[r]) for r in range(N)]
        bit = np.stack([mx_ref.matmul(qu[r], q[r])[::16] > 0 for r in range(N)])
        for k in range(STAGES):
            right = np.roll(at(bit, s), -1, axis=2)
            s = np.where(right, at(b, s), at(a, s))
        z = [gcols(decode(q[r]).astype(BF), s[r]) for r in range(N)]
        qz = [mx_ref.quantize(z[r]) for r in range(N)]
        made, change = [], []
        for r in range(N):
            p = r ^ step
            h = tile([mx_ref.matmul(pick(lay[r], np.arange(128 * k, 128 * k + 128)), qz[p]) * np.float32(0.03125) for k in range(4)])
            change.append(mx_ref.matmul(qu[r], mx_ref.quantize(h))[::16] > 0)
            made.append((z[r].astype(np.float32) + gcols(h, s[p]).astype(np.float32)).astype(BF))
        c = np.stack(change)
        a, b = np.where(c, b, a), np.where(c, a, b)
        now = made
    y, op = np.zeros((N, 128, C), np.float32), np.zeros((N, 8, 3 * C), np.float32)
    oc, osc = np.zeros((N, 128, 4 * C), np.uint8), np.zeros((N, 16, C), np.uint8)
    for r in range(N):
        q = mx_ref.quantize(now[r])
        y[r] = mx_ref.matmul(mx_ref.quantize(v[r]), q)
        op[r] = np.concatenate([s[r], a[r], b[r]], axis=1)
        oc[r], osc[r] = emit(q)
    return {"y": y, "op": op, "oc": oc, "osc": osc}

@@ -1,0 +1,367 @@
+from concourse.bass import DstId, RemoteDMATransfer
+from concourse.mybir import dt, AluOpType, ActivationFunctionType
+
+C = 480
+L = 31
+RUN = 16 * L
+DUP = 2048
+WIN = DUP + 2 * C
+STEP = [1, 2, 3]
+STAGES = 5
+
+SCRATCH = {}
+
+
+def _add(name, shape, dtype, where="sbuf"):
+    SCRATCH[name] = (where, shape, dtype)
+
+
+CODES = "float8_e4m3fn_x4"
+for _n in ("xt",):
+    _add(_n, [128, 4 * C], "bfloat16")
+for _n in ("ut", "vt"):
+    _add(_n, [128, 512], "bfloat16")
+for _n in ("qu", "qr", "qv", "qe0", "qe1", "qe2", "qe3"):
+    _add(_n, [128, 128], CODES)
+    _add(_n + "s", [128, 128], "uint8")
+_add("wq", [128, 512], CODES)
+_add("wqs", [128, 512], "uint8")
+for _r in range(4):
+    _add("q%d" % _r, [128, C], CODES)
+    _add("q%ds" % _r, [128, C], "uint8")
+    _add("sl%d" % _r, [128, 32], "uint16")
+for _r in range(3):
+    _add("ql%d" % _r, [128, C], CODES)
+    _add("ql%ds" % _r, [128, C], "uint8")
+    _add("ll%d" % _r, [128, 32], "uint16")
+for _n in ("qz", "qh"):
+    _add(_n, [128, C], CODES)
+    _add(_n + "s", [128, C], "uint8")
+for _n in ("X", "Zp", "H"):
+    _add(_n, [128, 4 * C], "bfloat16")
+for _b in range(4):
+    _add("to%d" % _b, [128, C], "bfloat16")
+    _add("tp%d" % _b, [128, C], "bfloat16")
+    _add("zo%d" % _b, [128, C], "bfloat16")
+for _n in ("hw0", "hw1", "sg", "xs", "d0h"):
+    _add(_n, [128, C], "bfloat16")
+for _n in ("raw", "words"):
+    _add(_n, [128, WIN], "float32")
+for _n in ("t", "i2"):
+    _add(_n, [128, C], "float32")
+_add("G", [128, RUN + 16], "float32")
+_add("St", [128, RUN], "float32")
+_add("d0", [128, RUN], "float32")
+_add("one", [128, 528], "bfloat16")
+_add("eye", [128, 528], "bfloat16")
+for _n in ("wt", "sm", "s2", "bt", "mv", "laf", "lbf", "df"):
+    _add(_n, [128, 32], "float32")
+for _n in ("o", "la", "lb", "l2", "l3"):
+    _add(_n, [128, 32], "uint16")
+for _n in ("sti", "tai", "tbi"):
+    _add(_n, [128, 30], "int32")
+_add("di", [128, 16], "int32")
+_add("dm", [128, 16], "int32")
+_add("qi", [128, 8], "int32")
+_add("qm", [128, 8], "int32")
+_add("ip", [128, 8], "int32")
+_add("ip16", [128, 8], "uint16")
+_add("ma", [128, 16], "float32")
+_add("mb", [128, 16], "float32")
+_add("mc", [128, 16], "float32")
+for _n in ("ka", "kb", "kc", "kd", "ke", "sc", "sch", "si", "wp"):
+    _add(_n, [128, 8], "float32")
+_add("yb", [128, C], "float32")
+_add("opb", [128, 3 * C], "float32")
+for _b in range(8):
+    _add("ps%d" % _b, [128, 512], "float32", "psum")
+
+LOADS = ["x", "u", "st", "ta", "tb", "wc", "ws", "v"]
+SEMAPHORES = ["cv", "ca", "cp", "cg", "out", "left"] + ["ld_" + n for n in LOADS]
+SEMAPHORES += ["rq%d" % r for r in range(3)] + ["rl%d" % r for r in range(3)]
+
+
+def rank_program(g, core, T, topo):
+    rank = T.rank_of(core)
+    if rank is None:
+        return
+    A = AluOpType
+    COPY = ActivationFunctionType.Copy
+    SIGN = ActivationFunctionType.Sign
+    eng = {"v": g.vector, "a": g.scalar, "p": g.tensor, "g": g, "s": g.sync}
+    total = {}
+    know = {q: {} for q in eng}
+    wrote = {}
+    read = {}
+
+    def wait(q, toks):
+        toks = [t for t in toks if know[q].get(t[1], 0) < t[2]]
+        keep = []
+        for i, t in enumerate(toks):
+            if not any(j != i and o[3].get(t[1], 0) >= t[2] and (o[1:3] != t[1:3] or j < i) for j, o in enumerate(toks)):
+                keep.append(t)
+        for t in keep:
+            eng[q].wait_ge(T.sem[t[1]], t[2])
+            for s, n in t[3].items():
+                know[q][s] = max(know[q].get(s, 0), n)
+
+    def before(q, reads, writes, banks):
+        toks = [wrote[k] for k in reads if k in wrote]
+        for k in list(writes) + list(banks):
+            if k in wrote and (wrote[k][0] != q):
+                toks.append(wrote[k])
+            toks += [t for t in read.get(k, {}).values() if t[0] != q]
+        wait(q, toks)
+
+    def after(q, sem, n, reads, writes, banks):
+        total[sem] = total.get(sem, 0) + n
+        clk = dict(know[q])
+        clk[sem] = total[sem]
+        tok = (q, sem, total[sem], clk)
+        for k in reads:
+            read.setdefault(k, {})[q] = tok
+        for k in list(writes) + list(banks):
+            wrote[k] = tok
+            read[k] = {}
+        return tok
+
+    def op(q, call, reads, writes, banks=()):
+        before(q, reads, writes, banks)
+        call().then_inc(T.sem["c" + q], 1)
+        return after(q, "c" + q, 1, reads, writes, banks)
+
+    def dma(q, out, in_, sem, reads=(), writes=()):
+        before(q, reads, writes, ())
+        eng[q].dma_start(out, in_).then_inc(T.sem[sem], 16)
+        return after(q + "dma" + sem, sem, 16, reads, writes, ()) if False else _dma_after(q, sem, reads, writes)
+
+    def _dma_after(q, sem, reads, writes):
+        total[sem] = total.get(sem, 0) + 16
+        clk = dict(know[q])
+        clk[sem] = total[sem]
+        tok = ("dma", sem, total[sem], clk)
+        for k in reads:
+            read.setdefault(k, {})["dma" + sem] = tok
+        for k in writes:
+            wrote[k] = tok
+            read[k] = {}
+        return tok
+
+    def vcopy(out, in_, reads, writes, banks=()):
+        return op("v", lambda: g.vector.tensor_copy(out, in_), reads, writes, banks)
+
+    def vts(out, in_, s1, s2, op0, op1, reads, writes, banks=()):
+        if op1 is None:
+            return op("v", lambda: g.vector.tensor_scalar(out, in_, s1, None, op0), reads, writes, banks)
+        return op("v", lambda: g.vector.tensor_scalar(out, in_, s1, s2, op0, op1), reads, writes, banks)
+
+    def vtt(out, a, b, o, reads, writes, banks=()):
+        return op("v", lambda: g.vector.tensor_tensor(out, a, b, o), reads, writes, banks)
+
+    def vset(ap, c, writes):
+        return op("v", lambda: g.vector.memset(ap, c), [], writes)
+
+    def act(out, in_, reads, writes, banks=(), func=COPY, scale=1.0):
+        if scale == 1.0:
+            return op("a", lambda: g.scalar.activation(out, in_, func), reads, writes, banks)
+        return op("a", lambda: g.scalar.activation(out, in_, func, scale=scale), reads, writes, banks)
+
+    def quant(name, tile_ap, reads):
+        return op("v", lambda: g.vector.quantize_mx(T[name][:], T[name + "s"][:], tile_ap), reads, [name])
+
+    def mx(bank, w, wcols, x, xcols):
+        n = xcols[1] - xcols[0]
+        return op("p", lambda: g.tensor.matmul_mx(T["ps%d" % bank][:, 0:n], T[w][:, wcols[0]:wcols[1]], T[w + "s"][:, wcols[0]:wcols[1]],
+                                                   T[x][:, xcols[0]:xcols[1]], T[x + "s"][:, xcols[0]:xcols[1]], True, True),
+                  [w, x], [], ["ps%d" % bank])
+
+    ALL = (0, C)
+    W0 = (0, 128)
+    ps = lambda b: T["ps%d" % b][:, 0:C]
+    bank = lambda b: ["ps%d" % b]
+    ends = T.St[:, 15:RUN:16]
+
+    dma("s", T.xt[:], T.x[:], "ld_x", writes=["xt"])
+    dma("a", T.ut[:], T.u[:], "ld_u", writes=["ut"])
+    dma("a", T.sti[:], T.st[:], "ld_st", writes=["sti"])
+    dma("a", T.tai[:], T.ta[:], "ld_ta", writes=["tai"])
+    dma("a", T.tbi[:], T.tb[:], "ld_tb", writes=["tbi"])
+    dma("s", T.wq[:].bitcast(dt.uint8), T.wc[:], "ld_wc", writes=["wq"])
+    dma("s", T.wqs[:], T.ws[:], "ld_ws", writes=["wqs"])
+    dma("s", T.vt[:], T.v[:], "ld_v", writes=["vt"])
+
+    vset(T.one[:], 1.0, ["one"])
+    op("g", lambda: g.iota(T.ip[:], [[16, 8]], 0, 0), [], ["ip"])
+    op("g", lambda: g.iota(T.qi[:], [[0, 8]], 0, 1), [], ["qi"])
+    op("g", lambda: g.iota(T.di[:], [[1, 16]], 128, -1), [], ["di"])
+    op("g", lambda: g.iota(T.i2[:], [[2, C]], 0, 0, allow_small_or_imprecise_dtypes=True), [], ["i2"])
+    op("g", lambda: g.affine_select(T.eye[:], T.one[:], [[-1, 528]], A.is_equal, 0.0, 3, 4), ["one"], ["eye"])
+    vset(T.raw[:, 2 * C:DUP], 0.0, ["rawgap"])
+    vset(T.words[:, 2 * C:DUP], 0.0, ["wordgap"])
+    vset(T.G[:, RUN:RUN + 16], 0.0, ["Gtail"])
+    vcopy(T.ip16[:], T.ip[:], ["ip"], ["ip16"])
+    c1 = slice(0, 1)
+    vts(T.qm[:], T.qi[:], 15, None, A.bitwise_and, None, ["qi"], ["qm"])
+    vts(T.dm[:], T.di[:], 15, None, A.bitwise_and, None, ["di"], ["dm"])
+    vts(T.ka[:], T.qm[:], 13, 2.0 ** -27, A.is_le, A.mult, ["qm"], ["ka"])
+    vts(T.kb[:], T.qm[:], 14, 2.0 ** -11, A.is_equal, A.mult, ["qm"], ["kb"])
+    vts(T.kc[:], T.qm[:], 15, 1.0, A.is_equal, A.mult, ["qm"], ["kc"])
+    vts(T.kd[:], T.qm[:], 13, 2.0 ** 28, A.is_le, A.mult, ["qm"], ["kd"])
+    vts(T.ke[:], T.qm[:], 14, 2.0 ** 12, A.is_equal, A.mult, ["qm"], ["ke"])
+    vts(T.wp[:], T.qm[:], 15, 2.0 ** -11, A.is_equal, A.mult, ["qm"], ["wp"])
+    vts(T.ma[:], T.dm[:], 1, 2047.0, A.is_equal, A.mult, ["dm"], ["ma"])
+    vts(T.mb[:], T.dm[:], 2, 65535.0, A.is_equal, A.mult, ["dm"], ["mb"])
+    vts(T.mc[:], T.dm[:], 0, 1.0, A.not_equal, A.mult, ["dm"], ["mc"])
+    vtt(T.ka[:], T.ka[:], T.kb[:], A.add, ["ka", "kb"], ["ka"])
+    vtt(T.kd[:], T.kd[:], T.ke[:], A.add, ["kd", "ke"], ["kd"])
+    vts(T.ke[:], T.kc[:], 2.0, None, A.mult, None, ["kc", "kd"], ["ke"])
+    vtt(T.ma[:], T.ma[:], T.mb[:], A.add, ["ma", "mb"], ["ma"])
+    vtt(T.sc[:], T.ka[:], T.kc[:], A.add, ["ka", "kc"], ["sc"])
+    vtt(T.si[:], T.kd[:], T.ke[:], A.add, ["kd", "ke"], ["si"])
+    vtt(T.d0[:, 0:16], T.ma[:], T.mc[:], A.add, ["ma", "mc"], ["d0"])
+    vts(T.sch[:], T.sc[:], 0.5, None, A.mult, None, ["sc"], ["sch"])
+    vcopy(T.la[:, 0:30], T.tai[:], ["tai"], ["la"])
+    vcopy(T.lb[:, 0:30], T.tbi[:], ["tbi"], ["lb"])
+    vcopy(T.sl0[:, 0:30], T.sti[:], ["sti"], ["sl0"])
+    vcopy(T.sl0[:, 30:31], T.sti[:, 0:1], ["sti"], ["sl0"])
+    n = 16
+    while n < RUN:
+        m = min(n, RUN - n)
+        vcopy(T.d0[:, n:n + m], T.d0[:, 0:m], ["d0"], ["d0"])
+        n += m
+    quant("qu", T.ut[:], ["ut"])
+    quant_pick = T.qu[:, 0:128].bitcast(dt.uint32).indirect(T.ip16[:, 0:8])
+    vcopy(T.qr[:, 0:128].bitcast(dt.uint32), quant_pick, ["qu", "ip16"], ["qr"])
+    vcopy(T.qrs[:, 0:128], T.qus[:, 0:128].indirect(T.ip16[:, 0:8]), ["qu", "ip16"], ["qrs"])
+    quant("q0", T.xt[:], ["xt"])
+    for b in range(4):
+        quant("qe%d" % b, T.eye[:, 3 - b:515 - b], ["eye"])
+    vcopy(T.d0h[:], T.d0[:, 0:C], ["d0"], ["d0h"])
+    vts(T.s2[:, 0:L], T.sl0[:, 0:L], T.si[:, c1], None, A.mult, None, ["sl0", "si"], ["s2"])
+    vcopy(T.laf[:, 0:30], T.tai[:], ["tai"], ["laf"])
+    vcopy(T.lbf[:, 0:30], T.tbi[:], ["tbi"], ["lbf"])
+    vtt(T.df[:, 0:30], T.lbf[:, 0:30], T.laf[:, 0:30], A.subtract, ["laf", "lbf"], ["df"])
+
+    def tables():
+        act(T.raw[:, 0:2 * C:2], T.i2[:, 0:C].indirect(T.la[:, 0:30]), ["i2", "la"], ["raw0"])
+        act(T.raw[:, 1:2 * C:2], T.i2[:, 0:C].indirect(T.lb[:, 0:30]), ["i2", "lb"], ["raw1"])
+
+    def scan():
+        return op("v", lambda: g.vector.tensor_tensor_scan(T.St[:], T.d0[:], T.G[:, 0:RUN], 0.0, A.mult, A.add), ["d0", "G"], ["St"])
+
+    def send(r, dst, name, land, cols, sem, reads, codes=False):
+        rid, pid = topo.addr(dst)[:2]
+        mask = topo.mask(core, dst)
+        before("g", reads, [], [])
+        n = len(topo.engines(core, dst))
+        src, out = T[name][:, 0:cols], T[land][:, 0:cols]
+        if codes:
+            src, out = src.bitcast(dt.uint8), out.bitcast(dt.uint8)
+        g.remote_dma(out, src, T.sem[sem], T.sem.left, pid, rid, mask)
+        total["left"] = total.get("left", 0) + n
+        total[sem] = total.get(sem, 0) + n
+
+    def arrives(keys, sem):
+        for k in keys:
+            wrote[k] = ("far", sem, total[sem], {sem: total[sem]})
+
+    for r, step in enumerate(STEP):
+        last = r == len(STEP) - 1
+        dst = T.cores[rank ^ step]
+        q, ql, ll, sl, sn = "q%d" % r, "ql%d" % r, "ll%d" % r, "sl%d" % r, "sl%d" % (r + 1)
+        send(r, dst, q, ql, C, "rq%d" % r, [q], codes=True)
+        send(r, dst, q + "s", ql + "s", C, "rq%d" % r, [q])
+        arrives([ql], "rq%d" % r)
+        op("p", lambda: g.tensor.matmul_mx(ps(0), T.qr[:], T.qrs[:], T[q][:], T[q + "s"][:], True, True), ["qr", "qrs", q], [], bank(0))
+        tables()
+        vts(T.t[:], ps(0), 0.0, float(DUP), A.is_gt, A.mult, [], ["t"], bank(0)) if False else None
+        op("v", lambda: g.vector.tensor_scalar(T.t[:], ps(0), 0.0, float(DUP), A.is_gt, A.mult), ["ps0"], ["t"], bank(0))
+        act(T.G[:, 0:RUN], T.t[:, 0:C].indirect(T[sl][:, 0:L]), ["t", sl], ["G"])
+        for h, ls in ((0, "la"), (1, "lb")):
+            vtt(T.words[:, h:2 * C:2], T.t[:, 0:C].indirect(T[ls][:, 0:30]), T.raw[:, h:2 * C:2], A.add, ["t", ls, "raw%d" % h], ["words%d" % h])
+            act(T.words[:, DUP + h:WIN:2], T.words[:, h:2 * C:2], ["words%d" % h], ["dup%d" % h])
+        act(T.raw[:, DUP:WIN], T.raw[:, 0:2 * C], ["raw0", "raw1"], ["rawdup"])
+        for b in range(4):
+            mx(2 + b, "qe%d" % b, W0, q, ALL)
+            act(T["to%d" % b][:], ps(2 + b), ["ps%d" % (2 + b)], ["to%d" % b], bank(2 + b))
+        for b, k in enumerate((6, 7, 2, 3)):
+            mx(k, "qe%d" % b, W0, ql, ALL)
+            act(T["tp%d" % b][:], ps(k), ["ps%d" % k], ["tp%d" % b], bank(k))
+        for k in range(STAGES):
+            if k:
+                op("v", lambda: g.vector.tensor_copy(T.G[:, 0:RUN], T.words[:, 0:WIN].indirect(T.o[:, 0:L])),
+                   ["o", "words0", "words1", "dup0", "dup1", "wordgap"], ["G"])
+            scan()
+            vts(T.wt[:, 0:L], T.G[:, 16:RUN + 16:16], T.wp[:, c1], None, A.mult, None, ["G", "Gtail", "wp"], ["wt"])
+            if k == 0:
+                vtt(T.wt[:, 0:L], T.wt[:, 0:L], T.s2[:, 0:L], A.add, ["wt", "s2"], ["wt"])
+            vtt(T.sm[:, 0:L], ends, T.wt[:, 0:L], A.add, ["St", "wt"], ["sm"])
+            vts(T.o[:, 0:L], T.sm[:, 0:L], T.sc[:, c1], 0.015625, A.mult, A.add, ["sm", "sc"], ["o"])
+        vcopy(T.G[:, 0:RUN], T.raw[:, 0:WIN].indirect(T.o[:, 0:L]), ["o", "raw0", "raw1", "rawdup", "rawgap"], ["G"])
+        scan()
+        vts(T[sn][:, 0:L], ends, T.sch[:, c1], 0.015625, A.mult, A.add, ["St", "sch"], [sn])
+        send(r, dst, sn, ll, 30, "rl%d" % r, [sn])
+        arrives([ll], "rl%d" % r)
+        own = T[sn][:, 0:30]
+        for b in (0, 1):
+            act(T["zo%d" % b][:], T["to%d" % b][:, 0:C].indirect(own), ["to%d" % b, sn], ["zo%d" % b])
+        for b in (2, 3):
+            vcopy(T["zo%d" % b][:], T["to%d" % b][:, 0:C].indirect(own), ["to%d" % b, sn], ["zo%d" % b])
+        if not last:
+            vts(T.s2[:, 0:L], T[sn][:, 0:L], T.si[:, c1], None, A.mult, None, [sn, "si"], ["s2"])
+        if r == 0:
+            quant("qv", T.vt[:], ["vt"])
+        if last:
+            vts(T.opb[:, 0:C], T.G[:, 0:C], 0.5, None, A.mult, None, ["G"], ["op0"])
+        far = T[ll][:, 0:30]
+        for b in (0, 1):
+            act(T.Zp[:, b:4 * C:4], T["tp%d" % b][:, 0:C].indirect(far), ["tp%d" % b, ll], ["Zp%d" % b])
+        for b in (2, 3):
+            vcopy(T.Zp[:, b:4 * C:4], T["tp%d" % b][:, 0:C].indirect(far), ["tp%d" % b, ll], ["Zp%d" % b])
+        quant("qz", T.Zp[:], ["Zp%d" % b for b in range(4)])
+        for b in (2, 3):
+            vts(T["l%d" % b][:, 0:30], far, 4, b, A.mult, A.add, [ll], ["l%d" % b])
+        for b in range(4):
+            op("p", lambda: g.tensor.matmul_mx(ps(4 + b), T.wq[:, 128 * b:128 * b + 128], T.wqs[:, 128 * b:128 * b + 128], T.qz[:], T.qzs[:], True, True),
+               ["wq", "wqs", "qz"], [], bank(4 + b))
+            if b < 2:
+                act(T["hw%d" % b][:], ps(4 + b), ["ps%d" % (4 + b)], ["hw%d" % b], bank(4 + b), scale=0.03125)
+            else:
+                act(T.H[:, b:4 * C:4], ps(4 + b), ["ps%d" % (4 + b)], ["H%d" % b], bank(4 + b), scale=0.03125)
+        for b in (0, 1):
+            vtt(T.X[:, b:4 * C:4], T["hw%d" % b][:, 0:C].indirect(far), T["zo%d" % b][:], A.add, ["hw%d" % b, ll, "zo%d" % b], ["X%d" % b])
+        for b in (0, 1):
+            vcopy(T.H[:, b:4 * C:4], T["hw%d" % b][:], ["hw%d" % b], ["H%d" % b])
+        HS = ["H%d" % b for b in range(4)]
+        quant("qh", T.H[:], HS)
+        op("p", lambda: g.tensor.matmul_mx(ps(1), T.qr[:], T.qrs[:], T.qh[:], T.qhs[:], True, True), ["qr", "qrs", "qh"], [], bank(1))
+        act(T.sg[:], ps(1), ["ps1"], ["sg"], bank(1), func=SIGN)
+        for b in (2, 3):
+            vtt(T.X[:, b:4 * C:4], T.H[:, 0:4 * C].indirect(T["l%d" % b][:, 0:30]), T["zo%d" % b][:], A.add, HS + ["l%d" % b, "zo%d" % b], ["X%d" % b])
+        quant("q%d" % (r + 1), T.X[:], ["X%d" % b for b in range(4)])
+        op("v", lambda: g.vector.tensor_tensor_scan(T.xs[:], T.d0h[:], T.sg[:], 0.0, A.mult, A.add), ["d0h", "sg"], ["xs"])
+        vts(T.bt[:, 0:30], T.xs[:, 15:C:16], T.sc[:, c1], 0.5, A.mult, A.is_gt, ["xs", "sc"], ["bt"])
+        vtt(T.mv[:, 0:30], T.bt[:, 0:30], T.df[:, 0:30], A.mult, ["bt", "df"], ["mv"])
+        vtt(T.laf[:, 0:30], T.laf[:, 0:30], T.mv[:, 0:30], A.add, ["laf", "mv"], ["laf"])
+        vtt(T.lbf[:, 0:30], T.lbf[:, 0:30], T.mv[:, 0:30], A.subtract, ["lbf", "mv"], ["lbf"])
+        vcopy(T.la[:, 0:30], T.laf[:, 0:30], ["laf"], ["la"])
+        vcopy(T.lb[:, 0:30], T.lbf[:, 0:30], ["lbf"], ["lb"])
+        if not last:
+            vtt(T.df[:, 0:30], T.lbf[:, 0:30], T.laf[:, 0:30], A.subtract, ["laf", "lbf"], ["df"])
+
+    dma("s", T.oc[:], T.q3[:].bitcast(dt.uint8), "out", reads=["q3"])
+    for k in range(4):
+        dma("s", T.osc[4 * k:4 * k + 4, :], T.q3s[32 * k:32 * k + 4, :], "out", reads=["q3"])
+    half = C // 2
+    mx(0, "qv", W0, "q3", (0, half))
+    mx(2, "qv", W0, "q3", (half, C))
+    op("a", lambda: g.scalar.activation(T.yb[:, 0:half], T.ps0[:, 0:half], COPY), ["ps0"], ["y0"], bank(0))
+    dma("s", T.y[:, 0:half], T.yb[:, 0:half], "out", reads=["y0"])
+    op("v", lambda: g.vector.tensor_copy(T.yb[:, half:C], T.ps2[:, 0:half]), ["ps2"], ["y1"], bank(2))
+    dma("s", T.y[:, half:C], T.yb[:, half:C], "out", reads=["y1"])
+    act(T.opb[:, C:2 * C], T.i2[:, 0:C].indirect(T.la[:, 0:30]), ["i2", "la"], ["op1"], scale=0.5)
+    vts(T.opb[:, 2 * C:3 * C], T.i2[:, 0:C].indirect(T.lb[:, 0:30]), 0.5, None, A.mult, None, ["i2", "lb"], ["op2"])
+    dma("s", T.op[:], T.opb[0:128:16, :], "out", reads=["op0", "op1", "op2"])
+    for s in sorted(total):
+        if know["g"].get(s, 0) < total[s]:
+            g.wait_ge(T.sem[s], total[s])

@@ -1,4 +1,3 @@
-from concourse.bass import DstId, RemoteDMATransfer
 from concourse.mybir import dt, AluOpType, ActivationFunctionType
 
 C = 480
@@ -8,6 +7,10 @@ DUP = 2048
 WIN = DUP + 2 * C
 STEP = [1, 2, 3]
 STAGES = 5
+XCUT = 352
+ZCUT = 288
+BASE = 1055
+TINY = 2.0 ** -100
 
 SCRATCH = {}
 
@@ -17,8 +20,7 @@ def _add(name, shape, dtype, where="sbuf"):
 
 
 CODES = "float8_e4m3fn_x4"
-for _n in ("xt",):
-    _add(_n, [128, 4 * C], "bfloat16")
+_add("xt", [128, 4 * C], "bfloat16")
 for _n in ("ut", "vt"):
     _add(_n, [128, 512], "bfloat16")
 for _n in ("qu", "qr", "qv", "qe0", "qe1", "qe2", "qe3"):
@@ -43,40 +45,37 @@ for _b in range(4):
     _add("to%d" % _b, [128, C], "bfloat16")
     _add("tp%d" % _b, [128, C], "bfloat16")
     _add("zo%d" % _b, [128, C], "bfloat16")
-for _n in ("hw0", "hw1", "sg", "xs", "d0h"):
+    _add("l%d" % _b, [128, 32], "uint16")
+for _n in ("sg", "sv", "xs"):
     _add(_n, [128, C], "bfloat16")
 for _n in ("raw", "words"):
     _add(_n, [128, WIN], "float32")
-for _n in ("t", "i2"):
+for _n in ("t", "i1", "i5"):
     _add(_n, [128, C], "float32")
-_add("G", [128, RUN + 16], "float32")
-_add("St", [128, RUN], "float32")
-_add("d0", [128, RUN], "float32")
-_add("one", [128, 528], "bfloat16")
+for _n in ("G", "St"):
+    _add(_n, [128, 512], "float16")
+for _n in ("G0", "St0", "d0"):
+    _add(_n, [128, 512], "bfloat16")
+_add("one", [128, 544], "bfloat16")
 _add("eye", [128, 528], "bfloat16")
-for _n in ("wt", "sm", "s2", "bt", "mv", "laf", "lbf", "df"):
+for _n in ("sm", "s2", "m2", "hs", "hn", "ma", "mb", "mc", "oh", "ks"):
     _add(_n, [128, 32], "float32")
-for _n in ("o", "la", "lb", "l2", "l3"):
-    _add(_n, [128, 32], "uint16")
+_add("labf", [128, 64], "float32")
+_add("lab", [128, 64], "uint16")
+_add("o", [128, 32], "uint16")
 for _n in ("sti", "tai", "tbi"):
     _add(_n, [128, 30], "int32")
-_add("di", [128, 16], "int32")
-_add("dm", [128, 16], "int32")
-_add("qi", [128, 8], "int32")
-_add("qm", [128, 8], "int32")
+_add("di", [128, 32], "int32")
+_add("dm", [128, 32], "int32")
 _add("ip", [128, 8], "int32")
 _add("ip16", [128, 8], "uint16")
-_add("ma", [128, 16], "float32")
-_add("mb", [128, 16], "float32")
-_add("mc", [128, 16], "float32")
-for _n in ("ka", "kb", "kc", "kd", "ke", "sc", "sch", "si", "wp"):
-    _add(_n, [128, 8], "float32")
+_add("rc", [128, 8], "float32")
 _add("yb", [128, C], "float32")
 _add("opb", [128, 3 * C], "float32")
 for _b in range(8):
     _add("ps%d" % _b, [128, 512], "float32", "psum")
 
-LOADS = ["x", "u", "st", "ta", "tb", "wc", "ws", "v"]
+LOADS = ["x0", "x1", "u", "st", "ta", "tb", "wc", "ws", "v"]
 SEMAPHORES = ["cv", "ca", "cp", "cg", "out", "left"] + ["ld_" + n for n in LOADS]
 SEMAPHORES += ["rq%d" % r for r in range(3)] + ["rl%d" % r for r in range(3)]
 
@@ -88,6 +87,7 @@ def rank_program(g, core, T, topo):
     A = AluOpType
     COPY = ActivationFunctionType.Copy
     SIGN = ActivationFunctionType.Sign
+    IDENT = ActivationFunctionType.Identity
     eng = {"v": g.vector, "a": g.scalar, "p": g.tensor, "g": g, "s": g.sync}
     total = {}
     know = {q: {} for q in eng}
@@ -105,83 +105,80 @@ def rank_program(g, core, T, topo):
             for s, n in t[3].items():
                 know[q][s] = max(know[q].get(s, 0), n)
 
-    def before(q, reads, writes, banks):
+    def before(q, reads, writes):
         toks = [wrote[k] for k in reads if k in wrote]
-        for k in list(writes) + list(banks):
+        for k in writes:
             if k in wrote and (wrote[k][0] != q):
                 toks.append(wrote[k])
             toks += [t for t in read.get(k, {}).values() if t[0] != q]
         wait(q, toks)
 
-    def after(q, sem, n, reads, writes, banks):
+    def after(q, who, sem, n, reads, writes):
         total[sem] = total.get(sem, 0) + n
         clk = dict(know[q])
         clk[sem] = total[sem]
-        tok = (q, sem, total[sem], clk)
+        tok = (who, sem, total[sem], clk)
         for k in reads:
-            read.setdefault(k, {})[q] = tok
-        for k in list(writes) + list(banks):
-            wrote[k] = tok
-            read[k] = {}
-        return tok
-
-    def op(q, call, reads, writes, banks=()):
-        before(q, reads, writes, banks)
-        call().then_inc(T.sem["c" + q], 1)
-        return after(q, "c" + q, 1, reads, writes, banks)
-
-    def dma(q, out, in_, sem, reads=(), writes=()):
-        before(q, reads, writes, ())
-        eng[q].dma_start(out, in_).then_inc(T.sem[sem], 16)
-        return after(q + "dma" + sem, sem, 16, reads, writes, ()) if False else _dma_after(q, sem, reads, writes)
-
-    def _dma_after(q, sem, reads, writes):
-        total[sem] = total.get(sem, 0) + 16
-        clk = dict(know[q])
-        clk[sem] = total[sem]
-        tok = ("dma", sem, total[sem], clk)
-        for k in reads:
-            read.setdefault(k, {})["dma" + sem] = tok
+            read.setdefault(k, {})[who + sem] = tok
         for k in writes:
             wrote[k] = tok
             read[k] = {}
-        return tok
 
-    def vcopy(out, in_, reads, writes, banks=()):
-        return op("v", lambda: g.vector.tensor_copy(out, in_), reads, writes, banks)
+    def op(q, call, reads, writes):
+        before(q, reads, writes)
+        call().then_inc(T.sem["c" + q], 1)
+        after(q, q, "c" + q, 1, reads, writes)
 
-    def vts(out, in_, s1, s2, op0, op1, reads, writes, banks=()):
+    def dma(q, out, in_, sem, reads=(), writes=()):
+        before(q, reads, writes)
+        eng[q].dma_start(out, in_).then_inc(T.sem[sem], 16)
+        after(q, "dma", sem, 16, reads, writes)
+
+    def vcopy(out, in_, reads, writes):
+        op("v", lambda: g.vector.tensor_copy(out, in_), reads, writes)
+
+    def vts(out, in_, s1, s2, op0, op1, reads, writes):
         if op1 is None:
-            return op("v", lambda: g.vector.tensor_scalar(out, in_, s1, None, op0), reads, writes, banks)
-        return op("v", lambda: g.vector.tensor_scalar(out, in_, s1, s2, op0, op1), reads, writes, banks)
+            op("v", lambda: g.vector.tensor_scalar(out, in_, s1, None, op0), reads, writes)
+        else:
+            op("v", lambda: g.vector.tensor_scalar(out, in_, s1, s2, op0, op1), reads, writes)
 
-    def vtt(out, a, b, o, reads, writes, banks=()):
-        return op("v", lambda: g.vector.tensor_tensor(out, a, b, o), reads, writes, banks)
+    def vtt(out, a, b, o, reads, writes):
+        op("v", lambda: g.vector.tensor_tensor(out, a, b, o), reads, writes)
+
+    def vscan(out, d0, d1, first, op0, reads, writes):
+        op("v", lambda: g.vector.tensor_tensor_scan(out, d0, d1, first, op0, A.add), reads, writes)
 
     def vset(ap, c, writes):
-        return op("v", lambda: g.vector.memset(ap, c), [], writes)
+        op("v", lambda: g.vector.memset(ap, c), [], writes)
 
-    def act(out, in_, reads, writes, banks=(), func=COPY, scale=1.0):
-        if scale == 1.0:
-            return op("a", lambda: g.scalar.activation(out, in_, func), reads, writes, banks)
-        return op("a", lambda: g.scalar.activation(out, in_, func, scale=scale), reads, writes, banks)
+    def act(out, in_, reads, writes, func=COPY, **more):
+        op("a", lambda: g.scalar.activation(out, in_, func, **more), reads, writes)
 
-    def quant(name, tile_ap, reads):
-        return op("v", lambda: g.vector.quantize_mx(T[name][:], T[name + "s"][:], tile_ap), reads, [name])
+    def quant(name, cols, tile, reads, key):
+        a, b = cols
+        op("v", lambda: g.vector.quantize_mx(T[name][:, a:b], T[name + "s"][:, a:b], tile[:, 4 * a:4 * b]), reads, [key])
 
-    def mx(bank, w, wcols, x, xcols):
-        n = xcols[1] - xcols[0]
-        return op("p", lambda: g.tensor.matmul_mx(T["ps%d" % bank][:, 0:n], T[w][:, wcols[0]:wcols[1]], T[w + "s"][:, wcols[0]:wcols[1]],
-                                                   T[x][:, xcols[0]:xcols[1]], T[x + "s"][:, xcols[0]:xcols[1]], True, True),
-                  [w, x], [], ["ps%d" % bank])
+    def mx(bank, w, w0, x, cols, reads):
+        a, b = cols
+        op("p", lambda: g.tensor.matmul_mx(T["ps%d" % bank][:, 0:b - a], T[w][:, w0:w0 + 128], T[w + "s"][:, w0:w0 + 128],
+                                           T[x][:, a:b], T[x + "s"][:, a:b], True, True), reads, ["ps%d" % bank])
 
-    ALL = (0, C)
-    W0 = (0, 128)
-    ps = lambda b: T["ps%d" % b][:, 0:C]
-    bank = lambda b: ["ps%d" % b]
-    ends = T.St[:, 15:RUN:16]
+    def ps(bank, cols):
+        return T["ps%d" % bank][:, 0:cols[1] - cols[0]]
 
-    dma("s", T.xt[:], T.x[:], "ld_x", writes=["xt"])
+    def by(win, lst, cols):
+        return win.indirect(lst[:, cols[0] // 16:cols[1] // 16])
+
+    ALL, W0 = (0, C), (0, 128)
+    XH = ((0, XCUT), (XCUT, C))
+    ZH = ((0, ZCUT), (ZCUT, C))
+    FOUR = range(4)
+    la, lb = T.lab[:, 0:30], T.lab[:, 32:62]
+    own_scale, pair_scale, run_scale = T.rc[:, 0:1], T.rc[:, 1:2], T.ks[:, 15:16]
+
+    for h, (a, b) in enumerate(XH):
+        dma("s", T.xt[:, 4 * a:4 * b], T.x[:, 4 * a:4 * b], "ld_x%d" % h, writes=["xt%d" % h])
     dma("a", T.ut[:], T.u[:], "ld_u", writes=["ut"])
     dma("a", T.sti[:], T.st[:], "ld_st", writes=["sti"])
     dma("a", T.tai[:], T.ta[:], "ld_ta", writes=["tai"])
@@ -191,177 +188,179 @@ def rank_program(g, core, T, topo):
     dma("s", T.vt[:], T.v[:], "ld_v", writes=["vt"])
 
     vset(T.one[:], 1.0, ["one"])
+    op("g", lambda: g.iota(T.di[:], [[1, 32]], 128, -1), [], ["di"])
     op("g", lambda: g.iota(T.ip[:], [[16, 8]], 0, 0), [], ["ip"])
-    op("g", lambda: g.iota(T.qi[:], [[0, 8]], 0, 1), [], ["qi"])
-    op("g", lambda: g.iota(T.di[:], [[1, 16]], 128, -1), [], ["di"])
-    op("g", lambda: g.iota(T.i2[:], [[2, C]], 0, 0, allow_small_or_imprecise_dtypes=True), [], ["i2"])
-    op("g", lambda: g.affine_select(T.eye[:], T.one[:], [[-1, 528]], A.is_equal, 0.0, 3, 4), ["one"], ["eye"])
-    vset(T.raw[:, 2 * C:DUP], 0.0, ["rawgap"])
-    vset(T.words[:, 2 * C:DUP], 0.0, ["wordgap"])
-    vset(T.G[:, RUN:RUN + 16], 0.0, ["Gtail"])
-    vcopy(T.ip16[:], T.ip[:], ["ip"], ["ip16"])
-    c1 = slice(0, 1)
-    vts(T.qm[:], T.qi[:], 15, None, A.bitwise_and, None, ["qi"], ["qm"])
+    op("g", lambda: g.affine_select(T.eye[:], T.one[:, 0:528], [[-1, 528]], A.is_equal, 0.0, 3, 4), ["one"], ["eye"])
+    op("g", lambda: g.iota(T.i1[:], [[1, C]], BASE, 0, allow_small_or_imprecise_dtypes=True), [], ["i1"])
+    vset(T.labf[:], 0.0, ["labf0", "labf1"])
+    vset(T.G0[:, RUN:512], 0.0, ["G0tail"])
     vts(T.dm[:], T.di[:], 15, None, A.bitwise_and, None, ["di"], ["dm"])
-    vts(T.ka[:], T.qm[:], 13, 2.0 ** -27, A.is_le, A.mult, ["qm"], ["ka"])
-    vts(T.kb[:], T.qm[:], 14, 2.0 ** -11, A.is_equal, A.mult, ["qm"], ["kb"])
-    vts(T.kc[:], T.qm[:], 15, 1.0, A.is_equal, A.mult, ["qm"], ["kc"])
-    vts(T.kd[:], T.qm[:], 13, 2.0 ** 28, A.is_le, A.mult, ["qm"], ["kd"])
-    vts(T.ke[:], T.qm[:], 14, 2.0 ** 12, A.is_equal, A.mult, ["qm"], ["ke"])
-    vts(T.wp[:], T.qm[:], 15, 2.0 ** -11, A.is_equal, A.mult, ["qm"], ["wp"])
+    vcopy(T.ip16[:], T.ip[:], ["ip"], ["ip16"])
+    vcopy(T.G[:, RUN:512], T.labf[:, 0:16], ["labf0"], ["Gtail"])
     vts(T.ma[:], T.dm[:], 1, 2047.0, A.is_equal, A.mult, ["dm"], ["ma"])
-    vts(T.mb[:], T.dm[:], 2, 65535.0, A.is_equal, A.mult, ["dm"], ["mb"])
+    vts(T.mb[:], T.dm[:], 2, 511.0, A.is_equal, A.mult, ["dm"], ["mb"])
     vts(T.mc[:], T.dm[:], 0, 1.0, A.not_equal, A.mult, ["dm"], ["mc"])
-    vtt(T.ka[:], T.ka[:], T.kb[:], A.add, ["ka", "kb"], ["ka"])
-    vtt(T.kd[:], T.kd[:], T.ke[:], A.add, ["kd", "ke"], ["kd"])
-    vts(T.ke[:], T.kc[:], 2.0, None, A.mult, None, ["kc", "kd"], ["ke"])
+    vts(T.oh[:], T.dm[:], 0, 2.0 ** -15, A.is_equal, A.mult, ["dm"], ["oh"])
     vtt(T.ma[:], T.ma[:], T.mb[:], A.add, ["ma", "mb"], ["ma"])
-    vtt(T.sc[:], T.ka[:], T.kc[:], A.add, ["ka", "kc"], ["sc"])
-    vtt(T.si[:], T.kd[:], T.ke[:], A.add, ["kd", "ke"], ["si"])
-    vtt(T.d0[:, 0:16], T.ma[:], T.mc[:], A.add, ["ma", "mc"], ["d0"])
-    vts(T.sch[:], T.sc[:], 0.5, None, A.mult, None, ["sc"], ["sch"])
-    vcopy(T.la[:, 0:30], T.tai[:], ["tai"], ["la"])
-    vcopy(T.lb[:, 0:30], T.tbi[:], ["tbi"], ["lb"])
+    vtt(T.d0[:, 0:32], T.ma[:], T.mc[:], A.add, ["ma", "mc"], ["d0"])
+    vscan(T.ks[:], T.d0[:, 0:32], T.oh[:], 0.0, A.mult, ["d0", "oh"], ["ks"])
+    vtt(T.ks[:, 16:17], T.ks[:, 16:17], T.ks[:, 15:16], A.add, ["ks"], ["ks"])
+    op("v", lambda: g.vector.reciprocal(T.rc[:, 0:2], T.ks[:, 15:17]), ["ks"], ["rc"])
+    for k in (0, 1):
+        act(T.words[:, 2 * C + 544 * k:2 * C + 544 * (k + 1)], T.one[:], ["one"], ["wordgap"])
+    n = 32
+    while n < 512:
+        act(T.d0[:, n:2 * n], T.d0[:, 0:n], ["d0"], ["d0"])
+        n *= 2
+    act(T.i5[:], T.i1[:], ["i1"], ["i5"], scale=2.0 ** -9)
+    quant("qu", W0, T.ut, ["ut"], "qu")
+    vcopy(T.qr[:, 0:128].bitcast(dt.uint32), T.qu[:, 0:128].bitcast(dt.uint32).indirect(T.ip16[:, 0:8]), ["qu", "ip16"], ["qr"])
+    act(T.qrs[:, 0:128], T.qus[:, 0:128].indirect(T.ip16[:, 0:8]), ["qu", "ip16"], ["qrs"])
+    for b in FOUR:
+        op("v", lambda: g.vector.quantize_mx(T["qe%d" % b][:], T["qe%ds" % b][:], T.eye[:, 3 - b:515 - b]), ["eye"], ["qe%d" % b])
     vcopy(T.sl0[:, 0:30], T.sti[:], ["sti"], ["sl0"])
     vcopy(T.sl0[:, 30:31], T.sti[:, 0:1], ["sti"], ["sl0"])
-    n = 16
-    while n < RUN:
-        m = min(n, RUN - n)
-        vcopy(T.d0[:, n:n + m], T.d0[:, 0:m], ["d0"], ["d0"])
-        n += m
-    quant("qu", T.ut[:], ["ut"])
-    quant_pick = T.qu[:, 0:128].bitcast(dt.uint32).indirect(T.ip16[:, 0:8])
-    vcopy(T.qr[:, 0:128].bitcast(dt.uint32), quant_pick, ["qu", "ip16"], ["qr"])
-    vcopy(T.qrs[:, 0:128], T.qus[:, 0:128].indirect(T.ip16[:, 0:8]), ["qu", "ip16"], ["qrs"])
-    quant("q0", T.xt[:], ["xt"])
-    for b in range(4):
-        quant("qe%d" % b, T.eye[:, 3 - b:515 - b], ["eye"])
-    vcopy(T.d0h[:], T.d0[:, 0:C], ["d0"], ["d0h"])
-    vts(T.s2[:, 0:L], T.sl0[:, 0:L], T.si[:, c1], None, A.mult, None, ["sl0", "si"], ["s2"])
-    vcopy(T.laf[:, 0:30], T.tai[:], ["tai"], ["laf"])
-    vcopy(T.lbf[:, 0:30], T.tbi[:], ["tbi"], ["lbf"])
-    vtt(T.df[:, 0:30], T.lbf[:, 0:30], T.laf[:, 0:30], A.subtract, ["laf", "lbf"], ["df"])
+    vcopy(la, T.tai[:], ["tai"], ["lab"])
+    vcopy(lb, T.tbi[:], ["tbi"], ["lab"])
 
-    def tables():
-        act(T.raw[:, 0:2 * C:2], T.i2[:, 0:C].indirect(T.la[:, 0:30]), ["i2", "la"], ["raw0"])
-        act(T.raw[:, 1:2 * C:2], T.i2[:, 0:C].indirect(T.lb[:, 0:30]), ["i2", "lb"], ["raw1"])
+    def first_offsets(sl):
+        vts(T.s2[:, 0:L], T[sl][:, 0:L], 0.25, run_scale, A.add, A.mult, [sl, "ks"], ["s2"])
 
-    def scan():
-        return op("v", lambda: g.vector.tensor_tensor_scan(T.St[:], T.d0[:], T.G[:, 0:RUN], 0.0, A.mult, A.add), ["d0", "G"], ["St"])
+    def half_difference():
+        vts(T.hs[:, 0:30], T.hn[:, 0:30], own_scale, 2.0 ** -15, A.mult, A.mult, ["hn", "rc"], ["hs"])
 
-    def send(r, dst, name, land, cols, sem, reads, codes=False):
+    def send(dst, name, land, cols, sem, reads, codes=False):
         rid, pid = topo.addr(dst)[:2]
-        mask = topo.mask(core, dst)
-        before("g", reads, [], [])
+        before("g", reads, [])
         n = len(topo.engines(core, dst))
         src, out = T[name][:, 0:cols], T[land][:, 0:cols]
         if codes:
             src, out = src.bitcast(dt.uint8), out.bitcast(dt.uint8)
-        g.remote_dma(out, src, T.sem[sem], T.sem.left, pid, rid, mask)
+        g.remote_dma(out, src, T.sem[sem], T.sem.left, pid, rid, topo.mask(core, dst))
         total["left"] = total.get("left", 0) + n
         total[sem] = total.get(sem, 0) + n
 
-    def arrives(keys, sem):
-        for k in keys:
-            wrote[k] = ("far", sem, total[sem], {sem: total[sem]})
+    def arrives(key, sem):
+        wrote[key] = ("far", sem, total[sem], {sem: total[sem]})
+
+    def scored(q, h, tile, reads):
+        quant(q, XH[h], tile, reads, q + "h%d" % h)
+        mx(h, "qr", 0, q, XH[h], ["qr", "qrs", q + "h%d" % h])
+        act(T.sg[:, XH[h][0]:XH[h][1]], ps(h, XH[h]), ["ps%d" % h], ["ps%d" % h, "sg%d" % h], func=SIGN, bias=-TINY)
+
+    def exchange():
+        vscan(T.xs[:], T.d0[:, 0:C], T.sv[:], 0.0, A.mult, ["d0", "sv"], ["xs"])
+        vtt(T.hn[:, 0:30], T.xs[:, 15:C:16], T.hs[:, 0:30], A.mult, ["xs", "hs"], ["hn"])
+        vtt(T.labf[:, 0:30], T.m2[:, 0:30], T.hn[:, 0:30], A.subtract, ["m2", "hn"], ["labf0"])
+        vtt(T.labf[:, 32:62], T.m2[:, 0:30], T.hn[:, 0:30], A.add, ["m2", "hn"], ["labf1"])
+        vts(T.lab[:, 0:62], T.labf[:, 0:62], 0.5, None, A.mult, None, ["labf0", "labf1"], ["lab"])
+
+    scored("q0", 0, T.xt, ["xt0"])
+    first_offsets("sl0")
+    scored("q0", 1, T.xt, ["xt1"])
 
     for r, step in enumerate(STEP):
         last = r == len(STEP) - 1
         dst = T.cores[rank ^ step]
-        q, ql, ll, sl, sn = "q%d" % r, "ql%d" % r, "ll%d" % r, "sl%d" % r, "sl%d" % (r + 1)
-        send(r, dst, q, ql, C, "rq%d" % r, [q], codes=True)
-        send(r, dst, q + "s", ql + "s", C, "rq%d" % r, [q])
-        arrives([ql], "rq%d" % r)
-        op("p", lambda: g.tensor.matmul_mx(ps(0), T.qr[:], T.qrs[:], T[q][:], T[q + "s"][:], True, True), ["qr", "qrs", q], [], bank(0))
-        tables()
-        vts(T.t[:], ps(0), 0.0, float(DUP), A.is_gt, A.mult, [], ["t"], bank(0)) if False else None
-        op("v", lambda: g.vector.tensor_scalar(T.t[:], ps(0), 0.0, float(DUP), A.is_gt, A.mult), ["ps0"], ["t"], bank(0))
-        act(T.G[:, 0:RUN], T.t[:, 0:C].indirect(T[sl][:, 0:L]), ["t", sl], ["G"])
-        for h, ls in ((0, "la"), (1, "lb")):
-            vtt(T.words[:, h:2 * C:2], T.t[:, 0:C].indirect(T[ls][:, 0:30]), T.raw[:, h:2 * C:2], A.add, ["t", ls, "raw%d" % h], ["words%d" % h])
-            act(T.words[:, DUP + h:WIN:2], T.words[:, h:2 * C:2], ["words%d" % h], ["dup%d" % h])
-        act(T.raw[:, DUP:WIN], T.raw[:, 0:2 * C], ["raw0", "raw1"], ["rawdup"])
-        for b in range(4):
-            mx(2 + b, "qe%d" % b, W0, q, ALL)
-            act(T["to%d" % b][:], ps(2 + b), ["ps%d" % (2 + b)], ["to%d" % b], bank(2 + b))
-        for b, k in enumerate((6, 7, 2, 3)):
-            mx(k, "qe%d" % b, W0, ql, ALL)
-            act(T["tp%d" % b][:], ps(k), ["ps%d" % k], ["tp%d" % b], bank(k))
-        for k in range(STAGES):
-            if k:
-                op("v", lambda: g.vector.tensor_copy(T.G[:, 0:RUN], T.words[:, 0:WIN].indirect(T.o[:, 0:L])),
-                   ["o", "words0", "words1", "dup0", "dup1", "wordgap"], ["G"])
-            scan()
-            vts(T.wt[:, 0:L], T.G[:, 16:RUN + 16:16], T.wp[:, c1], None, A.mult, None, ["G", "Gtail", "wp"], ["wt"])
-            if k == 0:
-                vtt(T.wt[:, 0:L], T.wt[:, 0:L], T.s2[:, 0:L], A.add, ["wt", "s2"], ["wt"])
-            vtt(T.sm[:, 0:L], ends, T.wt[:, 0:L], A.add, ["St", "wt"], ["sm"])
-            vts(T.o[:, 0:L], T.sm[:, 0:L], T.sc[:, c1], 0.015625, A.mult, A.add, ["sm", "sc"], ["o"])
-        vcopy(T.G[:, 0:RUN], T.raw[:, 0:WIN].indirect(T.o[:, 0:L]), ["o", "raw0", "raw1", "rawdup", "rawgap"], ["G"])
-        scan()
-        vts(T[sn][:, 0:L], ends, T.sch[:, c1], 0.015625, A.mult, A.add, ["St", "sch"], [sn])
-        send(r, dst, sn, ll, 30, "rl%d" % r, [sn])
-        arrives([ll], "rl%d" % r)
-        own = T[sn][:, 0:30]
-        for b in (0, 1):
-            act(T["zo%d" % b][:], T["to%d" % b][:, 0:C].indirect(own), ["to%d" % b, sn], ["zo%d" % b])
-        for b in (2, 3):
-            vcopy(T["zo%d" % b][:], T["to%d" % b][:, 0:C].indirect(own), ["to%d" % b, sn], ["zo%d" % b])
-        if not last:
-            vts(T.s2[:, 0:L], T[sn][:, 0:L], T.si[:, c1], None, A.mult, None, [sn, "si"], ["s2"])
+        q, ql, ll, sl, sn, qn = "q%d" % r, "ql%d" % r, "ll%d" % r, "sl%d" % r, "sl%d" % (r + 1), "q%d" % (r + 1)
+        QS, SG = [q + "h0", q + "h1"], ["sg0", "sg1"]
+        send(dst, q, ql, C, "rq%d" % r, QS, codes=True)
+        send(dst, q + "s", ql + "s", C, "rq%d" % r, QS)
+        arrives(ql, "rq%d" % r)
+        vscan(T.t[:], T.sg[:], T.i5[:], 2.0, A.min, SG + ["i5"], ["t"])
+        act(T.G0[:, 0:RUN], T.sg[:, 0:C].indirect(T[sl][:, 0:L]), SG + [sl], ["G0"], scale=2.0 ** -17)
+        vcopy(T.words[:, 0:2 * C:2], T.t[:, 0:C].indirect(la), ["t", "lab"], ["words0"])
+        act(T.words[:, 1:2 * C:2], T.t[:, 0:C].indirect(lb), ["t", "lab"], ["words1"])
+        act(T.words[:, DUP:WIN], T.words[:, 0:2 * C], ["words0", "words1"], ["dup"])
         if r == 0:
-            quant("qv", T.vt[:], ["vt"])
+            for k in (0, 1):
+                act(T.raw[:, 2 * C + 544 * k:2 * C + 544 * (k + 1)], T.one[:], ["one"], ["rawgap"])
+        act(T.raw[:, 0:2 * C:2], T.i5[:, 0:C].indirect(la), ["i5", "lab"], ["raw0"])
+        act(T.raw[:, 1:2 * C:2], T.i5[:, 0:C].indirect(lb), ["i5", "lab"], ["raw1"])
+        act(T.raw[:, DUP:WIN], T.raw[:, 0:2 * C], ["raw0", "raw1"], ["rawdup"])
+        for name, codes, reads, banks in (("to", q, QS, (2, 3, 4, 5)), ("tp", ql, [ql], (6, 7, 0, 1))):
+            for b, k in enumerate(banks):
+                mx(k, "qe%d" % b, 0, codes, ALL, ["qe%d" % b] + reads)
+                act(T[name + "%d" % b][:], ps(k, ALL), ["ps%d" % k], ["ps%d" % k, name + "%d" % b])
+        vscan(T.St0[:, 0:RUN], T.d0[:, 0:RUN], T.G0[:, 1:RUN + 1], 0.0, A.mult, ["d0", "G0", "G0tail"], ["St0"])
+        vtt(T.sm[:, 0:L], T.St0[:, 15:RUN:16], T.s2[:, 0:L], A.add, ["St0", "s2"], ["sm"])
+        vts(T.o[:, 0:L], T.sm[:, 0:L], own_scale, 2.0, A.mult, A.mult, ["sm", "rc"], ["o"])
+        for k in range(STAGES - 1):
+            win, keys = (2 * C, []) if k == 0 else (WIN, ["dup", "wordgap"])
+            vts(T.G[:, 0:RUN], T.words[:, 0:win].indirect(T.o[:, 0:L]), -2.0, 2.0 ** -5, A.add, A.mult,
+                ["o", "words0", "words1"] + keys, ["G"])
+            vscan(T.St[:, 0:RUN + 2], T.d0[:, 0:RUN + 2], T.G[:, 0:RUN + 2], 0.0, A.mult, ["d0", "G", "Gtail"], ["St"])
+            vtt(T.sm[:, 0:L], T.St[:, 15:RUN:16], T.St[:, 16:RUN + 1:16], A.add, ["St"], ["sm"])
+            vts(T.o[:, 0:L], T.sm[:, 0:L], pair_scale, 962.25, A.mult, A.add, ["sm", "rc"], ["o"])
+        vts(T.G[:, 0:RUN], T.raw[:, 0:WIN].indirect(T.o[:, 0:L]), -BASE / 512.0, 2.0 ** -5, A.add, A.mult,
+            ["o", "raw0", "raw1", "rawdup", "rawgap"], ["G"])
+        vscan(T.St[:, 0:RUN], T.d0[:, 0:RUN], T.G[:, 0:RUN], 0.0, A.mult, ["d0", "G"], ["St"])
+        vts(T[sn][:, 0:L], T.St[:, 15:RUN:16], own_scale, 0.5, A.mult, A.mult, ["St", "rc"], [sn])
+        send(dst, sn, ll, 30, "rl%d" % r, [sn])
+        arrives(ll, "rl%d" % r)
+        own = T[sn][:, 0:30]
+        for b in (0, 1, 2):
+            vcopy(T["zo%d" % b][:], T["to%d" % b][:, 0:C].indirect(own), ["to%d" % b, sn], ["zo%d" % b])
+        act(T.zo3[:], T.to3[:, 0:C].indirect(own), ["to3", sn], ["zo3"])
+        if r == 0:
+            vtt(T.m2[:, 0:30], T.tai[:], T.tbi[:], A.add, ["tai", "tbi"], ["m2"])
+            vtt(T.hn[:, 0:30], T.tbi[:], T.tai[:], A.subtract, ["tai", "tbi"], ["hn"])
+            quant("qv", W0, T.vt, ["vt"], "qv")
+        half_difference()
         if last:
-            vts(T.opb[:, 0:C], T.G[:, 0:C], 0.5, None, A.mult, None, ["G"], ["op0"])
-        far = T[ll][:, 0:30]
-        for b in (0, 1):
-            act(T.Zp[:, b:4 * C:4], T["tp%d" % b][:, 0:C].indirect(far), ["tp%d" % b, ll], ["Zp%d" % b])
-        for b in (2, 3):
-            vcopy(T.Zp[:, b:4 * C:4], T["tp%d" % b][:, 0:C].indirect(far), ["tp%d" % b, ll], ["Zp%d" % b])
-        quant("qz", T.Zp[:], ["Zp%d" % b for b in range(4)])
-        for b in (2, 3):
-            vts(T["l%d" % b][:, 0:30], far, 4, b, A.mult, A.add, [ll], ["l%d" % b])
-        for b in range(4):
-            op("p", lambda: g.tensor.matmul_mx(ps(4 + b), T.wq[:, 128 * b:128 * b + 128], T.wqs[:, 128 * b:128 * b + 128], T.qz[:], T.qzs[:], True, True),
-               ["wq", "wqs", "qz"], [], bank(4 + b))
-            if b < 2:
-                act(T["hw%d" % b][:], ps(4 + b), ["ps%d" % (4 + b)], ["hw%d" % b], bank(4 + b), scale=0.03125)
+            vts(T.opb[:, 0:C], T.G[:, 0:C], 2.0 ** 14, None, A.mult, None, ["G"], ["op0"])
+        else:
+            first_offsets(sn)
+        far = T[ll]
+        hbanks = ((2, 3, 4, 5), (6, 7, 0, 1))
+        for h, (a, e) in enumerate(ZH):
+            for b in (0, 1):
+                act(T.Zp[:, 4 * a + b:4 * e:4], by(T["tp%d" % b][:, 0:C], far, ZH[h]), ["tp%d" % b, ll], ["Zp%d%d" % (h, b)])
+            for b in (2, 3):
+                vcopy(T.Zp[:, 4 * a + b:4 * e:4], by(T["tp%d" % b][:, 0:C], far, ZH[h]), ["tp%d" % b, ll], ["Zp%d%d" % (h, b)])
+            quant("qz", ZH[h], T.Zp, ["Zp%d%d" % (h, b) for b in FOUR], "qz%d" % h)
+            for b in FOUR:
+                mx(hbanks[h][b], "wq", 128 * b, "qz", ZH[h], ["wq", "wqs", "qz%d" % h])
+        for b in FOUR:
+            vts(T["l%d" % b][:, 0:30], far[:, 0:30], 4, b, A.mult, A.add, [ll], ["l%d" % b])
+        for h, b in ((0, 0), (0, 1), (0, 2), (0, 3), (1, 0), (1, 1), (1, 2), (1, 3)):
+            a, e = ZH[h]
+            k = "ps%d" % hbanks[h][b]
+            out, src, key = T.H[:, 4 * a + b:4 * e:4], ps(hbanks[h][b], ZH[h]), "H%d%d" % (h, b)
+            if h == 0 or b == 3:
+                act(out, src, [k], [k, key], scale=0.03125)
             else:
-                act(T.H[:, b:4 * C:4], ps(4 + b), ["ps%d" % (4 + b)], ["H%d" % b], bank(4 + b), scale=0.03125)
-        for b in (0, 1):
-            vtt(T.X[:, b:4 * C:4], T["hw%d" % b][:, 0:C].indirect(far), T["zo%d" % b][:], A.add, ["hw%d" % b, ll, "zo%d" % b], ["X%d" % b])
-        for b in (0, 1):
-            vcopy(T.H[:, b:4 * C:4], T["hw%d" % b][:], ["hw%d" % b], ["H%d" % b])
-        HS = ["H%d" % b for b in range(4)]
-        quant("qh", T.H[:], HS)
-        op("p", lambda: g.tensor.matmul_mx(ps(1), T.qr[:], T.qrs[:], T.qh[:], T.qhs[:], True, True), ["qr", "qrs", "qh"], [], bank(1))
-        act(T.sg[:], ps(1), ["ps1"], ["sg"], bank(1), func=SIGN)
-        for b in (2, 3):
-            vtt(T.X[:, b:4 * C:4], T.H[:, 0:4 * C].indirect(T["l%d" % b][:, 0:30]), T["zo%d" % b][:], A.add, HS + ["l%d" % b, "zo%d" % b], ["X%d" % b])
-        quant("q%d" % (r + 1), T.X[:], ["X%d" % b for b in range(4)])
-        op("v", lambda: g.vector.tensor_tensor_scan(T.xs[:], T.d0h[:], T.sg[:], 0.0, A.mult, A.add), ["d0h", "sg"], ["xs"])
-        vts(T.bt[:, 0:30], T.xs[:, 15:C:16], T.sc[:, c1], 0.5, A.mult, A.is_gt, ["xs", "sc"], ["bt"])
-        vtt(T.mv[:, 0:30], T.bt[:, 0:30], T.df[:, 0:30], A.mult, ["bt", "df"], ["mv"])
-        vtt(T.laf[:, 0:30], T.laf[:, 0:30], T.mv[:, 0:30], A.add, ["laf", "mv"], ["laf"])
-        vtt(T.lbf[:, 0:30], T.lbf[:, 0:30], T.mv[:, 0:30], A.subtract, ["lbf", "mv"], ["lbf"])
-        vcopy(T.la[:, 0:30], T.laf[:, 0:30], ["laf"], ["la"])
-        vcopy(T.lb[:, 0:30], T.lbf[:, 0:30], ["lbf"], ["lb"])
+                vts(out, src, 0.03125, None, A.mult, None, [k], [k, key])
+        HS = ["H%d%d" % (h, b) for h in (0, 1) for b in FOUR]
+        quant("qh", ALL, T.H, HS, "qh")
+        mx(2, "qr", 0, "qh", ALL, ["qr", "qrs", "qh"])
+        act(T.sv[:], ps(2, ALL), ["ps2"], ["ps2", "sv"], func=SIGN, bias=TINY, scale=-1.0)
+        for h, (a, e) in enumerate(XH):
+            if last and h == 1:
+                exchange()
+                act(T.opb[:, C:2 * C], T.i1[:, 0:C].indirect(la), ["i1", "lab"], ["op1"], func=IDENT, bias=-float(BASE))
+                act(T.opb[:, 2 * C:3 * C], T.i1[:, 0:C].indirect(lb), ["i1", "lab"], ["op2"], func=IDENT, bias=-float(BASE))
+                dma("a", T.op[:], T.opb[0:128:16, :], "out", reads=["op0", "op1", "op2"])
+            for b in FOUR:
+                vtt(T.X[:, 4 * a + b:4 * e:4], by(T.H[:, 0:4 * C], T["l%d" % b], XH[h]), T["zo%d" % b][:, a:e], A.add,
+                    HS + ["l%d" % b, "zo%d" % b], ["X%d%d" % (h, b)])
+            XS = ["X%d%d" % (h, b) for b in FOUR]
+            if not last:
+                scored(qn, h, T.X, XS)
+                continue
+            key = qn + "h%d" % h
+            quant(qn, XH[h], T.X, XS, key)
+            dma("s", T.oc[:, 4 * a:4 * e], T[qn][:, a:e].bitcast(dt.uint8), "out", reads=[key])
+            mx(h, "qv", 0, qn, XH[h], ["qv", key])
+            if h == 0:
+                act(T.yb[:, a:e], ps(h, XH[h]), ["ps0"], ["ps0", "y0"])
+            else:
+                vcopy(T.yb[:, a:e], ps(h, XH[h]), ["ps1"], ["ps1", "y1"])
+                for k in FOUR:
+                    dma("s", T.osc[4 * k:4 * k + 4, :], T[qn + "s"][32 * k:32 * k + 4, :], "out", reads=[qn + "h0", key])
+            dma("s", T.y[:, a:e], T.yb[:, a:e], "out", reads=["y%d" % h])
         if not last:
-            vtt(T.df[:, 0:30], T.lbf[:, 0:30], T.laf[:, 0:30], A.subtract, ["laf", "lbf"], ["df"])
-
-    dma("s", T.oc[:], T.q3[:].bitcast(dt.uint8), "out", reads=["q3"])
-    for k in range(4):
-        dma("s", T.osc[4 * k:4 * k + 4, :], T.q3s[32 * k:32 * k + 4, :], "out", reads=["q3"])
-    half = C // 2
-    mx(0, "qv", W0, "q3", (0, half))
-    mx(2, "qv", W0, "q3", (half, C))
-    op("a", lambda: g.scalar.activation(T.yb[:, 0:half], T.ps0[:, 0:half], COPY), ["ps0"], ["y0"], bank(0))
-    dma("s", T.y[:, 0:half], T.yb[:, 0:half], "out", reads=["y0"])
-    op("v", lambda: g.vector.tensor_copy(T.yb[:, half:C], T.ps2[:, 0:half]), ["ps2"], ["y1"], bank(2))
-    dma("s", T.y[:, half:C], T.yb[:, half:C], "out", reads=["y1"])
-    act(T.opb[:, C:2 * C], T.i2[:, 0:C].indirect(T.la[:, 0:30]), ["i2", "la"], ["op1"], scale=0.5)
-    vts(T.opb[:, 2 * C:3 * C], T.i2[:, 0:C].indirect(T.lb[:, 0:30]), 0.5, None, A.mult, None, ["i2", "lb"], ["op2"])
-    dma("s", T.op[:], T.opb[0:128:16, :], "out", reads=["op0", "op1", "op2"])
+            exchange()
     for s in sorted(total):
         if know["g"].get(s, 0) < total[s]:
             g.wait_ge(T.sem[s], total[s])

@@ -1,16 +1,20 @@
 from concourse.mybir import dt, AluOpType, ActivationFunctionType
 
 C = 480
-L = 31
+L = 33
 RUN = 16 * L
+HALF = 256
 DUP = 2048
 WIN = DUP + 2 * C
 STEP = [1, 2, 3]
 STAGES = 5
 XCUT = 352
-ZCUT = 288
+ZCUT = 224
 BASE = 1055
+DCUT = 512
 TINY = 2.0 ** -100
+BIG = 2.0 ** 20
+LAYER = [(h, b) for h in (0, 1) for b in range(4)]
 
 SCRATCH = {}
 
@@ -31,11 +35,11 @@ _add("wqs", [128, 512], "uint8")
 for _r in range(4):
     _add("q%d" % _r, [128, C], CODES)
     _add("q%ds" % _r, [128, C], "uint8")
-    _add("sl%d" % _r, [128, 32], "uint16")
 for _r in range(3):
     _add("ql%d" % _r, [128, C], CODES)
     _add("ql%ds" % _r, [128, C], "uint8")
     _add("ll%d" % _r, [128, 32], "uint16")
+    _add("sn%d" % _r, [128, 32], "uint16")
 for _n in ("qz", "qh"):
     _add(_n, [128, C], CODES)
     _add(_n + "s", [128, C], "uint8")
@@ -45,31 +49,41 @@ for _b in range(4):
     _add("to%d" % _b, [128, C], "bfloat16")
     _add("tp%d" % _b, [128, C], "bfloat16")
     _add("zo%d" % _b, [128, C], "bfloat16")
-    _add("l%d" % _b, [128, 32], "uint16")
-for _n in ("sg", "sv", "xs"):
+for _n in ("hw0", "hw1", "sg", "sv", "xs", "d15"):
     _add(_n, [128, C], "bfloat16")
 for _n in ("raw", "words"):
     _add(_n, [128, WIN], "float32")
-for _n in ("t", "i1", "i5"):
+for _n in ("t", "i1", "i5", "row", "rowscan"):
     _add(_n, [128, C], "float32")
 for _n in ("G", "St"):
-    _add(_n, [128, 512], "float16")
-for _n in ("G0", "St0", "d0"):
-    _add(_n, [128, 512], "bfloat16")
+    _add(_n, [128, 544], "float16")
+for _n in ("G0", "St0", "dring"):
+    _add(_n, [128, 544], "bfloat16")
+_add("d16", [128, 512], "bfloat16")
+_add("dlast", [128, HALF], "bfloat16")
 _add("one", [128, 544], "bfloat16")
 _add("eye", [128, 528], "bfloat16")
-for _n in ("sm", "s2", "m2", "hs", "hn", "ma", "mb", "mc", "oh", "ks"):
+for _n in ("m2", "hs", "hn", "ma", "mb", "mc", "md", "oh", "ks"):
     _add(_n, [128, 32], "float32")
+for _n in ("sm", "s2", "F"):
+    _add(_n, [128, 48], "float32")
 _add("labf", [128, 64], "float32")
 _add("lab", [128, 64], "uint16")
-_add("o", [128, 32], "uint16")
+for _n in ("o", "sl"):
+    _add(_n, [128, 34], "uint16")
+for _n in ("s0", "l2", "l3"):
+    _add(_n, [128, 32], "uint16")
 for _n in ("sti", "tai", "tbi"):
     _add(_n, [128, 30], "int32")
-_add("di", [128, 32], "int32")
-_add("dm", [128, 32], "int32")
+for _n in ("di", "dm", "dj", "dn"):
+    _add(_n, [128, 32], "int32")
+for _n in ("ki", "km"):
+    _add(_n, [128, 16], "int32")
+_add("od", [128, 16], "uint16")
 _add("ip", [128, 8], "int32")
 _add("ip16", [128, 8], "uint16")
-_add("rc", [128, 8], "float32")
+for _n in ("rc", "col"):
+    _add(_n, [128, 8], "float32")
 _add("yb", [128, C], "float32")
 _add("opb", [128, 3 * C], "float32")
 for _b in range(8):
@@ -77,7 +91,7 @@ for _b in range(8):
 
 LOADS = ["x0", "x1", "u", "st", "ta", "tb", "wc", "ws", "v"]
 SEMAPHORES = ["cv", "ca", "cp", "cg", "out", "left"] + ["ld_" + n for n in LOADS]
-SEMAPHORES += ["rq%d" % r for r in range(3)] + ["rl%d" % r for r in range(3)]
+SEMAPHORES += ["rq%d" % r for r in range(3)] + ["rl%d%d" % (r, h) for r in range(3) for h in (0, 1)]
 
 
 def rank_program(g, core, T, topo):
@@ -155,6 +169,15 @@ def rank_program(g, core, T, topo):
     def act(out, in_, reads, writes, func=COPY, **more):
         op("a", lambda: g.scalar.activation(out, in_, func, **more), reads, writes)
 
+    def gcopy(out, in_, n, reads, writes):
+        op("g", lambda: g.affine_select(out, in_, [[1, n]], A.is_ge, 0.0, 0, 0), reads, writes)
+
+    def repeat(copy, *jobs):
+        for k in range(5):
+            for name, n, upto in jobs:
+                m = min(n << k, upto - (n << k))
+                copy(T[name][:, n << k:(n << k) + m], T[name][:, 0:m], [name], [name])
+
     def quant(name, cols, tile, reads, key):
         a, b = cols
         op("v", lambda: g.vector.quantize_mx(T[name][:, a:b], T[name + "s"][:, a:b], tile[:, 4 * a:4 * b]), reads, [key])
@@ -175,7 +198,7 @@ def rank_program(g, core, T, topo):
     ZH = ((0, ZCUT), (ZCUT, C))
     FOUR = range(4)
     la, lb = T.lab[:, 0:30], T.lab[:, 32:62]
-    own_scale, pair_scale, run_scale = T.rc[:, 0:1], T.rc[:, 1:2], T.ks[:, 15:16]
+    own_scale, pair_scale, run_scale, one_scale = T.rc[:, 0:1], T.rc[:, 1:2], T.ks[:, 15:16], T.col[:, 1:2]
 
     for h, (a, b) in enumerate(XH):
         dma("s", T.xt[:, 4 * a:4 * b], T.x[:, 4 * a:4 * b], "ld_x%d" % h, writes=["xt%d" % h])
@@ -183,57 +206,68 @@ def rank_program(g, core, T, topo):
     dma("a", T.sti[:], T.st[:], "ld_st", writes=["sti"])
     dma("a", T.tai[:], T.ta[:], "ld_ta", writes=["tai"])
     dma("a", T.tbi[:], T.tb[:], "ld_tb", writes=["tbi"])
-    dma("s", T.wq[:].bitcast(dt.uint8), T.wc[:], "ld_wc", writes=["wq"])
+    dma("s", T.wq[:].bitcast(dt.uint8), T.wc[:], "ld_wc", reads=["xt0"], writes=["wq"])
     dma("s", T.wqs[:], T.ws[:], "ld_ws", writes=["wqs"])
     dma("s", T.vt[:], T.v[:], "ld_v", writes=["vt"])
 
     vset(T.one[:], 1.0, ["one"])
     op("g", lambda: g.iota(T.di[:], [[1, 32]], 128, -1), [], ["di"])
     op("g", lambda: g.iota(T.ip[:], [[16, 8]], 0, 0), [], ["ip"])
+    op("g", lambda: g.iota(T.ki[:], [[15, 16]], 127, 1), [], ["ki"])
     op("g", lambda: g.affine_select(T.eye[:], T.one[:, 0:528], [[-1, 528]], A.is_equal, 0.0, 3, 4), ["one"], ["eye"])
     op("g", lambda: g.iota(T.i1[:], [[1, C]], BASE, 0, allow_small_or_imprecise_dtypes=True), [], ["i1"])
+    op("g", lambda: g.iota(T.raw[:, 2 * C:DUP], [[0, DUP - 2 * C]], 0, 0, allow_small_or_imprecise_dtypes=True), [], ["rawgap"])
     vset(T.labf[:], 0.0, ["labf0", "labf1"])
-    vset(T.G0[:, RUN:512], 0.0, ["G0tail"])
+    vset(T.G0[:, RUN:544], 0.0, ["G0tail"])
     vts(T.dm[:], T.di[:], 15, None, A.bitwise_and, None, ["di"], ["dm"])
-    vcopy(T.ip16[:], T.ip[:], ["ip"], ["ip16"])
-    vcopy(T.G[:, RUN:512], T.labf[:, 0:16], ["labf0"], ["Gtail"])
-    vts(T.ma[:], T.dm[:], 1, 2047.0, A.is_equal, A.mult, ["dm"], ["ma"])
-    vts(T.mb[:], T.dm[:], 2, 511.0, A.is_equal, A.mult, ["dm"], ["mb"])
-    vts(T.mc[:], T.dm[:], 0, 1.0, A.not_equal, A.mult, ["dm"], ["mc"])
-    vts(T.oh[:], T.dm[:], 0, 2.0 ** -15, A.is_equal, A.mult, ["dm"], ["oh"])
+    vcopy(T.G[:, RUN:544], T.labf[:, 0:16], ["labf0"], ["Gtail"])
+    vts(T.col[:, 0:1], T.dm[:, 0:1], 0, None, A.is_equal, None, ["dm"], ["first"])
+    vts(T.col[:, 2:3], T.dm[:, 0:1], 1, 2.0 ** -20 - 1.0, A.not_equal, A.mult, ["dm"], ["col2"])
+    vts(T.dj[:], T.di[:], T.col[:, 0:1], None, A.subtract, None, ["di", "first"], ["dj"])
+    vts(T.col[:, 1:2], T.col[:, 2:3], 1.0, None, A.add, None, ["col2"], ["one_scale"])
+    vts(T.dn[:], T.dj[:], 15, None, A.bitwise_and, None, ["dj"], ["dn"])
+    vts(T.F[:, 16:32], T.dm[:, 0:16], 0, None, A.not_equal, None, ["dm"], ["F1"])
+    vts(T.ma[:], T.dn[:], 1, 2047.0, A.is_equal, A.mult, ["dn"], ["ma"])
+    vts(T.mb[:], T.dn[:], 2, 511.0, A.is_equal, A.mult, ["dn"], ["mb"])
+    vts(T.mc[:], T.dn[:], 0, None, A.not_equal, None, ["dn"], ["mc"])
+    vts(T.md[:], T.dn[:], 1, BIG - 1.0, A.is_equal, A.mult, ["dn"], ["md"])
+    vts(T.oh[:], T.dn[:], 0, 2.0 ** -15, A.is_equal, A.mult, ["dn"], ["oh"])
     vtt(T.ma[:], T.ma[:], T.mb[:], A.add, ["ma", "mb"], ["ma"])
-    vtt(T.d0[:, 0:32], T.ma[:], T.mc[:], A.add, ["ma", "mc"], ["d0"])
-    vscan(T.ks[:], T.d0[:, 0:32], T.oh[:], 0.0, A.mult, ["d0", "oh"], ["ks"])
-    vtt(T.ks[:, 16:17], T.ks[:, 16:17], T.ks[:, 15:16], A.add, ["ks"], ["ks"])
+    vtt(T.d15[:, 0:15], T.md[:, 1:16], T.mc[:, 1:16], A.add, ["md", "mc"], ["d15"])
+    vtt(T.dring[:, 0:32], T.ma[:], T.mc[:], A.add, ["ma", "mc"], ["dring"])
+    vts(T.mb[:, 0:16], T.dm[:, 0:16], 1, BIG - 1.0, A.is_equal, A.mult, ["dm", "ma"], ["mb"])
+    vscan(T.ks[:], T.dring[:, 0:32], T.oh[:], 0.0, A.mult, ["dring", "oh"], ["ks"])
+    vts(T.F[:, 32:48], T.F[:, 16:32], 1.0 - BIG, BIG, A.mult, A.add, ["F1"], ["F2"])
+    vtt(T.F[:, 0:16], T.mb[:, 0:16], T.F[:, 16:32], A.add, ["mb", "F1"], ["F0"])
     op("v", lambda: g.vector.reciprocal(T.rc[:, 0:2], T.ks[:, 15:17]), ["ks"], ["rc"])
+    vcopy(T.ip16[:], T.ip[:], ["ip"], ["ip16"])
+    vts(T.col[:, 3:4], T.dm[:, 0:1], 15, 16.0, A.is_equal, A.mult, ["dm"], ["col3"])
+    vts(T.km[:], T.ki[:], 15, None, A.bitwise_and, None, ["ki"], ["km"])
+    vts(T.col[:, 4:5], T.col[:, 0:1], 32.0, T.col[:, 3:4], A.mult, A.add, ["first", "col3"], ["col4"])
+    vts(T.od[:], T.km[:], T.col[:, 4:5], None, A.add, None, ["km", "col4"], ["od"])
     for k in (0, 1):
         act(T.words[:, 2 * C + 544 * k:2 * C + 544 * (k + 1)], T.one[:], ["one"], ["wordgap"])
-    n = 32
-    while n < 512:
-        act(T.d0[:, n:2 * n], T.d0[:, 0:n], ["d0"], ["d0"])
-        n *= 2
-    act(T.i5[:], T.i1[:], ["i1"], ["i5"], scale=2.0 ** -9)
-    quant("qu", W0, T.ut, ["ut"], "qu")
-    vcopy(T.qr[:, 0:128].bitcast(dt.uint32), T.qu[:, 0:128].bitcast(dt.uint32).indirect(T.ip16[:, 0:8]), ["qu", "ip16"], ["qr"])
-    act(T.qrs[:, 0:128], T.qus[:, 0:128].indirect(T.ip16[:, 0:8]), ["qu", "ip16"], ["qrs"])
+    repeat(act, ("d15", 15, C), ("dring", 32, 544))
     for b in FOUR:
         op("v", lambda: g.vector.quantize_mx(T["qe%d" % b][:], T["qe%ds" % b][:], T.eye[:, 3 - b:515 - b]), ["eye"], ["qe%d" % b])
-    vcopy(T.sl0[:, 0:30], T.sti[:], ["sti"], ["sl0"])
-    vcopy(T.sl0[:, 30:31], T.sti[:, 0:1], ["sti"], ["sl0"])
-    vcopy(la, T.tai[:], ["tai"], ["lab"])
-    vcopy(lb, T.tbi[:], ["tbi"], ["lab"])
+    vts(T.i5[:], T.i1[:], 2.0 ** -9, None, A.mult, None, ["i1"], ["i5"])
+    quant("qu", W0, T.ut, ["ut"], "qu")
+    vcopy(T.s0[:, 0:30], T.sti[:], ["sti"], ["s0"])
+    vcopy(T.qr[:, 0:128].bitcast(dt.uint32), T.qu[:, 0:128].bitcast(dt.uint32).indirect(T.ip16[:, 0:8]), ["qu", "ip16"], ["qr"])
+    act(T.qrs[:, 0:128], T.qus[:, 0:128].indirect(T.ip16[:, 0:8]), ["qu", "ip16"], ["qrs"])
+    act(T.row[:], by(T.i1[:, 0:C], T.s0, ALL), ["i1", "s0"], ["row"])
 
-    def first_offsets(sl):
-        vts(T.s2[:, 0:L], T[sl][:, 0:L], 0.25, run_scale, A.add, A.mult, [sl, "ks"], ["s2"])
+    def first_offsets():
+        vts(T.s2[:, 0:L], T.sl[:, 0:L], 0.25, run_scale, A.add, A.mult, ["sl", "ks"], ["s2"])
 
     def half_difference():
-        vts(T.hs[:, 0:30], T.hn[:, 0:30], own_scale, 2.0 ** -15, A.mult, A.mult, ["hn", "rc"], ["hs"])
+        vts(T.hs[:, 0:30], T.hn[:, 0:30], one_scale, None, A.mult, None, ["hn", "one_scale"], ["hs"])
 
     def send(dst, name, land, cols, sem, reads, codes=False):
         rid, pid = topo.addr(dst)[:2]
         before("g", reads, [])
         n = len(topo.engines(core, dst))
-        src, out = T[name][:, 0:cols], T[land][:, 0:cols]
+        src, out = T[name][:, cols[0]:cols[1]], T[land][:, cols[0]:cols[1]]
         if codes:
             src, out = src.bitcast(dt.uint8), out.bitcast(dt.uint8)
         g.remote_dma(out, src, T.sem[sem], T.sem.left, pid, rid, topo.mask(core, dst))
@@ -248,119 +282,155 @@ def rank_program(g, core, T, topo):
         mx(h, "qr", 0, q, XH[h], ["qr", "qrs", q + "h%d" % h])
         act(T.sg[:, XH[h][0]:XH[h][1]], ps(h, XH[h]), ["ps%d" % h], ["ps%d" % h, "sg%d" % h], func=SIGN, bias=-TINY)
 
-    def exchange():
-        vscan(T.xs[:], T.d0[:, 0:C], T.sv[:], 0.0, A.mult, ["d0", "sv"], ["xs"])
+    def word_of(h):
+        a, e = XH[h]
+        vscan(T.t[:, a:e], T.sg[:, a:e], T.i5[:, a:e], 2.0, A.min, ["sg%d" % h, "i5"], ["t%d" % h])
+
+    def exchange(between=lambda: None):
+        vscan(T.xs[:], T.d16[:, 0:C], T.sv[:], 0.0, A.mult, ["d16", "sv"], ["xs"])
+        between()
         vtt(T.hn[:, 0:30], T.xs[:, 15:C:16], T.hs[:, 0:30], A.mult, ["xs", "hs"], ["hn"])
         vtt(T.labf[:, 0:30], T.m2[:, 0:30], T.hn[:, 0:30], A.subtract, ["m2", "hn"], ["labf0"])
         vtt(T.labf[:, 32:62], T.m2[:, 0:30], T.hn[:, 0:30], A.add, ["m2", "hn"], ["labf1"])
         vts(T.lab[:, 0:62], T.labf[:, 0:62], 0.5, None, A.mult, None, ["labf0", "labf1"], ["lab"])
 
     scored("q0", 0, T.xt, ["xt0"])
-    first_offsets("sl0")
     scored("q0", 1, T.xt, ["xt1"])
+    vscan(T.rowscan[:], T.d15[:], T.row[:], 0.0, A.mult, ["d15", "row"], ["rowscan"])
+    vcopy(la, T.tai[:], ["tai"], ["lab"])
+    vts(T.sl[:, 0:32], T.rowscan[:, 14:C:15], one_scale, -float(BASE), A.mult, A.add, ["rowscan", "one_scale"], ["sl"])
+    vts(T.sl[:, 32:33], T.rowscan[:, 14:15], one_scale, -float(BASE), A.mult, A.add, ["rowscan", "one_scale"], ["sl"])
+    vcopy(lb, T.tbi[:], ["tbi"], ["lab"])
+    first_offsets()
+    word_of(0)
 
     for r, step in enumerate(STEP):
         last = r == len(STEP) - 1
         dst = T.cores[rank ^ step]
-        q, ql, ll, sl, sn, qn = "q%d" % r, "ql%d" % r, "ll%d" % r, "sl%d" % r, "sl%d" % (r + 1), "q%d" % (r + 1)
-        QS, SG = [q + "h0", q + "h1"], ["sg0", "sg1"]
-        send(dst, q, ql, C, "rq%d" % r, QS, codes=True)
-        send(dst, q + "s", ql + "s", C, "rq%d" % r, QS)
+        q, ql, ll, sn, qn = "q%d" % r, "ql%d" % r, "ll%d" % r, "sn%d" % r, "q%d" % (r + 1)
+        QS, TS = [q + "h0", q + "h1"], ["t0", "t1"]
+        send(dst, q, ql, ALL, "rq%d" % r, QS, codes=True)
+        send(dst, q + "s", ql + "s", ALL, "rq%d" % r, QS)
         arrives(ql, "rq%d" % r)
-        vscan(T.t[:], T.sg[:], T.i5[:], 2.0, A.min, SG + ["i5"], ["t"])
-        act(T.G0[:, 0:RUN], T.sg[:, 0:C].indirect(T[sl][:, 0:L]), SG + [sl], ["G0"], scale=2.0 ** -17)
-        vcopy(T.words[:, 0:2 * C:2], T.t[:, 0:C].indirect(la), ["t", "lab"], ["words0"])
-        act(T.words[:, 1:2 * C:2], T.t[:, 0:C].indirect(lb), ["t", "lab"], ["words1"])
-        act(T.words[:, DUP:WIN], T.words[:, 0:2 * C], ["words0", "words1"], ["dup"])
-        if r == 0:
-            for k in (0, 1):
-                act(T.raw[:, 2 * C + 544 * k:2 * C + 544 * (k + 1)], T.one[:], ["one"], ["rawgap"])
+        word_of(1)
+        act(T.G0[:, 0:RUN], T.sg[:, 0:C].indirect(T.sl[:, 0:L]), ["sg0", "sg1", "sl"], ["G0"], scale=2.0 ** -17)
+        vcopy(T.words[:, 0:2 * C:2], T.t[:, 0:C].indirect(la), TS + ["lab"], ["words0"])
+        act(T.words[:, 1:2 * C:2], T.t[:, 0:C].indirect(lb), TS + ["lab"], ["words1"])
+        act(T.words[:, DUP:DUP + DCUT], T.words[:, 0:DCUT], ["words0", "words1"], ["dup0"])
+        gcopy(T.words[:, DUP + DCUT:WIN], T.words[:, DCUT:2 * C], 2 * C - DCUT, ["words0", "words1"], ["dup1"])
         act(T.raw[:, 0:2 * C:2], T.i5[:, 0:C].indirect(la), ["i5", "lab"], ["raw0"])
         act(T.raw[:, 1:2 * C:2], T.i5[:, 0:C].indirect(lb), ["i5", "lab"], ["raw1"])
-        act(T.raw[:, DUP:WIN], T.raw[:, 0:2 * C], ["raw0", "raw1"], ["rawdup"])
+        gcopy(T.raw[:, DUP:WIN], T.raw[:, 0:2 * C], 2 * C, ["raw0", "raw1"], ["rawdup"])
+        if r == 0:
+            act(T.dlast[:], T.F[:, 0:48].indirect(T.od[:, 0:16]), ["F0", "F1", "F2", "od"], ["dlast"])
         for name, codes, reads, banks in (("to", q, QS, (2, 3, 4, 5)), ("tp", ql, [ql], (6, 7, 0, 1))):
             for b, k in enumerate(banks):
                 mx(k, "qe%d" % b, 0, codes, ALL, ["qe%d" % b] + reads)
                 act(T[name + "%d" % b][:], ps(k, ALL), ["ps%d" % k], ["ps%d" % k, name + "%d" % b])
-        vscan(T.St0[:, 0:RUN], T.d0[:, 0:RUN], T.G0[:, 1:RUN + 1], 0.0, A.mult, ["d0", "G0", "G0tail"], ["St0"])
+        if r == 0:
+            act(T.d16[:, 0:16], T.F[:, 0:16], ["F0"], ["d16"])
+            repeat(act, ("d16", 16, 512))
+        vscan(T.St0[:, 0:RUN], T.dring[:, 0:RUN], T.G0[:, 1:RUN + 1], 0.0, A.mult, ["dring", "G0", "G0tail"], ["St0"])
         vtt(T.sm[:, 0:L], T.St0[:, 15:RUN:16], T.s2[:, 0:L], A.add, ["St0", "s2"], ["sm"])
         vts(T.o[:, 0:L], T.sm[:, 0:L], own_scale, 2.0, A.mult, A.mult, ["sm", "rc"], ["o"])
         for k in range(STAGES - 1):
-            win, keys = (2 * C, []) if k == 0 else (WIN, ["dup", "wordgap"])
+            win, keys = (2 * C, []) if k == 0 else (WIN, ["dup0", "dup1", "wordgap"])
             vts(T.G[:, 0:RUN], T.words[:, 0:win].indirect(T.o[:, 0:L]), -2.0, 2.0 ** -5, A.add, A.mult,
-                ["o", "words0", "words1"] + keys, ["G"])
-            vscan(T.St[:, 0:RUN + 2], T.d0[:, 0:RUN + 2], T.G[:, 0:RUN + 2], 0.0, A.mult, ["d0", "G", "Gtail"], ["St"])
-            vtt(T.sm[:, 0:L], T.St[:, 15:RUN:16], T.St[:, 16:RUN + 1:16], A.add, ["St"], ["sm"])
-            vts(T.o[:, 0:L], T.sm[:, 0:L], pair_scale, 962.25, A.mult, A.add, ["sm", "rc"], ["o"])
-        vts(T.G[:, 0:RUN], T.raw[:, 0:WIN].indirect(T.o[:, 0:L]), -BASE / 512.0, 2.0 ** -5, A.add, A.mult,
-            ["o", "raw0", "raw1", "rawdup", "rawgap"], ["G"])
-        vscan(T.St[:, 0:RUN], T.d0[:, 0:RUN], T.G[:, 0:RUN], 0.0, A.mult, ["d0", "G"], ["St"])
-        vts(T[sn][:, 0:L], T.St[:, 15:RUN:16], own_scale, 0.5, A.mult, A.mult, ["St", "rc"], [sn])
-        send(dst, sn, ll, 30, "rl%d" % r, [sn])
-        arrives(ll, "rl%d" % r)
-        own = T[sn][:, 0:30]
-        for b in (0, 1, 2):
-            vcopy(T["zo%d" % b][:], T["to%d" % b][:, 0:C].indirect(own), ["to%d" % b, sn], ["zo%d" % b])
-        act(T.zo3[:], T.to3[:, 0:C].indirect(own), ["to3", sn], ["zo3"])
+                ["o", "words0", "words1"] + keys, ["G0h", "G1h", "Gw"])
+            vscan(T.St[:, 0:RUN + 2], T.dring[:, 0:RUN + 2], T.G[:, 0:RUN + 2], 0.0, A.mult, ["dring", "Gw", "Gtail"], ["St"])
+            vts(T.o[:, 0:L], T.St[:, 16:RUN + 1:16], pair_scale, 962.25, A.mult, A.add, ["St", "rc"], ["o"])
+        far, own = T[ll], T[sn]
+        SN, LL = [sn + "h0", sn + "h1"], [ll + "h0", ll + "h1"]
+        for h in (0, 1):
+            a, e = HALF * h, HALF * (h + 1)
+            vts(T.G[:, a:e], by(T.raw[:, 0:WIN], T.o, (a, e)), -BASE / 512.0, 2.0 ** -5, A.add, A.mult,
+                ["o", "raw0", "raw1", "rawdup", "rawgap"], ["G%dh" % h])
+            vscan(T.St[:, a:e], T.dlast[:], T.G[:, a:e], 0.0, A.mult, ["dlast", "G%dh" % h], ["St%dh" % h])
+            vts(own[:, 15 * h:15 * h + 15], T.St[:, a + 17:e:17], one_scale, 2.0 ** 14, A.mult, A.mult, ["St%dh" % h, "one_scale"], [SN[h]])
+            send(dst, sn, ll, (15 * h, 15 * h + 15), "rl%d%d" % (r, h), [SN[h]])
+            arrives(LL[h], "rl%d%d" % (r, h))
+        if not last:
+            vcopy(T.G[:, 2 * HALF:RUN], T.G[:, 0:16], ["G0h"], ["Gw"])
+        for pick, b, cols, keys in ((act, 1, ZH[0], SN[0:1]), (act, 2, ZH[0], SN[0:1]), (act, 3, ZH[0], SN[0:1]), (vcopy, 0, ALL, SN),
+                                    (act, 2, ZH[1], SN), (vcopy, 1, ZH[1], SN), (act, 3, ZH[1], SN)):
+            pick(T["zo%d" % b][:, cols[0]:cols[1]], by(T["to%d" % b][:, 0:C], own, cols), ["to%d" % b] + keys, ["zo%d%d" % (b, cols[0] > 0)])
+        if not last:
+            vscan(T.St[:, 0:RUN], T.dring[:, 0:RUN], T.G[:, 0:RUN], 0.0, A.mult, ["dring", "G0h", "G1h", "Gw"], ["St"])
         if r == 0:
             vtt(T.m2[:, 0:30], T.tai[:], T.tbi[:], A.add, ["tai", "tbi"], ["m2"])
             vtt(T.hn[:, 0:30], T.tbi[:], T.tai[:], A.subtract, ["tai", "tbi"], ["hn"])
-            quant("qv", W0, T.vt, ["vt"], "qv")
-        half_difference()
-        if last:
-            vts(T.opb[:, 0:C], T.G[:, 0:C], 2.0 ** 14, None, A.mult, None, ["G"], ["op0"])
-        else:
-            first_offsets(sn)
-        far = T[ll]
         hbanks = ((2, 3, 4, 5), (6, 7, 0, 1))
         for h, (a, e) in enumerate(ZH):
-            for b in (0, 1):
-                act(T.Zp[:, 4 * a + b:4 * e:4], by(T["tp%d" % b][:, 0:C], far, ZH[h]), ["tp%d" % b, ll], ["Zp%d%d" % (h, b)])
-            for b in (2, 3):
-                vcopy(T.Zp[:, 4 * a + b:4 * e:4], by(T["tp%d" % b][:, 0:C], far, ZH[h]), ["tp%d" % b, ll], ["Zp%d%d" % (h, b)])
+            for b in FOUR:
+                (act if b < 2 else vcopy)(T.Zp[:, 4 * a + b:4 * e:4], by(T["tp%d" % b][:, 0:C], far, ZH[h]), ["tp%d" % b] + LL[0:h + 1],
+                                          ["Zp%d%d" % (h, b)])
             quant("qz", ZH[h], T.Zp, ["Zp%d%d" % (h, b) for b in FOUR], "qz%d" % h)
-            for b in FOUR:
-                mx(hbanks[h][b], "wq", 128 * b, "qz", ZH[h], ["wq", "wqs", "qz%d" % h])
-        for b in FOUR:
-            vts(T["l%d" % b][:, 0:30], far[:, 0:30], 4, b, A.mult, A.add, [ll], ["l%d" % b])
-        for h, b in ((0, 0), (0, 1), (0, 2), (0, 3), (1, 0), (1, 1), (1, 2), (1, 3)):
+        for h, b in LAYER:
+            mx(hbanks[h][b], "wq", 128 * b, "qz", ZH[h], ["wq", "wqs", "qz%d" % h])
+        for b in (2, 3):
+            vts(T["l%d" % b][:, 0:30], far[:, 0:30], 4, b, A.mult, A.add, LL, ["l%d" % b])
+        if last:
+            quant("qv", W0, T.vt, ["vt"], "qv")
+        else:
+            vts(T.sl[:, 0:L], T.St[:, 15:RUN:16], own_scale, 0.5, A.mult, A.mult, ["St", "rc"], ["sl"])
+        half_difference()
+        if not last:
+            first_offsets()
+        HS = ["H0", "H1", "H02", "H12", "H03", "H13"]
+
+        def answer(who, h, b):
             a, e = ZH[h]
-            k = "ps%d" % hbanks[h][b]
-            out, src, key = T.H[:, 4 * a + b:4 * e:4], ps(hbanks[h][b], ZH[h]), "H%d%d" % (h, b)
-            if h == 0 or b == 3:
-                act(out, src, [k], [k, key], scale=0.03125)
+            k, key = "ps%d" % hbanks[h][b], "H%d%d" % (h, b)
+            out = T["hw%d" % b][:, a:e] if b < 2 else T.H[:, 4 * a + b:4 * e:4]
+            if who == "a":
+                act(out, ps(hbanks[h][b], ZH[h]), [k], [k, key], scale=0.03125)
             else:
-                vts(out, src, 0.03125, None, A.mult, None, [k], [k, key])
-        HS = ["H%d%d" % (h, b) for h in (0, 1) for b in FOUR]
-        quant("qh", ALL, T.H, HS, "qh")
-        mx(2, "qr", 0, "qh", ALL, ["qr", "qrs", "qh"])
-        act(T.sv[:], ps(2, ALL), ["ps2"], ["ps2", "sv"], func=SIGN, bias=TINY, scale=-1.0)
-        for h, (a, e) in enumerate(XH):
-            if last and h == 1:
-                exchange()
-                act(T.opb[:, C:2 * C], T.i1[:, 0:C].indirect(la), ["i1", "lab"], ["op1"], func=IDENT, bias=-float(BASE))
-                act(T.opb[:, 2 * C:3 * C], T.i1[:, 0:C].indirect(lb), ["i1", "lab"], ["op2"], func=IDENT, bias=-float(BASE))
-                dma("a", T.op[:], T.opb[0:128:16, :], "out", reads=["op0", "op1", "op2"])
-            for b in FOUR:
-                vtt(T.X[:, 4 * a + b:4 * e:4], by(T.H[:, 0:4 * C], T["l%d" % b], XH[h]), T["zo%d" % b][:, a:e], A.add,
-                    HS + ["l%d" % b, "zo%d" % b], ["X%d%d" % (h, b)])
-            XS = ["X%d%d" % (h, b) for b in FOUR]
-            if not last:
-                scored(qn, h, T.X, XS)
-                continue
-            key = qn + "h%d" % h
-            quant(qn, XH[h], T.X, XS, key)
+                vts(out, ps(hbanks[h][b], ZH[h]), 0.03125, None, A.mult, None, [k], [k, key])
+
+        def state(h, parts=FOUR):
+            a, e = XH[h]
+            for b in parts:
+                if b < 2:
+                    picked, keys = by(T["hw%d" % b][:, 0:C], far, XH[h]), LL + ["H0%d" % b, "H1%d" % b]
+                else:
+                    picked, keys = by(T.H[:, 0:4 * C], T["l%d" % b], XH[h]), HS + ["l%d" % b]
+                vtt(T.X[:, 4 * a + b:4 * e:4], picked, T["zo%d" % b][:, a:e], A.add, keys + ["zo%d0" % b, "zo%d1" % b], ["X%d%d" % (h, b)])
+            return ["X%d%d" % (h, b) for b in FOUR]
+
+        def outputs(h, reads):
+            (a, e), key = XH[h], qn + "h%d" % h
+            quant(qn, XH[h], T.X, reads, key)
             dma("s", T.oc[:, 4 * a:4 * e], T[qn][:, a:e].bitcast(dt.uint8), "out", reads=[key])
             mx(h, "qv", 0, qn, XH[h], ["qv", key])
-            if h == 0:
-                act(T.yb[:, a:e], ps(h, XH[h]), ["ps0"], ["ps0", "y0"])
-            else:
-                vcopy(T.yb[:, a:e], ps(h, XH[h]), ["ps1"], ["ps1", "y1"])
+            (vcopy if h else act)(T.yb[:, a:e], ps(h, XH[h]), ["ps%d" % h], ["ps%d" % h, "y%d" % h])
+            if h == 1:
                 for k in FOUR:
                     dma("s", T.osc[4 * k:4 * k + 4, :], T[qn + "s"][32 * k:32 * k + 4, :], "out", reads=[qn + "h0", key])
             dma("s", T.y[:, a:e], T.yb[:, a:e], "out", reads=["y%d" % h])
+
+        for h, b in LAYER:
+            answer("v" if (h, b) == (1, 0) else "a", h, b)
+        for h, b in ((0, 0), (0, 1), (1, 0)):
+            a, e = ZH[h]
+            gcopy(T.H[:, 4 * a + b:4 * e:4], T["hw%d" % b][:, a:e], e - a, ["H%d%d" % (h, b)], ["H0"])
+        state(0, [0, 1])
+        vcopy(T.H[:, 4 * ZCUT + 1:4 * C:4], T.hw1[:, ZCUT:C], ["H11"], ["H1"])
+        quant("qh", ALL, T.H, HS, "qh")
+        mx(2, "qr", 0, "qh", ALL, ["qr", "qrs", "qh"])
+        act(T.sv[:], ps(2, ALL), ["ps2"], ["ps2", "sv"], func=SIGN, bias=TINY, scale=-1.0)
+        first = state(0, [2, 3])
         if not last:
+            scored(qn, 0, T.X, first)
+            scored(qn, 1, T.X, state(1))
+            exchange(lambda: word_of(0))
+        else:
+            act(T.opb[:, 0:C], by(T.i1[:, 0:C], own, ALL), ["i1"] + SN, ["op0"], func=IDENT, bias=-float(BASE))
+            outputs(0, first)
             exchange()
+            act(T.opb[:, C:2 * C], T.i1[:, 0:C].indirect(la), ["i1", "lab"], ["op1"], func=IDENT, bias=-float(BASE))
+            act(T.opb[:, 2 * C:3 * C], T.i1[:, 0:C].indirect(lb), ["i1", "lab"], ["op2"], func=IDENT, bias=-float(BASE))
+            dma("a", T.op[:], T.opb[0:128:16, :], "out", reads=["op0", "op1", "op2"])
+            outputs(1, state(1))
     for s in sorted(total):
         if know["g"].get(s, 0) < total[s]:
             g.wait_ge(T.sem[s], total[s])

@@ -172,11 +172,14 @@ def rank_program(g, core, T, topo):
     def gcopy(out, in_, n, reads, writes):
         op("g", lambda: g.affine_select(out, in_, [[1, n]], A.is_ge, 0.0, 0, 0), reads, writes)
 
-    def repeat(copy, *jobs):
+    def repeat(who, name, n, upto):
         for k in range(5):
-            for name, n, upto in jobs:
-                m = min(n << k, upto - (n << k))
-                copy(T[name][:, n << k:(n << k) + m], T[name][:, 0:m], [name], [name])
+            m = min(n << k, upto - (n << k))
+            out, in_ = T[name][:, n << k:(n << k) + m], T[name][:, 0:m]
+            if who == "g":
+                gcopy(out, in_, m, [name], [name])
+            else:
+                act(out, in_, [name], [name])
 
     def quant(name, cols, tile, reads, key):
         a, b = cols
@@ -213,49 +216,52 @@ def rank_program(g, core, T, topo):
     vset(T.one[:], 1.0, ["one"])
     op("g", lambda: g.iota(T.di[:], [[1, 32]], 128, -1), [], ["di"])
     op("g", lambda: g.iota(T.ip[:], [[16, 8]], 0, 0), [], ["ip"])
-    op("g", lambda: g.iota(T.ki[:], [[15, 16]], 127, 1), [], ["ki"])
-    op("g", lambda: g.affine_select(T.eye[:], T.one[:, 0:528], [[-1, 528]], A.is_equal, 0.0, 3, 4), ["one"], ["eye"])
     op("g", lambda: g.iota(T.i1[:], [[1, C]], BASE, 0, allow_small_or_imprecise_dtypes=True), [], ["i1"])
-    op("g", lambda: g.iota(T.raw[:, 2 * C:DUP], [[0, DUP - 2 * C]], 0, 0, allow_small_or_imprecise_dtypes=True), [], ["rawgap"])
-    vset(T.labf[:], 0.0, ["labf0", "labf1"])
-    vset(T.G0[:, RUN:544], 0.0, ["G0tail"])
+    op("g", lambda: g.iota(T.ki[:], [[15, 16]], 127, 1), [], ["ki"])
     vts(T.dm[:], T.di[:], 15, None, A.bitwise_and, None, ["di"], ["dm"])
-    vcopy(T.G[:, RUN:544], T.labf[:, 0:16], ["labf0"], ["Gtail"])
+    vcopy(T.ip16[:], T.ip[:], ["ip"], ["ip16"])
     vts(T.col[:, 0:1], T.dm[:, 0:1], 0, None, A.is_equal, None, ["dm"], ["first"])
     vts(T.col[:, 2:3], T.dm[:, 0:1], 1, 2.0 ** -20 - 1.0, A.not_equal, A.mult, ["dm"], ["col2"])
     vts(T.dj[:], T.di[:], T.col[:, 0:1], None, A.subtract, None, ["di", "first"], ["dj"])
     vts(T.col[:, 1:2], T.col[:, 2:3], 1.0, None, A.add, None, ["col2"], ["one_scale"])
     vts(T.dn[:], T.dj[:], 15, None, A.bitwise_and, None, ["dj"], ["dn"])
-    vts(T.F[:, 16:32], T.dm[:, 0:16], 0, None, A.not_equal, None, ["dm"], ["F1"])
-    vts(T.ma[:], T.dn[:], 1, 2047.0, A.is_equal, A.mult, ["dn"], ["ma"])
-    vts(T.mb[:], T.dn[:], 2, 511.0, A.is_equal, A.mult, ["dn"], ["mb"])
+    vset(T.labf[:], 0.0, ["labf0", "labf1"])
     vts(T.mc[:], T.dn[:], 0, None, A.not_equal, None, ["dn"], ["mc"])
     vts(T.md[:], T.dn[:], 1, BIG - 1.0, A.is_equal, A.mult, ["dn"], ["md"])
+    vts(T.ma[:], T.dn[:], 1, 2047.0, A.is_equal, A.mult, ["dn"], ["ma"])
+    vtt(T.d15[:, 0:15], T.md[:, 1:16], T.mc[:, 1:16], A.add, ["md", "mc"], ["d15"])
+    vts(T.mb[:], T.dn[:], 2, 511.0, A.is_equal, A.mult, ["dn"], ["mb"])
     vts(T.oh[:], T.dn[:], 0, 2.0 ** -15, A.is_equal, A.mult, ["dn"], ["oh"])
     vtt(T.ma[:], T.ma[:], T.mb[:], A.add, ["ma", "mb"], ["ma"])
-    vtt(T.d15[:, 0:15], T.md[:, 1:16], T.mc[:, 1:16], A.add, ["md", "mc"], ["d15"])
+    vset(T.G0[:, RUN:544], 0.0, ["G0tail"])
     vtt(T.dring[:, 0:32], T.ma[:], T.mc[:], A.add, ["ma", "mc"], ["dring"])
-    vts(T.mb[:, 0:16], T.dm[:, 0:16], 1, BIG - 1.0, A.is_equal, A.mult, ["dm", "ma"], ["mb"])
+    vcopy(T.G[:, RUN:544], T.labf[:, 0:16], ["labf0"], ["Gtail"])
     vscan(T.ks[:], T.dring[:, 0:32], T.oh[:], 0.0, A.mult, ["dring", "oh"], ["ks"])
-    vts(T.F[:, 32:48], T.F[:, 16:32], 1.0 - BIG, BIG, A.mult, A.add, ["F1"], ["F2"])
-    vtt(T.F[:, 0:16], T.mb[:, 0:16], T.F[:, 16:32], A.add, ["mb", "F1"], ["F0"])
-    op("v", lambda: g.vector.reciprocal(T.rc[:, 0:2], T.ks[:, 15:17]), ["ks"], ["rc"])
-    vcopy(T.ip16[:], T.ip[:], ["ip"], ["ip16"])
-    vts(T.col[:, 3:4], T.dm[:, 0:1], 15, 16.0, A.is_equal, A.mult, ["dm"], ["col3"])
-    vts(T.km[:], T.ki[:], 15, None, A.bitwise_and, None, ["ki"], ["km"])
-    vts(T.col[:, 4:5], T.col[:, 0:1], 32.0, T.col[:, 3:4], A.mult, A.add, ["first", "col3"], ["col4"])
-    vts(T.od[:], T.km[:], T.col[:, 4:5], None, A.add, None, ["km", "col4"], ["od"])
-    for k in (0, 1):
-        act(T.words[:, 2 * C + 544 * k:2 * C + 544 * (k + 1)], T.one[:], ["one"], ["wordgap"])
-    repeat(act, ("d15", 15, C), ("dring", 32, 544))
-    for b in FOUR:
-        op("v", lambda: g.vector.quantize_mx(T["qe%d" % b][:], T["qe%ds" % b][:], T.eye[:, 3 - b:515 - b]), ["eye"], ["qe%d" % b])
-    vts(T.i5[:], T.i1[:], 2.0 ** -9, None, A.mult, None, ["i1"], ["i5"])
     quant("qu", W0, T.ut, ["ut"], "qu")
-    vcopy(T.s0[:, 0:30], T.sti[:], ["sti"], ["s0"])
+    op("v", lambda: g.vector.reciprocal(T.rc[:, 0:2], T.ks[:, 15:17]), ["ks"], ["rc"])
     vcopy(T.qr[:, 0:128].bitcast(dt.uint32), T.qu[:, 0:128].bitcast(dt.uint32).indirect(T.ip16[:, 0:8]), ["qu", "ip16"], ["qr"])
+    vcopy(T.s0[:, 0:30], T.sti[:], ["sti"], ["s0"])
+    act(T.words[:, 2 * C:2 * C + 544], T.one[:], ["one"], ["wordgap"])
+    act(T.i5[:], T.i1[:], ["i1"], ["i5"], scale=2.0 ** -9)
+    repeat("a", "d15", 15, C)
     act(T.qrs[:, 0:128], T.qus[:, 0:128].indirect(T.ip16[:, 0:8]), ["qu", "ip16"], ["qrs"])
     act(T.row[:], by(T.i1[:, 0:C], T.s0, ALL), ["i1", "s0"], ["row"])
+    op("g", lambda: g.affine_select(T.eye[:], T.one[:, 0:528], [[-1, 528]], A.is_equal, 0.0, 3, 4), ["one"], ["eye"])
+    repeat("g", "dring", 32, 544)
+    later = [
+        lambda: vts(T.F[:, 16:32], T.dm[:, 0:16], 0, None, A.not_equal, None, ["dm"], ["F1"]),
+        lambda: vts(T.mb[:, 0:16], T.dm[:, 0:16], 1, BIG - 1.0, A.is_equal, A.mult, ["dm"], ["mb"]),
+        lambda: vts(T.F[:, 32:48], T.F[:, 16:32], 1.0 - BIG, BIG, A.mult, A.add, ["F1"], ["F2"]),
+        lambda: vtt(T.F[:, 0:16], T.mb[:, 0:16], T.F[:, 16:32], A.add, ["mb", "F1"], ["F0"]),
+        lambda: vts(T.col[:, 3:4], T.dm[:, 0:1], 15, 16.0, A.is_equal, A.mult, ["dm"], ["col3"]),
+        lambda: vts(T.km[:], T.ki[:], 15, None, A.bitwise_and, None, ["ki"], ["km"]),
+        lambda: vts(T.col[:, 4:5], T.col[:, 0:1], 32.0, T.col[:, 3:4], A.mult, A.add, ["first", "col3"], ["col4"]),
+        lambda: vts(T.od[:], T.km[:], T.col[:, 4:5], None, A.add, None, ["km", "col4"], ["od"]),
+    ]
+
+    def meanwhile():
+        if later:
+            later.pop(0)()
 
     def first_offsets():
         vts(T.s2[:, 0:L], T.sl[:, 0:L], 0.25, run_scale, A.add, A.mult, ["sl", "ks"], ["s2"])
@@ -296,6 +302,8 @@ def rank_program(g, core, T, topo):
 
     scored("q0", 0, T.xt, ["xt0"])
     scored("q0", 1, T.xt, ["xt1"])
+    for b in FOUR:
+        op("v", lambda: g.vector.quantize_mx(T["qe%d" % b][:], T["qe%ds" % b][:], T.eye[:, 3 - b:515 - b]), ["eye"], ["qe%d" % b])
     vscan(T.rowscan[:], T.d15[:], T.row[:], 0.0, A.mult, ["d15", "row"], ["rowscan"])
     vcopy(la, T.tai[:], ["tai"], ["lab"])
     vts(T.sl[:, 0:32], T.rowscan[:, 14:C:15], one_scale, -float(BASE), A.mult, A.add, ["rowscan", "one_scale"], ["sl"])
@@ -314,31 +322,38 @@ def rank_program(g, core, T, topo):
         arrives(ql, "rq%d" % r)
         word_of(1)
         act(T.G0[:, 0:RUN], T.sg[:, 0:C].indirect(T.sl[:, 0:L]), ["sg0", "sg1", "sl"], ["G0"], scale=2.0 ** -17)
+        meanwhile()
         vcopy(T.words[:, 0:2 * C:2], T.t[:, 0:C].indirect(la), TS + ["lab"], ["words0"])
         act(T.words[:, 1:2 * C:2], T.t[:, 0:C].indirect(lb), TS + ["lab"], ["words1"])
         act(T.words[:, DUP:DUP + DCUT], T.words[:, 0:DCUT], ["words0", "words1"], ["dup0"])
+        if r == 0:
+            gcopy(T.words[:, 2 * C + 544:DUP], T.one[:], 544, ["one"], ["wordgap2"])
         gcopy(T.words[:, DUP + DCUT:WIN], T.words[:, DCUT:2 * C], 2 * C - DCUT, ["words0", "words1"], ["dup1"])
         act(T.raw[:, 0:2 * C:2], T.i5[:, 0:C].indirect(la), ["i5", "lab"], ["raw0"])
         act(T.raw[:, 1:2 * C:2], T.i5[:, 0:C].indirect(lb), ["i5", "lab"], ["raw1"])
-        gcopy(T.raw[:, DUP:WIN], T.raw[:, 0:2 * C], 2 * C, ["raw0", "raw1"], ["rawdup"])
         if r == 0:
-            act(T.dlast[:], T.F[:, 0:48].indirect(T.od[:, 0:16]), ["F0", "F1", "F2", "od"], ["dlast"])
+            op("g", lambda: g.iota(T.raw[:, 2 * C:DUP], [[0, DUP - 2 * C]], 0, 0, allow_small_or_imprecise_dtypes=True), [], ["rawgap"])
+        gcopy(T.raw[:, DUP:WIN], T.raw[:, 0:2 * C], 2 * C, ["raw0", "raw1"], ["rawdup"])
+        vscan(T.St0[:, 0:RUN], T.dring[:, 0:RUN], T.G0[:, 1:RUN + 1], 0.0, A.mult, ["dring", "G0", "G0tail"], ["St0"])
+        meanwhile()
+        vtt(T.sm[:, 0:L], T.St0[:, 15:RUN:16], T.s2[:, 0:L], A.add, ["St0", "s2"], ["sm"])
+        meanwhile()
+        vts(T.o[:, 0:L], T.sm[:, 0:L], own_scale, 2.0, A.mult, A.mult, ["sm", "rc"], ["o"])
+        for k in range(STAGES - 1):
+            win, keys = (2 * C, []) if k == 0 else (WIN, ["dup0", "dup1", "wordgap", "wordgap2"])
+            meanwhile()
+            vts(T.G[:, 0:RUN], T.words[:, 0:win].indirect(T.o[:, 0:L]), -2.0, 2.0 ** -5, A.add, A.mult,
+                ["o", "words0", "words1"] + keys, ["G0h", "G1h", "Gw"])
+            meanwhile()
+            vscan(T.St[:, 0:RUN + 2], T.dring[:, 0:RUN + 2], T.G[:, 0:RUN + 2], 0.0, A.mult, ["dring", "Gw", "Gtail"], ["St"])
+            meanwhile()
+            vts(T.o[:, 0:L], T.St[:, 16:RUN + 1:16], pair_scale, 962.25, A.mult, A.add, ["St", "rc"], ["o"])
         for name, codes, reads, banks in (("to", q, QS, (2, 3, 4, 5)), ("tp", ql, [ql], (6, 7, 0, 1))):
             for b, k in enumerate(banks):
                 mx(k, "qe%d" % b, 0, codes, ALL, ["qe%d" % b] + reads)
                 act(T[name + "%d" % b][:], ps(k, ALL), ["ps%d" % k], ["ps%d" % k, name + "%d" % b])
-        if r == 0:
-            act(T.d16[:, 0:16], T.F[:, 0:16], ["F0"], ["d16"])
-            repeat(act, ("d16", 16, 512))
-        vscan(T.St0[:, 0:RUN], T.dring[:, 0:RUN], T.G0[:, 1:RUN + 1], 0.0, A.mult, ["dring", "G0", "G0tail"], ["St0"])
-        vtt(T.sm[:, 0:L], T.St0[:, 15:RUN:16], T.s2[:, 0:L], A.add, ["St0", "s2"], ["sm"])
-        vts(T.o[:, 0:L], T.sm[:, 0:L], own_scale, 2.0, A.mult, A.mult, ["sm", "rc"], ["o"])
-        for k in range(STAGES - 1):
-            win, keys = (2 * C, []) if k == 0 else (WIN, ["dup0", "dup1", "wordgap"])
-            vts(T.G[:, 0:RUN], T.words[:, 0:win].indirect(T.o[:, 0:L]), -2.0, 2.0 ** -5, A.add, A.mult,
-                ["o", "words0", "words1"] + keys, ["G0h", "G1h", "Gw"])
-            vscan(T.St[:, 0:RUN + 2], T.dring[:, 0:RUN + 2], T.G[:, 0:RUN + 2], 0.0, A.mult, ["dring", "Gw", "Gtail"], ["St"])
-            vts(T.o[:, 0:L], T.St[:, 16:RUN + 1:16], pair_scale, 962.25, A.mult, A.add, ["St", "rc"], ["o"])
+            if r == 0 and name == "to":
+                act(T.dlast[:], T.F[:, 0:48].indirect(T.od[:, 0:16]), ["F0", "F1", "F2", "od"], ["dlast"])
         far, own = T[ll], T[sn]
         SN, LL = [sn + "h0", sn + "h1"], [ll + "h0", ll + "h1"]
         for h in (0, 1):
@@ -351,9 +366,15 @@ def rank_program(g, core, T, topo):
             arrives(LL[h], "rl%d%d" % (r, h))
         if not last:
             vcopy(T.G[:, 2 * HALF:RUN], T.G[:, 0:16], ["G0h"], ["Gw"])
-        for pick, b, cols, keys in ((act, 1, ZH[0], SN[0:1]), (act, 2, ZH[0], SN[0:1]), (act, 3, ZH[0], SN[0:1]), (vcopy, 0, ALL, SN),
-                                    (act, 2, ZH[1], SN), (vcopy, 1, ZH[1], SN), (act, 3, ZH[1], SN)):
-            pick(T["zo%d" % b][:, cols[0]:cols[1]], by(T["to%d" % b][:, 0:C], own, cols), ["to%d" % b] + keys, ["zo%d%d" % (b, cols[0] > 0)])
+
+        def own_columns(pick, b, cols):
+            keys = SN[0:1] if cols[1] <= ZCUT else SN
+            pick(T["zo%d" % b][:, cols[0]:cols[1]], by(T["to%d" % b][:, 0:C], own, cols), ["to%d" % b] + keys, ["zo%d_%d" % (b, cols[1])])
+
+        own_columns(vcopy, 0, XH[0])
+        for cols in (ZH[0], (ZCUT, XCUT)):
+            for b in (1, 2):
+                own_columns(act, b, cols)
         if not last:
             vscan(T.St[:, 0:RUN], T.dring[:, 0:RUN], T.G[:, 0:RUN], 0.0, A.mult, ["dring", "G0h", "G1h", "Gw"], ["St"])
         if r == 0:
@@ -394,7 +415,7 @@ def rank_program(g, core, T, topo):
                     picked, keys = by(T["hw%d" % b][:, 0:C], far, XH[h]), LL + ["H0%d" % b, "H1%d" % b]
                 else:
                     picked, keys = by(T.H[:, 0:4 * C], T["l%d" % b], XH[h]), HS + ["l%d" % b]
-                vtt(T.X[:, 4 * a + b:4 * e:4], picked, T["zo%d" % b][:, a:e], A.add, keys + ["zo%d0" % b, "zo%d1" % b], ["X%d%d" % (h, b)])
+                vtt(T.X[:, 4 * a + b:4 * e:4], picked, T["zo%d" % b][:, a:e], A.add, keys + ["zo%d_%d" % (b, e)], ["X%d%d" % (h, b)])
             return ["X%d%d" % (h, b) for b in FOUR]
 
         def outputs(h, reads):
@@ -413,11 +434,17 @@ def rank_program(g, core, T, topo):
         for h, b in ((0, 0), (0, 1), (1, 0)):
             a, e = ZH[h]
             gcopy(T.H[:, 4 * a + b:4 * e:4], T["hw%d" % b][:, a:e], e - a, ["H%d%d" % (h, b)], ["H0"])
+        own_columns(act, 3, XH[0])
+        for b in FOUR:
+            own_columns(act, b, XH[1])
         state(0, [0, 1])
         vcopy(T.H[:, 4 * ZCUT + 1:4 * C:4], T.hw1[:, ZCUT:C], ["H11"], ["H1"])
         quant("qh", ALL, T.H, HS, "qh")
         mx(2, "qr", 0, "qh", ALL, ["qr", "qrs", "qh"])
         act(T.sv[:], ps(2, ALL), ["ps2"], ["ps2", "sv"], func=SIGN, bias=TINY, scale=-1.0)
+        if r == 0:
+            gcopy(T.d16[:, 0:16], T.F[:, 0:16], 16, ["F0"], ["d16"])
+            repeat("g", "d16", 16, 512)
         first = state(0, [2, 3])
         if not last:
             scored(qn, 0, T.X, first)

@@ -15,6 +15,8 @@ DCUT = 512
 TINY = 2.0 ** -100
 BIG = 2.0 ** 20
 LAYER = [(h, b) for h in (0, 1) for b in range(4)]
+BESIDE = ((0, ["rA", "rB"]), (0, ["to0", "to1", "to2"]), (0, ["to3", "tp2"]), (192, ["last", "tp3"]), (HALF, ["tp0", "tp1"]))
+EARLY = (1,)
 
 SCRATCH = {}
 
@@ -59,6 +61,7 @@ for _n in ("G", "St"):
     _add(_n, [128, 544], "float16")
 for _n in ("G0", "St0", "dring"):
     _add(_n, [128, 544], "bfloat16")
+_add("Gs", [128, HALF + 16], "float32")
 _add("d16", [128, 512], "bfloat16")
 _add("dlast", [128, HALF], "bfloat16")
 _add("one", [128, 544], "bfloat16")
@@ -203,9 +206,9 @@ def rank_program(g, core, T, topo):
     la, lb = T.lab[:, 0:30], T.lab[:, 32:62]
     own_scale, pair_scale, run_scale, one_scale = T.rc[:, 0:1], T.rc[:, 1:2], T.ks[:, 15:16], T.col[:, 1:2]
 
+    dma("s", T.ut[:], T.u[:], "ld_u", writes=["ut"])
     for h, (a, b) in enumerate(XH):
         dma("s", T.xt[:, 4 * a:4 * b], T.x[:, 4 * a:4 * b], "ld_x%d" % h, writes=["xt%d" % h])
-    dma("a", T.ut[:], T.u[:], "ld_u", writes=["ut"])
     dma("a", T.sti[:], T.st[:], "ld_st", writes=["sti"])
     dma("a", T.tai[:], T.ta[:], "ld_ta", writes=["tai"])
     dma("a", T.tbi[:], T.tb[:], "ld_tb", writes=["tbi"])
@@ -230,25 +233,36 @@ def rank_program(g, core, T, topo):
     vts(T.md[:], T.dn[:], 1, BIG - 1.0, A.is_equal, A.mult, ["dn"], ["md"])
     vts(T.ma[:], T.dn[:], 1, 2047.0, A.is_equal, A.mult, ["dn"], ["ma"])
     vtt(T.d15[:, 0:15], T.md[:, 1:16], T.mc[:, 1:16], A.add, ["md", "mc"], ["d15"])
+
+    def twice(k):
+        vcopy(T.d15[:, 15 << k:30 << k], T.d15[:, 0:15 << k], ["d15"], ["d15"])
+
     vts(T.mb[:], T.dn[:], 2, 511.0, A.is_equal, A.mult, ["dn"], ["mb"])
-    vts(T.oh[:], T.dn[:], 0, 2.0 ** -15, A.is_equal, A.mult, ["dn"], ["oh"])
+    twice(0)
     vtt(T.ma[:], T.ma[:], T.mb[:], A.add, ["ma", "mb"], ["ma"])
-    vset(T.G0[:, RUN:544], 0.0, ["G0tail"])
+    vts(T.oh[:], T.dn[:], 0, 2.0 ** -15, A.is_equal, A.mult, ["dn"], ["oh"])
     vtt(T.dring[:, 0:32], T.ma[:], T.mc[:], A.add, ["ma", "mc"], ["dring"])
-    vcopy(T.G[:, RUN:544], T.labf[:, 0:16], ["labf0"], ["Gtail"])
+    twice(1)
     vscan(T.ks[:], T.dring[:, 0:32], T.oh[:], 0.0, A.mult, ["dring", "oh"], ["ks"])
-    quant("qu", W0, T.ut, ["ut"], "qu")
-    op("v", lambda: g.vector.reciprocal(T.rc[:, 0:2], T.ks[:, 15:17]), ["ks"], ["rc"])
-    vcopy(T.qr[:, 0:128].bitcast(dt.uint32), T.qu[:, 0:128].bitcast(dt.uint32).indirect(T.ip16[:, 0:8]), ["qu", "ip16"], ["qr"])
     vcopy(T.s0[:, 0:30], T.sti[:], ["sti"], ["s0"])
-    act(T.words[:, 2 * C:2 * C + 544], T.one[:], ["one"], ["wordgap"])
+    twice(2)
+    quant("qu", W0, T.ut, ["ut"], "qu")
+    twice(3)
+    vcopy(T.qr[:, 0:128].bitcast(dt.uint32), T.qu[:, 0:128].bitcast(dt.uint32).indirect(T.ip16[:, 0:8]), ["qu", "ip16"], ["qr"])
+    twice(4)
+    op("v", lambda: g.vector.reciprocal(T.rc[:, 0:2], T.ks[:, 15:17]), ["ks"], ["rc"])
+    for k in (0, 1):
+        act(T.words[:, 2 * C + 544 * k:2 * C + 544 * (k + 1)], T.one[:], ["one"], ["wordgap"])
     act(T.i5[:], T.i1[:], ["i1"], ["i5"], scale=2.0 ** -9)
-    repeat("a", "d15", 15, C)
-    act(T.qrs[:, 0:128], T.qus[:, 0:128].indirect(T.ip16[:, 0:8]), ["qu", "ip16"], ["qrs"])
     act(T.row[:], by(T.i1[:, 0:C], T.s0, ALL), ["i1", "s0"], ["row"])
+    act(T.qrs[:, 0:128], T.qus[:, 0:128].indirect(T.ip16[:, 0:8]), ["qu", "ip16"], ["qrs"])
     op("g", lambda: g.affine_select(T.eye[:], T.one[:, 0:528], [[-1, 528]], A.is_equal, 0.0, 3, 4), ["one"], ["eye"])
     repeat("g", "dring", 32, 544)
-    later = [
+    vcopy(T.G[:, RUN:544], T.labf[:, 0:16], ["labf0"], ["Gtail"])
+    later = [lambda: first_offsets()]
+    later += [lambda b=b: op("v", lambda: g.vector.quantize_mx(T["qe%d" % b][:], T["qe%ds" % b][:], T.eye[:, 3 - b:515 - b]), ["eye"], ["qe%d" % b])
+              for b in FOUR]
+    later += [
         lambda: vts(T.F[:, 16:32], T.dm[:, 0:16], 0, None, A.not_equal, None, ["dm"], ["F1"]),
         lambda: vts(T.mb[:, 0:16], T.dm[:, 0:16], 1, BIG - 1.0, A.is_equal, A.mult, ["dm"], ["mb"]),
         lambda: vts(T.F[:, 32:48], T.F[:, 16:32], 1.0 - BIG, BIG, A.mult, A.add, ["F1"], ["F2"]),
@@ -294,22 +308,20 @@ def rank_program(g, core, T, topo):
 
     def exchange(between=lambda: None):
         vscan(T.xs[:], T.d16[:, 0:C], T.sv[:], 0.0, A.mult, ["d16", "sv"], ["xs"])
-        between()
         vtt(T.hn[:, 0:30], T.xs[:, 15:C:16], T.hs[:, 0:30], A.mult, ["xs", "hs"], ["hn"])
         vtt(T.labf[:, 0:30], T.m2[:, 0:30], T.hn[:, 0:30], A.subtract, ["m2", "hn"], ["labf0"])
         vtt(T.labf[:, 32:62], T.m2[:, 0:30], T.hn[:, 0:30], A.add, ["m2", "hn"], ["labf1"])
+        between()
         vts(T.lab[:, 0:62], T.labf[:, 0:62], 0.5, None, A.mult, None, ["labf0", "labf1"], ["lab"])
 
     scored("q0", 0, T.xt, ["xt0"])
     scored("q0", 1, T.xt, ["xt1"])
-    for b in FOUR:
-        op("v", lambda: g.vector.quantize_mx(T["qe%d" % b][:], T["qe%ds" % b][:], T.eye[:, 3 - b:515 - b]), ["eye"], ["qe%d" % b])
     vscan(T.rowscan[:], T.d15[:], T.row[:], 0.0, A.mult, ["d15", "row"], ["rowscan"])
     vcopy(la, T.tai[:], ["tai"], ["lab"])
     vts(T.sl[:, 0:32], T.rowscan[:, 14:C:15], one_scale, -float(BASE), A.mult, A.add, ["rowscan", "one_scale"], ["sl"])
     vts(T.sl[:, 32:33], T.rowscan[:, 14:15], one_scale, -float(BASE), A.mult, A.add, ["rowscan", "one_scale"], ["sl"])
     vcopy(lb, T.tbi[:], ["tbi"], ["lab"])
-    first_offsets()
+    vset(T.G0[:, RUN:544], 0.0, ["G0tail"])
     word_of(0)
 
     for r, step in enumerate(STEP):
@@ -326,66 +338,87 @@ def rank_program(g, core, T, topo):
         vcopy(T.words[:, 0:2 * C:2], T.t[:, 0:C].indirect(la), TS + ["lab"], ["words0"])
         act(T.words[:, 1:2 * C:2], T.t[:, 0:C].indirect(lb), TS + ["lab"], ["words1"])
         act(T.words[:, DUP:DUP + DCUT], T.words[:, 0:DCUT], ["words0", "words1"], ["dup0"])
-        if r == 0:
-            gcopy(T.words[:, 2 * C + 544:DUP], T.one[:], 544, ["one"], ["wordgap2"])
         gcopy(T.words[:, DUP + DCUT:WIN], T.words[:, DCUT:2 * C], 2 * C - DCUT, ["words0", "words1"], ["dup1"])
-        act(T.raw[:, 0:2 * C:2], T.i5[:, 0:C].indirect(la), ["i5", "lab"], ["raw0"])
-        act(T.raw[:, 1:2 * C:2], T.i5[:, 0:C].indirect(lb), ["i5", "lab"], ["raw1"])
-        if r == 0:
-            op("g", lambda: g.iota(T.raw[:, 2 * C:DUP], [[0, DUP - 2 * C]], 0, 0, allow_small_or_imprecise_dtypes=True), [], ["rawgap"])
-        gcopy(T.raw[:, DUP:WIN], T.raw[:, 0:2 * C], 2 * C, ["raw0", "raw1"], ["rawdup"])
+
+        def scalar_job(name):
+            if name[0] == "r":
+                h = "AB".index(name[1])
+                act(T.raw[:, h:2 * C:2], T.i5[:, 0:C].indirect((la, lb)[h]), ["i5", "lab"], ["raw%d" % h])
+                if h and r == 0:
+                    op("g", lambda: g.iota(T.raw[:, 2 * C:DUP], [[0, DUP - 2 * C]], 0, 0, allow_small_or_imprecise_dtypes=True), [], ["rawgap"])
+                if h:
+                    gcopy(T.raw[:, DUP:WIN], T.raw[:, 0:2 * C], 2 * C, ["raw0", "raw1"], ["rawdup"])
+            elif name[0] == "t":
+                b = int(name[2])
+                codes, reads, k = (q, QS, 2 + b) if name[1] == "o" else (ql, [ql], (6 + b) % 8)
+                mx(k, "qe%d" % b, 0, codes, ALL, ["qe%d" % b] + reads)
+                act(T[name][:], ps(k, ALL), ["ps%d" % k], ["ps%d" % k, name])
+            elif r == 0:
+                act(T.dlast[:], T.F[:, 0:48].indirect(T.od[:, 0:16]), ["F0", "F1", "F2", "od"], ["dlast"])
+
         vscan(T.St0[:, 0:RUN], T.dring[:, 0:RUN], T.G0[:, 1:RUN + 1], 0.0, A.mult, ["dring", "G0", "G0tail"], ["St0"])
         meanwhile()
         vtt(T.sm[:, 0:L], T.St0[:, 15:RUN:16], T.s2[:, 0:L], A.add, ["St0", "s2"], ["sm"])
         meanwhile()
         vts(T.o[:, 0:L], T.sm[:, 0:L], own_scale, 2.0, A.mult, A.mult, ["sm", "rc"], ["o"])
-        for k in range(STAGES - 1):
-            win, keys = (2 * C, []) if k == 0 else (WIN, ["dup0", "dup1", "wordgap", "wordgap2"])
+        for k, (n, jobs) in enumerate(BESIDE[:-1]):
+            win, keys = (2 * C, []) if k == 0 else (WIN, ["dup0", "dup1", "wordgap"])
+            keys += ["o", "words0", "words1"]
             meanwhile()
-            vts(T.G[:, 0:RUN], T.words[:, 0:win].indirect(T.o[:, 0:L]), -2.0, 2.0 ** -5, A.add, A.mult,
-                ["o", "words0", "words1"] + keys, ["G0h", "G1h", "Gw"])
+            if n:
+                act(T.Gs[:, 0:n + 16], by(T.words[:, 0:win], T.o, (0, n + 16)), keys, ["Gs"], func=IDENT, scale=2.0 ** -5, bias=-2.0 ** -4)
+            for name in jobs:
+                scalar_job(name)
+            vts(T.G[:, n:RUN], by(T.words[:, 0:win], T.o, (n, RUN)), -2.0, 2.0 ** -5, A.add, A.mult, keys, ["G"])
             meanwhile()
-            vscan(T.St[:, 0:RUN + 2], T.dring[:, 0:RUN + 2], T.G[:, 0:RUN + 2], 0.0, A.mult, ["dring", "Gw", "Gtail"], ["St"])
+            a = n + 1 if n else 0
+            vscan(T.St[:, a:RUN + 2], T.dring[:, a:RUN + 2], T.G[:, a:RUN + 2], 0.0, A.mult, ["dring", "G", "Gtail"], ["St"])
+            if n:
+                vscan(T.St[:, 0:a], T.dring[:, 0:a], T.Gs[:, 0:a], 0.0, A.mult, ["dring", "Gs"], ["St"])
             meanwhile()
             vts(T.o[:, 0:L], T.St[:, 16:RUN + 1:16], pair_scale, 962.25, A.mult, A.add, ["St", "rc"], ["o"])
-        for name, codes, reads, banks in (("to", q, QS, (2, 3, 4, 5)), ("tp", ql, [ql], (6, 7, 0, 1))):
-            for b, k in enumerate(banks):
-                mx(k, "qe%d" % b, 0, codes, ALL, ["qe%d" % b] + reads)
-                act(T[name + "%d" % b][:], ps(k, ALL), ["ps%d" % k], ["ps%d" % k, name + "%d" % b])
-            if r == 0 and name == "to":
-                act(T.dlast[:], T.F[:, 0:48].indirect(T.od[:, 0:16]), ["F0", "F1", "F2", "od"], ["dlast"])
         far, own = T[ll], T[sn]
         SN, LL = [sn + "h0", sn + "h1"], [ll + "h0", ll + "h1"]
-        for h in (0, 1):
+        keys = ["o", "raw0", "raw1", "rawdup", "rawgap"]
+        act(T.Gs[:, 0:HALF], by(T.raw[:, 0:WIN], T.o, (HALF, 2 * HALF)), keys, ["Gs"], func=IDENT, scale=2.0 ** -5, bias=-BASE * 2.0 ** -14)
+        for name in BESIDE[-1][1]:
+            scalar_job(name)
+        vts(T.G[:, 0:HALF], by(T.raw[:, 0:WIN], T.o, (0, HALF)), -BASE / 512.0, 2.0 ** -5, A.add, A.mult, keys, ["G"])
+        for h, name in enumerate(("G", "Gs")):
             a, e = HALF * h, HALF * (h + 1)
-            vts(T.G[:, a:e], by(T.raw[:, 0:WIN], T.o, (a, e)), -BASE / 512.0, 2.0 ** -5, A.add, A.mult,
-                ["o", "raw0", "raw1", "rawdup", "rawgap"], ["G%dh" % h])
-            vscan(T.St[:, a:e], T.dlast[:], T.G[:, a:e], 0.0, A.mult, ["dlast", "G%dh" % h], ["St%dh" % h])
+            vscan(T.St[:, a:e], T.dlast[:], T[name][:, 0:HALF], 0.0, A.mult, ["dlast", name], ["St%dh" % h])
             vts(own[:, 15 * h:15 * h + 15], T.St[:, a + 17:e:17], one_scale, 2.0 ** 14, A.mult, A.mult, ["St%dh" % h, "one_scale"], [SN[h]])
             send(dst, sn, ll, (15 * h, 15 * h + 15), "rl%d%d" % (r, h), [SN[h]])
             arrives(LL[h], "rl%d%d" % (r, h))
         if not last:
-            vcopy(T.G[:, 2 * HALF:RUN], T.G[:, 0:16], ["G0h"], ["Gw"])
+            vcopy(T.Gs[:, HALF:HALF + 16], T.G[:, 0:16], ["G"], ["Gw"])
 
         def own_columns(pick, b, cols):
             keys = SN[0:1] if cols[1] <= ZCUT else SN
             pick(T["zo%d" % b][:, cols[0]:cols[1]], by(T["to%d" % b][:, 0:C], own, cols), ["to%d" % b] + keys, ["zo%d_%d" % (b, cols[1])])
 
         own_columns(vcopy, 0, XH[0])
-        for cols in (ZH[0], (ZCUT, XCUT)):
-            for b in (1, 2):
-                own_columns(act, b, cols)
+        for b in EARLY:
+            own_columns(act, b, XH[0])
         if not last:
-            vscan(T.St[:, 0:RUN], T.dring[:, 0:RUN], T.G[:, 0:RUN], 0.0, A.mult, ["dring", "G0h", "G1h", "Gw"], ["St"])
+            vscan(T.St[:, 0:HALF], T.dring[:, 0:HALF], T.G[:, 0:HALF], 0.0, A.mult, ["dring", "G"], ["St"])
+            vscan(T.St[:, HALF:RUN], T.dring[:, HALF:RUN], T.Gs[:, 0:HALF + 16], 0.0, A.mult, ["dring", "Gs", "Gw"], ["St"])
         if r == 0:
             vtt(T.m2[:, 0:30], T.tai[:], T.tbi[:], A.add, ["tai", "tbi"], ["m2"])
             vtt(T.hn[:, 0:30], T.tbi[:], T.tai[:], A.subtract, ["tai", "tbi"], ["hn"])
         hbanks = ((2, 3, 4, 5), (6, 7, 0, 1))
-        for h, (a, e) in enumerate(ZH):
-            for b in FOUR:
+
+        def far_columns(h, parts):
+            a, e = ZH[h]
+            for b in parts:
                 (act if b < 2 else vcopy)(T.Zp[:, 4 * a + b:4 * e:4], by(T["tp%d" % b][:, 0:C], far, ZH[h]), ["tp%d" % b] + LL[0:h + 1],
                                           ["Zp%d%d" % (h, b)])
-            quant("qz", ZH[h], T.Zp, ["Zp%d%d" % (h, b) for b in FOUR], "qz%d" % h)
+
+        far_columns(0, FOUR)
+        far_columns(1, [2])
+        quant("qz", ZH[0], T.Zp, ["Zp0%d" % b for b in FOUR], "qz0")
+        far_columns(1, [0, 1, 3])
+        quant("qz", ZH[1], T.Zp, ["Zp1%d" % b for b in FOUR], "qz1")
         for h, b in LAYER:
             mx(hbanks[h][b], "wq", 128 * b, "qz", ZH[h], ["wq", "wqs", "qz%d" % h])
         for b in (2, 3):
@@ -434,7 +467,9 @@ def rank_program(g, core, T, topo):
         for h, b in ((0, 0), (0, 1), (1, 0)):
             a, e = ZH[h]
             gcopy(T.H[:, 4 * a + b:4 * e:4], T["hw%d" % b][:, a:e], e - a, ["H%d%d" % (h, b)], ["H0"])
-        own_columns(act, 3, XH[0])
+        for b in (1, 2, 3):
+            if b not in EARLY:
+                own_columns(act, b, XH[0])
         for b in FOUR:
             own_columns(act, b, XH[1])
         state(0, [0, 1])

@@ -14,9 +14,15 @@ BASE = 1055
 DCUT = 512
 TINY = 2.0 ** -100
 BIG = 2.0 ** 20
-LAYER = [(h, b) for h in (0, 1) for b in range(4)]
-BESIDE = ((0, ["rA", "rB"]), (0, ["to0", "to1", "to2"]), (0, ["to3", "tp2"]), (192, ["last", "tp3"]), (HALF, ["tp0", "tp1"]))
-EARLY = (1,)
+LAYER = ((0, 0), (0, 1), (0, 2), (1, 0), (1, 1), (0, 3), (1, 2), (1, 3))
+BESIDE = ((0, ["rA", "rB"]), (224, ["to0"]), (224, ["to1"]), (224, ["to2", "last"]), (HALF, ["to3"]))
+ZP = ((0, 192), (192, 352), (352, 480))
+ZO = "a00 v02 a01 v03 a11 a12 a10 q0 v13 q1 a21 v22 a20 v23 q2"
+HO = "a00 a01 v03 a02 ig00 a12 v11 a10 ig10 v13 v20 a21 iv20 a22 a23 x00"
+XO = "p10 p03 x01 p02 p13 p12 Q p11 x10 x03 x02 V x13 S0 x11 x12 S1 E"
+XL = "Q p03 p02 x01 x03 x02 p13 V p11 p12 S0 x10 E A x12 x11 x13 S1 B"
+PLANAR = 1
+NE = 0
 
 SCRATCH = {}
 
@@ -42,15 +48,13 @@ for _r in range(3):
     _add("ql%ds" % _r, [128, C], "uint8")
     _add("ll%d" % _r, [128, 32], "uint16")
     _add("sn%d" % _r, [128, 32], "uint16")
-for _n in ("qz", "qh"):
+for _n in ("qz0", "qz1", "qz2", "qh"):
     _add(_n, [128, C], CODES)
     _add(_n + "s", [128, C], "uint8")
-for _n in ("X", "Zp", "H"):
+for _n in ("X", "Zp", "H", "Hp"):
     _add(_n, [128, 4 * C], "bfloat16")
 for _b in range(4):
     _add("to%d" % _b, [128, C], "bfloat16")
-    _add("tp%d" % _b, [128, C], "bfloat16")
-    _add("zo%d" % _b, [128, C], "bfloat16")
 for _n in ("hw0", "hw1", "sg", "sv", "xs", "d15"):
     _add(_n, [128, C], "bfloat16")
 for _n in ("raw", "words"):
@@ -74,7 +78,7 @@ _add("labf", [128, 64], "float32")
 _add("lab", [128, 64], "uint16")
 for _n in ("o", "sl"):
     _add(_n, [128, 34], "uint16")
-for _n in ("s0", "l2", "l3"):
+for _n in ("s0", "l0", "l1", "l2", "l3"):
     _add(_n, [128, 32], "uint16")
 for _n in ("sti", "tai", "tbi"):
     _add(_n, [128, 30], "int32")
@@ -94,7 +98,7 @@ for _b in range(8):
 
 LOADS = ["x0", "x1", "u", "st", "ta", "tb", "wc", "ws", "v"]
 SEMAPHORES = ["cv", "ca", "cp", "cg", "out", "left"] + ["ld_" + n for n in LOADS]
-SEMAPHORES += ["rq%d" % r for r in range(3)] + ["rl%d%d" % (r, h) for r in range(3) for h in (0, 1)]
+SEMAPHORES += ["rq%d%d" % (r, h) for r in range(3) for h in range(3)] + ["rl%d" % r for r in range(3)]
 
 
 def rank_program(g, core, T, topo):
@@ -329,9 +333,6 @@ def rank_program(g, core, T, topo):
         dst = T.cores[rank ^ step]
         q, ql, ll, sn, qn = "q%d" % r, "ql%d" % r, "ll%d" % r, "sn%d" % r, "q%d" % (r + 1)
         QS, TS = [q + "h0", q + "h1"], ["t0", "t1"]
-        send(dst, q, ql, ALL, "rq%d" % r, QS, codes=True)
-        send(dst, q + "s", ql + "s", ALL, "rq%d" % r, QS)
-        arrives(ql, "rq%d" % r)
         word_of(1)
         act(T.G0[:, 0:RUN], T.sg[:, 0:C].indirect(T.sl[:, 0:L]), ["sg0", "sg1", "sl"], ["G0"], scale=2.0 ** -17)
         meanwhile()
@@ -350,9 +351,9 @@ def rank_program(g, core, T, topo):
                     gcopy(T.raw[:, DUP:WIN], T.raw[:, 0:2 * C], 2 * C, ["raw0", "raw1"], ["rawdup"])
             elif name[0] == "t":
                 b = int(name[2])
-                codes, reads, k = (q, QS, 2 + b) if name[1] == "o" else (ql, [ql], (6 + b) % 8)
-                mx(k, "qe%d" % b, 0, codes, ALL, ["qe%d" % b] + reads)
-                act(T[name][:], ps(k, ALL), ["ps%d" % k], ["ps%d" % k, name])
+                k, cols = 2 + b, XH[1] if b < NE and r else ALL
+                mx(k, "qe%d" % b, 0, q, cols, ["qe%d" % b] + QS)
+                act(T[name][:, cols[0]:cols[1]], ps(k, cols), ["ps%d" % k], ["ps%d" % k, name])
             elif r == 0:
                 act(T.dlast[:], T.F[:, 0:48].indirect(T.od[:, 0:16]), ["F0", "F1", "F2", "od"], ["dlast"])
 
@@ -388,40 +389,33 @@ def rank_program(g, core, T, topo):
             a, e = HALF * h, HALF * (h + 1)
             vscan(T.St[:, a:e], T.dlast[:], T[name][:, 0:HALF], 0.0, A.mult, ["dlast", name], ["St%dh" % h])
             vts(own[:, 15 * h:15 * h + 15], T.St[:, a + 17:e:17], one_scale, 2.0 ** 14, A.mult, A.mult, ["St%dh" % h, "one_scale"], [SN[h]])
-            send(dst, sn, ll, (15 * h, 15 * h + 15), "rl%d%d" % (r, h), [SN[h]])
-            arrives(LL[h], "rl%d%d" % (r, h))
+        LL = [ll]
+        send(dst, sn, ll, (0, 30), "rl%d" % r, SN)
+        arrives(ll, "rl%d" % r)
+        qz = "qz%d" % r
+        for w in ZO.split():
+            h = int(w[1])
+            a, e = ZP[h]
+            if w[0] == "q":
+                sem = "rq%d%d" % (r, h)
+                quant(qz, ZP[h], T.Zp, ["Z%d%d" % (h, b) for b in FOUR], "qz%d" % h)
+                send(dst, qz, ql, ZP[h], sem, ["qz%d" % h], codes=True)
+                send(dst, qz + "s", ql + "s", ZP[h], sem, ["qz%d" % h])
+                arrives(ql + "_%d" % h, sem)
+            else:
+                b = int(w[2])
+                (act if w[0] == "a" else vcopy)(T.Zp[:, 4 * a + b:4 * e:4], by(T["to%d" % b][:, 0:C], own, ZP[h]),
+                                                ["to%d" % b] + (SN[0:1] if e <= ZCUT else SN), ["Z%d%d" % (h, b)])
         if not last:
             vcopy(T.Gs[:, HALF:HALF + 16], T.G[:, 0:16], ["G"], ["Gw"])
-
-        def own_columns(pick, b, cols):
-            keys = SN[0:1] if cols[1] <= ZCUT else SN
-            pick(T["zo%d" % b][:, cols[0]:cols[1]], by(T["to%d" % b][:, 0:C], own, cols), ["to%d" % b] + keys, ["zo%d_%d" % (b, cols[1])])
-
-        own_columns(vcopy, 0, XH[0])
-        for b in EARLY:
-            own_columns(act, b, XH[0])
-        if not last:
             vscan(T.St[:, 0:HALF], T.dring[:, 0:HALF], T.G[:, 0:HALF], 0.0, A.mult, ["dring", "G"], ["St"])
             vscan(T.St[:, HALF:RUN], T.dring[:, HALF:RUN], T.Gs[:, 0:HALF + 16], 0.0, A.mult, ["dring", "Gs", "Gw"], ["St"])
+        if last:
+            act(T.opb[:, 0:C], by(T.i1[:, 0:C], own, ALL), ["i1"] + SN, ["op0"], func=IDENT, bias=-float(BASE))
         if r == 0:
             vtt(T.m2[:, 0:30], T.tai[:], T.tbi[:], A.add, ["tai", "tbi"], ["m2"])
             vtt(T.hn[:, 0:30], T.tbi[:], T.tai[:], A.subtract, ["tai", "tbi"], ["hn"])
-        hbanks = ((2, 3, 4, 5), (6, 7, 0, 1))
-
-        def far_columns(h, parts):
-            a, e = ZH[h]
-            for b in parts:
-                (act if b < 2 else vcopy)(T.Zp[:, 4 * a + b:4 * e:4], by(T["tp%d" % b][:, 0:C], far, ZH[h]), ["tp%d" % b] + LL[0:h + 1],
-                                          ["Zp%d%d" % (h, b)])
-
-        far_columns(0, FOUR)
-        far_columns(1, [2])
-        quant("qz", ZH[0], T.Zp, ["Zp0%d" % b for b in FOUR], "qz0")
-        far_columns(1, [0, 1, 3])
-        quant("qz", ZH[1], T.Zp, ["Zp1%d" % b for b in FOUR], "qz1")
-        for h, b in LAYER:
-            mx(hbanks[h][b], "wq", 128 * b, "qz", ZH[h], ["wq", "wqs", "qz%d" % h])
-        for b in (2, 3):
+        for b in range(PLANAR, 4):
             vts(T["l%d" % b][:, 0:30], far[:, 0:30], 4, b, A.mult, A.add, LL, ["l%d" % b])
         if last:
             quant("qv", W0, T.vt, ["vt"], "qv")
@@ -430,26 +424,45 @@ def rank_program(g, core, T, topo):
         half_difference()
         if not last:
             first_offsets()
-        HS = ["H0", "H1", "H02", "H12", "H03", "H13"]
+        PIECES = range(len(ZP))
+        HS = ["H%d%d" % (h, b) for h in PIECES for b in FOUR]
 
         def answer(who, h, b):
-            a, e = ZH[h]
-            k, key = "ps%d" % hbanks[h][b], "H%d%d" % (h, b)
-            out = T["hw%d" % b][:, a:e] if b < 2 else T.H[:, 4 * a + b:4 * e:4]
+            a, e = ZP[h]
+            bank = (2 + 4 * h + b) % 8 if h < 2 else 2 + b
+            k = "ps%d" % bank
+            mx(bank, "wq", 128 * b, ql, ZP[h], ["wq", "wqs", ql + "_%d" % h])
+            out, key = (T["hw%d" % b][:, a:e], "P%d%d" % (h, b)) if b < PLANAR else (T.H[:, 4 * a + b:4 * e:4], "H%d%d" % (h, b))
             if who == "a":
-                act(out, ps(hbanks[h][b], ZH[h]), [k], [k, key], scale=0.03125)
+                act(out, ps(bank, ZP[h]), [k], [k, key], scale=0.03125)
             else:
-                vts(out, ps(hbanks[h][b], ZH[h]), 0.03125, None, A.mult, None, [k], [k, key])
+                vts(out, ps(bank, ZP[h]), 0.03125, None, A.mult, None, [k], [k, key])
 
-        def state(h, parts=FOUR):
+        def into_tile(who, h, b):
+            a, e = ZP[h]
+            out, in_, keys = T.H[:, 4 * a + b:4 * e:4], T["hw%d" % b][:, a:e], (["P%d%d" % (h, b)], ["H%d%d" % (h, b)])
+            if who == "g":
+                gcopy(out, in_, e - a, *keys)
+            else:
+                (act if who == "a" else vcopy)(out, in_, *keys)
+
+        ahead = []
+
+        def picked(h, b):
+            if b < PLANAR:
+                return by(T["hw%d" % b][:, 0:C], far, XH[h]), LL + ["P%d%d" % (k, b) for k in PIECES]
+            return by(T.H[:, 0:4 * C], T["l%d" % b], XH[h]), HS + ["l%d" % b]
+
+        def pick_ahead(h, b):
+            (a, e), (src, keys) = XH[h], picked(h, b)
+            act(T.Hp[:, 4 * a + b:4 * e:4], src, keys, ["Hp%d%d" % (h, b)])
+            ahead.append((h, b))
+
+        def state(h, b):
             a, e = XH[h]
-            for b in parts:
-                if b < 2:
-                    picked, keys = by(T["hw%d" % b][:, 0:C], far, XH[h]), LL + ["H0%d" % b, "H1%d" % b]
-                else:
-                    picked, keys = by(T.H[:, 0:4 * C], T["l%d" % b], XH[h]), HS + ["l%d" % b]
-                vtt(T.X[:, 4 * a + b:4 * e:4], picked, T["zo%d" % b][:, a:e], A.add, keys + ["zo%d_%d" % (b, e)], ["X%d%d" % (h, b)])
-            return ["X%d%d" % (h, b) for b in FOUR]
+            part, parts = (slice(4 * a, 4 * e), FOUR) if b == 4 else (slice(4 * a + b, 4 * e, 4), [b])
+            src, keys = (T.Hp[:, part], ["Hp%d%d" % (h, c) for c in parts]) if b == 4 or (h, b) in ahead else picked(h, b)
+            vtt(T.X[:, part], src, T.Zp[:, part], A.add, keys + ["Z%d%d" % (k, c) for k in PIECES for c in parts], ["X%d%d" % (h, c) for c in parts])
 
         def outputs(h, reads):
             (a, e), key = XH[h], qn + "h%d" % h
@@ -462,37 +475,41 @@ def rank_program(g, core, T, topo):
                     dma("s", T.osc[4 * k:4 * k + 4, :], T[qn + "s"][32 * k:32 * k + 4, :], "out", reads=[qn + "h0", key])
             dma("s", T.y[:, a:e], T.yb[:, a:e], "out", reads=["y%d" % h])
 
-        for h, b in LAYER:
-            answer("v" if (h, b) == (1, 0) else "a", h, b)
-        for h, b in ((0, 0), (0, 1), (1, 0)):
-            a, e = ZH[h]
-            gcopy(T.H[:, 4 * a + b:4 * e:4], T["hw%d" % b][:, a:e], e - a, ["H%d%d" % (h, b)], ["H0"])
-        for b in (1, 2, 3):
-            if b not in EARLY:
-                own_columns(act, b, XH[0])
-        for b in FOUR:
-            own_columns(act, b, XH[1])
-        state(0, [0, 1])
-        vcopy(T.H[:, 4 * ZCUT + 1:4 * C:4], T.hw1[:, ZCUT:C], ["H11"], ["H1"])
-        quant("qh", ALL, T.H, HS, "qh")
-        mx(2, "qr", 0, "qh", ALL, ["qr", "qrs", "qh"])
-        act(T.sv[:], ps(2, ALL), ["ps2"], ["ps2", "sv"], func=SIGN, bias=TINY, scale=-1.0)
-        if r == 0:
-            gcopy(T.d16[:, 0:16], T.F[:, 0:16], 16, ["F0"], ["d16"])
-            repeat("g", "d16", 16, 512)
-        first = state(0, [2, 3])
-        if not last:
-            scored(qn, 0, T.X, first)
-            scored(qn, 1, T.X, state(1))
-            exchange(lambda: word_of(0))
-        else:
-            act(T.opb[:, 0:C], by(T.i1[:, 0:C], own, ALL), ["i1"] + SN, ["op0"], func=IDENT, bias=-float(BASE))
-            outputs(0, first)
-            exchange()
-            act(T.opb[:, C:2 * C], T.i1[:, 0:C].indirect(la), ["i1", "lab"], ["op1"], func=IDENT, bias=-float(BASE))
-            act(T.opb[:, 2 * C:3 * C], T.i1[:, 0:C].indirect(lb), ["i1", "lab"], ["op2"], func=IDENT, bias=-float(BASE))
-            dma("a", T.op[:], T.opb[0:128:16, :], "out", reads=["op0", "op1", "op2"])
-            outputs(1, state(1))
+        for w in (HO + " " + (XL if last else XO)).split():
+            if w[0] in "av":
+                answer(w[0], int(w[1]), int(w[2]))
+            elif w[0] == "i":
+                into_tile(w[1], int(w[2]), int(w[3]))
+            elif w[0] == "p":
+                pick_ahead(int(w[1]), int(w[2]))
+            elif w[0] == "x":
+                state(int(w[1]), int(w[2]))
+            elif w == "Q":
+                quant("qh", ALL, T.H, HS, "qh")
+                mx(2, "qr", 0, "qh", ALL, ["qr", "qrs", "qh"])
+                if r == 0:
+                    gcopy(T.d16[:, 0:16], T.F[:, 0:16], 16, ["F0"], ["d16"])
+                    repeat("g", "d16", 16, 512)
+            elif w == "V":
+                act(T.sv[:], ps(2, ALL), ["ps2"], ["ps2", "sv"], func=SIGN, bias=TINY, scale=-1.0)
+            elif w[0] == "S":
+                h = int(w[1])
+                if last:
+                    outputs(h, ["X%d%d" % (h, b) for b in FOUR])
+                else:
+                    scored(qn, h, T.X, ["X%d%d" % (h, b) for b in FOUR])
+                    for b in range(NE if h == 0 else 0):
+                        mx(3 + b, "qe%d" % b, 0, qn, XH[0], ["qe%d" % b, qn + "h0"])
+                        act(T["to%d" % b][:, 0:XCUT], ps(3 + b, XH[0]), ["ps%d" % (3 + b)], ["ps%d" % (3 + b), "to%d" % b])
+            elif w == "E":
+                exchange((lambda: None) if last else (lambda: word_of(0)))
+            elif w == "A":
+                act(T.opb[:, C:2 * C], T.i1[:, 0:C].indirect(la), ["i1", "lab"], ["op1"], func=IDENT, bias=-float(BASE))
+            elif w == "Av":
+                vts(T.opb[:, C:2 * C], T.i1[:, 0:C].indirect(la), -float(BASE), None, A.add, None, ["i1", "lab"], ["op1"])
+            else:
+                act(T.opb[:, 2 * C:3 * C], T.i1[:, 0:C].indirect(lb), ["i1", "lab"], ["op2"], func=IDENT, bias=-float(BASE))
+                dma("a", T.op[:], T.opb[0:128:16, :], "out", reads=["op0", "op1", "op2"])
     for s in sorted(total):
         if know["g"].get(s, 0) < total[s]:
             g.wait_ge(T.sem[s], total[s])

@@ -11,11 +11,12 @@ STAGES = 5
 XCUT = 352
 ZCUT = 224
 BASE = 1055
-DCUT = 512
+SIZE = 272.5
+MID = 270.5
 TINY = 2.0 ** -100
 BIG = 2.0 ** 20
 LAYER = ((0, 0), (0, 1), (0, 2), (1, 0), (1, 1), (0, 3), (1, 2), (1, 3))
-BESIDE = ((0, ["rA", "rB"]), (224, ["to0"]), (224, ["to1"]), (224, ["to2", "last"]), (HALF, ["to3"]))
+BESIDE = ((256, ["dup"]), (256, ["to0"]), (256, ["to1"]), (256, ["last", "to2"]), (0, ["to3"]))
 ZP = ((0, 192), (192, 352), (352, 480))
 ZO = "a00 v02 a01 v03 a11 a12 a10 q0 v13 q1 a21 v22 a20 v23 q2"
 HO = "a00 a01 v03 a02 ig00 a12 v11 a10 ig10 v13 v20 a21 iv20 a22 a23 x00"
@@ -57,15 +58,14 @@ for _b in range(4):
     _add("to%d" % _b, [128, C], "bfloat16")
 for _n in ("hw0", "hw1", "sg", "sv", "xs", "d15"):
     _add(_n, [128, C], "bfloat16")
-for _n in ("raw", "words"):
-    _add(_n, [128, WIN], "float32")
-for _n in ("t", "i1", "i5", "row", "rowscan"):
+_add("words", [128, WIN], "float32")
+for _n in ("t", "i5", "i1", "row", "rowscan"):
     _add(_n, [128, C], "float32")
 for _n in ("G", "St"):
     _add(_n, [128, 544], "float16")
 for _n in ("G0", "St0", "dring"):
     _add(_n, [128, 544], "bfloat16")
-_add("Gs", [128, HALF + 16], "float32")
+_add("Gs", [128, 544], "float16")
 _add("d16", [128, 512], "bfloat16")
 _add("dlast", [128, HALF], "bfloat16")
 _add("one", [128, 544], "bfloat16")
@@ -109,6 +109,7 @@ def rank_program(g, core, T, topo):
     COPY = ActivationFunctionType.Copy
     SIGN = ActivationFunctionType.Sign
     IDENT = ActivationFunctionType.Identity
+    ABS = ActivationFunctionType.Abs
     eng = {"v": g.vector, "a": g.scalar, "p": g.tensor, "g": g, "s": g.sync}
     total = {}
     know = {q: {} for q in eng}
@@ -208,7 +209,8 @@ def rank_program(g, core, T, topo):
     ZH = ((0, ZCUT), (ZCUT, C))
     FOUR = range(4)
     la, lb = T.lab[:, 0:30], T.lab[:, 32:62]
-    own_scale, pair_scale, run_scale, one_scale = T.rc[:, 0:1], T.rc[:, 1:2], T.ks[:, 15:16], T.col[:, 1:2]
+    own_scale, pair_scale, one_scale = T.rc[:, 0:1], T.rc[:, 1:2], T.col[:, 1:2]
+    sign_scale, ring_scale, last_scale = T.rc[:, 2:3], T.rc[:, 3:4], T.col[:, 5:6]
 
     dma("s", T.ut[:], T.u[:], "ld_u", writes=["ut"])
     for h, (a, b) in enumerate(XH):
@@ -255,26 +257,34 @@ def rank_program(g, core, T, topo):
     vcopy(T.qr[:, 0:128].bitcast(dt.uint32), T.qu[:, 0:128].bitcast(dt.uint32).indirect(T.ip16[:, 0:8]), ["qu", "ip16"], ["qr"])
     twice(4)
     op("v", lambda: g.vector.reciprocal(T.rc[:, 0:2], T.ks[:, 15:17]), ["ks"], ["rc"])
+    vts(sign_scale, own_scale, 2.0 ** -16, None, A.mult, None, ["rc"], ["sign_scale"])
     for k in (0, 1):
         act(T.words[:, 2 * C + 544 * k:2 * C + 544 * (k + 1)], T.one[:], ["one"], ["wordgap"])
-    act(T.i5[:], T.i1[:], ["i1"], ["i5"], scale=2.0 ** -9)
+    act(T.i5[:], T.i1[:], ["i1"], ["i5"], func=COPY, scale=2.0 ** -9, bias=(SIZE - BASE) / 512.0)
     act(T.row[:], by(T.i1[:, 0:C], T.s0, ALL), ["i1", "s0"], ["row"])
     act(T.qrs[:, 0:128], T.qus[:, 0:128].indirect(T.ip16[:, 0:8]), ["qu", "ip16"], ["qrs"])
     op("g", lambda: g.affine_select(T.eye[:], T.one[:, 0:528], [[-1, 528]], A.is_equal, 0.0, 3, 4), ["one"], ["eye"])
     repeat("g", "dring", 32, 544)
     vcopy(T.G[:, RUN:544], T.labf[:, 0:16], ["labf0"], ["Gtail"])
-    later = [lambda: first_offsets()]
-    later += [lambda b=b: op("v", lambda: g.vector.quantize_mx(T["qe%d" % b][:], T["qe%ds" % b][:], T.eye[:, 3 - b:515 - b]), ["eye"], ["qe%d" % b])
-              for b in FOUR]
-    later += [
+    def unpacker(b):
+        op("v", lambda: g.vector.quantize_mx(T["qe%d" % b][:], T["qe%ds" % b][:], T.eye[:, 3 - b:515 - b]), ["eye"], ["qe%d" % b])
+
+    later = [
+        lambda: first_offsets(),
+        lambda: unpacker(0),
         lambda: vts(T.F[:, 16:32], T.dm[:, 0:16], 0, None, A.not_equal, None, ["dm"], ["F1"]),
         lambda: vts(T.mb[:, 0:16], T.dm[:, 0:16], 1, BIG - 1.0, A.is_equal, A.mult, ["dm"], ["mb"]),
+        lambda: unpacker(1),
         lambda: vts(T.F[:, 32:48], T.F[:, 16:32], 1.0 - BIG, BIG, A.mult, A.add, ["F1"], ["F2"]),
         lambda: vtt(T.F[:, 0:16], T.mb[:, 0:16], T.F[:, 16:32], A.add, ["mb", "F1"], ["F0"]),
+        lambda: unpacker(2),
         lambda: vts(T.col[:, 3:4], T.dm[:, 0:1], 15, 16.0, A.is_equal, A.mult, ["dm"], ["col3"]),
         lambda: vts(T.km[:], T.ki[:], 15, None, A.bitwise_and, None, ["ki"], ["km"]),
         lambda: vts(T.col[:, 4:5], T.col[:, 0:1], 32.0, T.col[:, 3:4], A.mult, A.add, ["first", "col3"], ["col4"]),
         lambda: vts(T.od[:], T.km[:], T.col[:, 4:5], None, A.add, None, ["km", "col4"], ["od"]),
+        lambda: unpacker(3),
+        lambda: vts(last_scale, one_scale, 2.0 ** 14, None, A.mult, None, ["one_scale"], ["last_scale"]),
+        lambda: vts(ring_scale, own_scale, 0.5, None, A.mult, None, ["rc"], ["ring_scale"]),
     ]
 
     def meanwhile():
@@ -282,7 +292,7 @@ def rank_program(g, core, T, topo):
             later.pop(0)()
 
     def first_offsets():
-        vts(T.s2[:, 0:L], T.sl[:, 0:L], 0.25, run_scale, A.add, A.mult, ["sl", "ks"], ["s2"])
+        vts(T.s2[:, 0:L], T.sl[:, 0:L], 2.0, 0.5, A.mult, A.add, ["sl"], ["s2"])
 
     def half_difference():
         vts(T.hs[:, 0:30], T.hn[:, 0:30], one_scale, None, A.mult, None, ["hn", "one_scale"], ["hs"])
@@ -308,15 +318,14 @@ def rank_program(g, core, T, topo):
 
     def word_of(h):
         a, e = XH[h]
-        vscan(T.t[:, a:e], T.sg[:, a:e], T.i5[:, a:e], 2.0, A.min, ["sg%d" % h, "i5"], ["t%d" % h])
+        op("v", lambda: g.vector.tensor_tensor_scan(T.t[:, a:e], T.i5[:, a:e], T.sg[:, a:e], 0.0, A.max, A.mult), ["sg%d" % h, "i5"], ["t%d" % h])
 
     def exchange(between=lambda: None):
         vscan(T.xs[:], T.d16[:, 0:C], T.sv[:], 0.0, A.mult, ["d16", "sv"], ["xs"])
         vtt(T.hn[:, 0:30], T.xs[:, 15:C:16], T.hs[:, 0:30], A.mult, ["xs", "hs"], ["hn"])
-        vtt(T.labf[:, 0:30], T.m2[:, 0:30], T.hn[:, 0:30], A.subtract, ["m2", "hn"], ["labf0"])
-        vtt(T.labf[:, 32:62], T.m2[:, 0:30], T.hn[:, 0:30], A.add, ["m2", "hn"], ["labf1"])
         between()
-        vts(T.lab[:, 0:62], T.labf[:, 0:62], 0.5, None, A.mult, None, ["labf0", "labf1"], ["lab"])
+        vtt(la, T.m2[:, 0:30], T.hn[:, 0:30], A.subtract, ["m2", "hn"], ["lab"])
+        vtt(lb, T.m2[:, 0:30], T.hn[:, 0:30], A.add, ["m2", "hn"], ["lab"])
 
     scored("q0", 0, T.xt, ["xt0"])
     scored("q0", 1, T.xt, ["xt1"])
@@ -334,61 +343,50 @@ def rank_program(g, core, T, topo):
         q, ql, ll, sn, qn = "q%d" % r, "ql%d" % r, "ll%d" % r, "sn%d" % r, "q%d" % (r + 1)
         QS, TS = [q + "h0", q + "h1"], ["t0", "t1"]
         word_of(1)
-        act(T.G0[:, 0:RUN], T.sg[:, 0:C].indirect(T.sl[:, 0:L]), ["sg0", "sg1", "sl"], ["G0"], scale=2.0 ** -17)
+        act(T.G0[:, 0:RUN], T.sg[:, 0:C].indirect(T.sl[:, 0:L]), ["sg0", "sg1", "sl", "sign_scale"], ["G0"], func=IDENT, scale=sign_scale)
         meanwhile()
-        vcopy(T.words[:, 0:2 * C:2], T.t[:, 0:C].indirect(la), TS + ["lab"], ["words0"])
-        act(T.words[:, 1:2 * C:2], T.t[:, 0:C].indirect(lb), TS + ["lab"], ["words1"])
-        act(T.words[:, DUP:DUP + DCUT], T.words[:, 0:DCUT], ["words0", "words1"], ["dup0"])
-        gcopy(T.words[:, DUP + DCUT:WIN], T.words[:, DCUT:2 * C], 2 * C - DCUT, ["words0", "words1"], ["dup1"])
+        vcopy(T.words[:, DUP:WIN:2], T.t[:, 0:C].indirect(la), TS + ["lab"], ["words0"])
+        act(T.words[:, DUP + 1:WIN:2], T.t[:, 0:C].indirect(lb), TS + ["lab"], ["words1"])
+        gcopy(T.words[:, 2 * C - 2::-2], T.words[:, DUP:WIN:2], C, ["words0"], ["dup0"])
 
         def scalar_job(name):
-            if name[0] == "r":
-                h = "AB".index(name[1])
-                act(T.raw[:, h:2 * C:2], T.i5[:, 0:C].indirect((la, lb)[h]), ["i5", "lab"], ["raw%d" % h])
-                if h and r == 0:
-                    op("g", lambda: g.iota(T.raw[:, 2 * C:DUP], [[0, DUP - 2 * C]], 0, 0, allow_small_or_imprecise_dtypes=True), [], ["rawgap"])
-                if h:
-                    gcopy(T.raw[:, DUP:WIN], T.raw[:, 0:2 * C], 2 * C, ["raw0", "raw1"], ["rawdup"])
+            if name == "dup":
+                act(T.words[:, 2 * C - 1::-2], T.words[:, DUP + 1:WIN:2], ["words1"], ["dup1"])
             elif name[0] == "t":
                 b = int(name[2])
                 k, cols = 2 + b, XH[1] if b < NE and r else ALL
                 mx(k, "qe%d" % b, 0, q, cols, ["qe%d" % b] + QS)
-                act(T[name][:, cols[0]:cols[1]], ps(k, cols), ["ps%d" % k], ["ps%d" % k, name])
+                (vcopy if b == 3 else act)(T[name][:, cols[0]:cols[1]], ps(k, cols), ["ps%d" % k], ["ps%d" % k, name])
             elif r == 0:
                 act(T.dlast[:], T.F[:, 0:48].indirect(T.od[:, 0:16]), ["F0", "F1", "F2", "od"], ["dlast"])
 
         vscan(T.St0[:, 0:RUN], T.dring[:, 0:RUN], T.G0[:, 1:RUN + 1], 0.0, A.mult, ["dring", "G0", "G0tail"], ["St0"])
         meanwhile()
-        vtt(T.sm[:, 0:L], T.St0[:, 15:RUN:16], T.s2[:, 0:L], A.add, ["St0", "s2"], ["sm"])
-        meanwhile()
-        vts(T.o[:, 0:L], T.sm[:, 0:L], own_scale, 2.0, A.mult, A.mult, ["sm", "rc"], ["o"])
+        vtt(T.o[:, 0:L], T.St0[:, 15:RUN:16], T.s2[:, 0:L], A.add, ["St0", "s2"], ["o"])
         for k, (n, jobs) in enumerate(BESIDE[:-1]):
-            win, keys = (2 * C, []) if k == 0 else (WIN, ["dup0", "dup1", "wordgap"])
+            win, keys = (T.words[:, DUP:WIN], []) if k == 0 else (T.words[:, 0:WIN], ["dup0", "dup1", "wordgap"])
             keys += ["o", "words0", "words1"]
             meanwhile()
-            if n:
-                act(T.Gs[:, 0:n + 16], by(T.words[:, 0:win], T.o, (0, n + 16)), keys, ["Gs"], func=IDENT, scale=2.0 ** -5, bias=-2.0 ** -4)
+            act(T.G[:, n:RUN], by(win, T.o, (n, RUN)), keys, ["Ga"], func=IDENT, scale=2.0 ** -5, bias=MID * 2.0 ** -14)
             for name in jobs:
                 scalar_job(name)
-            vts(T.G[:, n:RUN], by(T.words[:, 0:win], T.o, (n, RUN)), -2.0, 2.0 ** -5, A.add, A.mult, keys, ["G"])
+            vts(T.G[:, 0:n], by(win, T.o, (0, n)), MID / 512.0, 2.0 ** -5, A.add, A.mult, keys, ["G"])
             meanwhile()
-            a = n + 1 if n else 0
-            vscan(T.St[:, a:RUN + 2], T.dring[:, a:RUN + 2], T.G[:, a:RUN + 2], 0.0, A.mult, ["dring", "G", "Gtail"], ["St"])
-            if n:
-                vscan(T.St[:, 0:a], T.dring[:, 0:a], T.Gs[:, 0:a], 0.0, A.mult, ["dring", "Gs"], ["St"])
+            vscan(T.St[:, 0:RUN + 2], T.dring[:, 0:RUN + 2], T.G[:, 0:RUN + 2], 0.0, A.mult, ["dring", "G", "Ga", "Gtail"], ["St"])
             meanwhile()
             vts(T.o[:, 0:L], T.St[:, 16:RUN + 1:16], pair_scale, 962.25, A.mult, A.add, ["St", "rc"], ["o"])
         far, own = T[ll], T[sn]
         SN, LL = [sn + "h0", sn + "h1"], [ll + "h0", ll + "h1"]
-        keys = ["o", "raw0", "raw1", "rawdup", "rawgap"]
-        act(T.Gs[:, 0:HALF], by(T.raw[:, 0:WIN], T.o, (HALF, 2 * HALF)), keys, ["Gs"], func=IDENT, scale=2.0 ** -5, bias=-BASE * 2.0 ** -14)
+        keys = ["o", "words0", "words1", "dup0", "dup1", "wordgap"]
+        for h, name in enumerate(("G", "Gs")):
+            act(T[name][:, 0:HALF], by(T.words[:, 0:WIN], T.o, (h * HALF, (h + 1) * HALF)), keys, [name], func=ABS, scale=2.0 ** -5)
+        meanwhile()
         for name in BESIDE[-1][1]:
             scalar_job(name)
-        vts(T.G[:, 0:HALF], by(T.raw[:, 0:WIN], T.o, (0, HALF)), -BASE / 512.0, 2.0 ** -5, A.add, A.mult, keys, ["G"])
         for h, name in enumerate(("G", "Gs")):
             a, e = HALF * h, HALF * (h + 1)
             vscan(T.St[:, a:e], T.dlast[:], T[name][:, 0:HALF], 0.0, A.mult, ["dlast", name], ["St%dh" % h])
-            vts(own[:, 15 * h:15 * h + 15], T.St[:, a + 17:e:17], one_scale, 2.0 ** 14, A.mult, A.mult, ["St%dh" % h, "one_scale"], [SN[h]])
+            vts(own[:, 15 * h:15 * h + 15], T.St[:, a + 17:e:17], last_scale, -SIZE, A.mult, A.add, ["St%dh" % h, "last_scale"], [SN[h]])
         LL = [ll]
         send(dst, sn, ll, (0, 30), "rl%d" % r, SN)
         arrives(ll, "rl%d" % r)
@@ -413,14 +411,16 @@ def rank_program(g, core, T, topo):
         if last:
             act(T.opb[:, 0:C], by(T.i1[:, 0:C], own, ALL), ["i1"] + SN, ["op0"], func=IDENT, bias=-float(BASE))
         if r == 0:
-            vtt(T.m2[:, 0:30], T.tai[:], T.tbi[:], A.add, ["tai", "tbi"], ["m2"])
-            vtt(T.hn[:, 0:30], T.tbi[:], T.tai[:], A.subtract, ["tai", "tbi"], ["hn"])
+            vtt(T.labf[:, 0:30], T.tai[:], T.tbi[:], A.add, ["tai", "tbi"], ["labf0"])
+            vtt(T.labf[:, 32:62], T.tbi[:], T.tai[:], A.subtract, ["tai", "tbi"], ["labf1"])
+            vts(T.m2[:, 0:30], T.labf[:, 0:30], 0.5, None, A.mult, None, ["labf0"], ["m2"])
+            vts(T.hn[:, 0:30], T.labf[:, 32:62], 0.5, None, A.mult, None, ["labf1"], ["hn"])
         for b in range(PLANAR, 4):
             vts(T["l%d" % b][:, 0:30], far[:, 0:30], 4, b, A.mult, A.add, LL, ["l%d" % b])
         if last:
             quant("qv", W0, T.vt, ["vt"], "qv")
         else:
-            vts(T.sl[:, 0:L], T.St[:, 15:RUN:16], own_scale, 0.5, A.mult, A.mult, ["St", "rc"], ["sl"])
+            vts(T.sl[:, 0:L], T.St[:, 15:RUN:16], ring_scale, -SIZE - 0.25, A.mult, A.add, ["St", "ring_scale"], ["sl"])
         half_difference()
         if not last:
             first_offsets()

from concourse.mybir import dt, AluOpType, ActivationFunctionType

C = 480
L = 33
RUN = 16 * L
HALF = 256
DUP = 2048
WIN = DUP + 2 * C
STEP = [1, 2, 3]
STAGES = 5
XCUT = 352
ZCUT = 224
BASE = 1055
SIZE = 272.5
MID = 270.5
TINY = 2.0 ** -100
BIG = 2.0 ** 20
LAYER = ((0, 0), (0, 1), (0, 2), (1, 0), (1, 1), (0, 3), (1, 2), (1, 3))
BESIDE = ((256, ["dup"]), (256, ["to0"]), (256, ["to1"]), (256, ["last", "to2"]), (0, ["to3"]))
ZP = ((0, 192), (192, 352), (352, 480))
ZO = "a00 v02 a01 v03 a11 a12 a10 q0 v13 q1 a21 v22 a20 v23 q2"
HO = "a00 a01 v03 a02 ig00 a12 v11 a10 ig10 v13 v20 a21 iv20 a22 a23 x00"
XO = "p10 p03 x01 p02 p13 p12 Q p11 x10 x03 x02 V x13 S0 x11 x12 S1 E"
XL = "Q p03 p02 x01 x03 x02 p13 V p11 p12 S0 x10 E A x12 x11 x13 S1 B"
PLANAR = 1
NE = 0

SCRATCH = {}


def _add(name, shape, dtype, where="sbuf"):
    SCRATCH[name] = (where, shape, dtype)


CODES = "float8_e4m3fn_x4"
_add("xt", [128, 4 * C], "bfloat16")
for _n in ("ut", "vt"):
    _add(_n, [128, 512], "bfloat16")
for _n in ("qu", "qr", "qv", "qe0", "qe1", "qe2", "qe3"):
    _add(_n, [128, 128], CODES)
    _add(_n + "s", [128, 128], "uint8")
_add("wq", [128, 512], CODES)
_add("wqs", [128, 512], "uint8")
for _r in range(4):
    _add("q%d" % _r, [128, C], CODES)
    _add("q%ds" % _r, [128, C], "uint8")
for _r in range(3):
    _add("ql%d" % _r, [128, C], CODES)
    _add("ql%ds" % _r, [128, C], "uint8")
    _add("ll%d" % _r, [128, 32], "uint16")
    _add("sn%d" % _r, [128, 32], "uint16")
for _n in ("qz0", "qz1", "qz2", "qh"):
    _add(_n, [128, C], CODES)
    _add(_n + "s", [128, C], "uint8")
for _n in ("X", "Zp", "H", "Hp"):
    _add(_n, [128, 4 * C], "bfloat16")
for _b in range(4):
    _add("to%d" % _b, [128, C], "bfloat16")
for _n in ("hw0", "hw1", "sg", "sv", "xs", "d15"):
    _add(_n, [128, C], "bfloat16")
_add("words", [128, WIN], "float32")
for _n in ("t", "i5", "i1", "row", "rowscan"):
    _add(_n, [128, C], "float32")
for _n in ("G", "St"):
    _add(_n, [128, 544], "float16")
for _n in ("G0", "St0", "dring"):
    _add(_n, [128, 544], "bfloat16")
_add("Gs", [128, 544], "float16")
_add("d16", [128, 512], "bfloat16")
_add("dlast", [128, HALF], "bfloat16")
_add("one", [128, 544], "bfloat16")
_add("eye", [128, 528], "bfloat16")
for _n in ("m2", "hs", "hn", "ma", "mb", "mc", "md", "oh", "ks"):
    _add(_n, [128, 32], "float32")
for _n in ("sm", "s2", "F"):
    _add(_n, [128, 48], "float32")
_add("labf", [128, 64], "float32")
_add("lab", [128, 64], "uint16")
for _n in ("o", "sl"):
    _add(_n, [128, 34], "uint16")
for _n in ("s0", "l0", "l1", "l2", "l3"):
    _add(_n, [128, 32], "uint16")
for _n in ("sti", "tai", "tbi"):
    _add(_n, [128, 30], "int32")
for _n in ("di", "dm", "dj", "dn"):
    _add(_n, [128, 32], "int32")
for _n in ("ki", "km"):
    _add(_n, [128, 16], "int32")
_add("od", [128, 16], "uint16")
_add("ip", [128, 8], "int32")
_add("ip16", [128, 8], "uint16")
for _n in ("rc", "col"):
    _add(_n, [128, 8], "float32")
_add("yb", [128, C], "float32")
_add("opb", [128, 3 * C], "float32")
for _b in range(8):
    _add("ps%d" % _b, [128, 512], "float32", "psum")

LOADS = ["x0", "x1", "u", "st", "ta", "tb", "wc", "ws", "v"]
SEMAPHORES = ["cv", "ca", "cp", "cg", "out", "left"] + ["ld_" + n for n in LOADS]
SEMAPHORES += ["rq%d%d" % (r, h) for r in range(3) for h in range(3)] + ["rl%d" % r for r in range(3)]


def rank_program(g, core, T, topo):
    rank = T.rank_of(core)
    if rank is None:
        return
    A = AluOpType
    COPY = ActivationFunctionType.Copy
    SIGN = ActivationFunctionType.Sign
    IDENT = ActivationFunctionType.Identity
    ABS = ActivationFunctionType.Abs
    eng = {"v": g.vector, "a": g.scalar, "p": g.tensor, "g": g, "s": g.sync}
    total = {}
    know = {q: {} for q in eng}
    wrote = {}
    read = {}

    def wait(q, toks):
        toks = [t for t in toks if know[q].get(t[1], 0) < t[2]]
        keep = []
        for i, t in enumerate(toks):
            if not any(j != i and o[3].get(t[1], 0) >= t[2] and (o[1:3] != t[1:3] or j < i) for j, o in enumerate(toks)):
                keep.append(t)
        for t in keep:
            eng[q].wait_ge(T.sem[t[1]], t[2])
            for s, n in t[3].items():
                know[q][s] = max(know[q].get(s, 0), n)

    def before(q, reads, writes):
        toks = [wrote[k] for k in reads if k in wrote]
        for k in writes:
            if k in wrote and (wrote[k][0] != q):
                toks.append(wrote[k])
            toks += [t for t in read.get(k, {}).values() if t[0] != q]
        wait(q, toks)

    def after(q, who, sem, n, reads, writes):
        total[sem] = total.get(sem, 0) + n
        clk = dict(know[q])
        clk[sem] = total[sem]
        tok = (who, sem, total[sem], clk)
        for k in reads:
            read.setdefault(k, {})[who + sem] = tok
        for k in writes:
            wrote[k] = tok
            read[k] = {}

    def op(q, call, reads, writes):
        before(q, reads, writes)
        call().then_inc(T.sem["c" + q], 1)
        after(q, q, "c" + q, 1, reads, writes)

    def dma(q, out, in_, sem, reads=(), writes=()):
        before(q, reads, writes)
        eng[q].dma_start(out, in_).then_inc(T.sem[sem], 16)
        after(q, "dma", sem, 16, reads, writes)

    def vcopy(out, in_, reads, writes):
        op("v", lambda: g.vector.tensor_copy(out, in_), reads, writes)

    def vts(out, in_, s1, s2, op0, op1, reads, writes):
        if op1 is None:
            op("v", lambda: g.vector.tensor_scalar(out, in_, s1, None, op0), reads, writes)
        else:
            op("v", lambda: g.vector.tensor_scalar(out, in_, s1, s2, op0, op1), reads, writes)

    def vtt(out, a, b, o, reads, writes):
        op("v", lambda: g.vector.tensor_tensor(out, a, b, o), reads, writes)

    def vscan(out, d0, d1, first, op0, reads, writes):
        op("v", lambda: g.vector.tensor_tensor_scan(out, d0, d1, first, op0, A.add), reads, writes)

    def vset(ap, c, writes):
        op("v", lambda: g.vector.memset(ap, c), [], writes)

    def act(out, in_, reads, writes, func=COPY, **more):
        op("a", lambda: g.scalar.activation(out, in_, func, **more), reads, writes)

    def gcopy(out, in_, n, reads, writes):
        op("g", lambda: g.affine_select(out, in_, [[1, n]], A.is_ge, 0.0, 0, 0), reads, writes)

    def repeat(who, name, n, upto):
        for k in range(5):
            m = min(n << k, upto - (n << k))
            out, in_ = T[name][:, n << k:(n << k) + m], T[name][:, 0:m]
            if who == "g":
                gcopy(out, in_, m, [name], [name])
            else:
                act(out, in_, [name], [name])

    def quant(name, cols, tile, reads, key):
        a, b = cols
        op("v", lambda: g.vector.quantize_mx(T[name][:, a:b], T[name + "s"][:, a:b], tile[:, 4 * a:4 * b]), reads, [key])

    def mx(bank, w, w0, x, cols, reads):
        a, b = cols
        op("p", lambda: g.tensor.matmul_mx(T["ps%d" % bank][:, 0:b - a], T[w][:, w0:w0 + 128], T[w + "s"][:, w0:w0 + 128],
                                           T[x][:, a:b], T[x + "s"][:, a:b], True, True), reads, ["ps%d" % bank])

    def ps(bank, cols):
        return T["ps%d" % bank][:, 0:cols[1] - cols[0]]

    def by(win, lst, cols):
        return win.indirect(lst[:, cols[0] // 16:cols[1] // 16])

    ALL, W0 = (0, C), (0, 128)
    XH = ((0, XCUT), (XCUT, C))
    ZH = ((0, ZCUT), (ZCUT, C))
    FOUR = range(4)
    la, lb = T.lab[:, 0:30], T.lab[:, 32:62]
    own_scale, pair_scale, one_scale = T.rc[:, 0:1], T.rc[:, 1:2], T.col[:, 1:2]
    sign_scale, ring_scale, last_scale = T.rc[:, 2:3], T.rc[:, 3:4], T.col[:, 5:6]

    dma("s", T.ut[:], T.u[:], "ld_u", writes=["ut"])
    for h, (a, b) in enumerate(XH):
        dma("s", T.xt[:, 4 * a:4 * b], T.x[:, 4 * a:4 * b], "ld_x%d" % h, writes=["xt%d" % h])
    dma("a", T.sti[:], T.st[:], "ld_st", writes=["sti"])
    dma("a", T.tai[:], T.ta[:], "ld_ta", writes=["tai"])
    dma("a", T.tbi[:], T.tb[:], "ld_tb", writes=["tbi"])
    dma("s", T.wq[:].bitcast(dt.uint8), T.wc[:], "ld_wc", reads=["xt0"], writes=["wq"])
    dma("s", T.wqs[:], T.ws[:], "ld_ws", writes=["wqs"])
    dma("s", T.vt[:], T.v[:], "ld_v", writes=["vt"])

    vset(T.one[:], 1.0, ["one"])
    op("g", lambda: g.iota(T.di[:], [[1, 32]], 128, -1), [], ["di"])
    op("g", lambda: g.iota(T.ip[:], [[16, 8]], 0, 0), [], ["ip"])
    op("g", lambda: g.iota(T.i1[:], [[1, C]], BASE, 0, allow_small_or_imprecise_dtypes=True), [], ["i1"])
    op("g", lambda: g.iota(T.ki[:], [[15, 16]], 127, 1), [], ["ki"])
    vts(T.dm[:], T.di[:], 15, None, A.bitwise_and, None, ["di"], ["dm"])
    vcopy(T.ip16[:], T.ip[:], ["ip"], ["ip16"])
    vts(T.col[:, 0:1], T.dm[:, 0:1], 0, None, A.is_equal, None, ["dm"], ["first"])
    vts(T.col[:, 2:3], T.dm[:, 0:1], 1, 2.0 ** -20 - 1.0, A.not_equal, A.mult, ["dm"], ["col2"])
    vts(T.dj[:], T.di[:], T.col[:, 0:1], None, A.subtract, None, ["di", "first"], ["dj"])
    vts(T.col[:, 1:2], T.col[:, 2:3], 1.0, None, A.add, None, ["col2"], ["one_scale"])
    vts(T.dn[:], T.dj[:], 15, None, A.bitwise_and, None, ["dj"], ["dn"])
    vset(T.labf[:], 0.0, ["labf0", "labf1"])
    vts(T.mc[:], T.dn[:], 0, None, A.not_equal, None, ["dn"], ["mc"])
    vts(T.md[:], T.dn[:], 1, BIG - 1.0, A.is_equal, A.mult, ["dn"], ["md"])
    vts(T.ma[:], T.dn[:], 1, 2047.0, A.is_equal, A.mult, ["dn"], ["ma"])
    vtt(T.d15[:, 0:15], T.md[:, 1:16], T.mc[:, 1:16], A.add, ["md", "mc"], ["d15"])

    def twice(k):
        vcopy(T.d15[:, 15 << k:30 << k], T.d15[:, 0:15 << k], ["d15"], ["d15"])

    vts(T.mb[:], T.dn[:], 2, 511.0, A.is_equal, A.mult, ["dn"], ["mb"])
    twice(0)
    vtt(T.ma[:], T.ma[:], T.mb[:], A.add, ["ma", "mb"], ["ma"])
    vts(T.oh[:], T.dn[:], 0, 2.0 ** -15, A.is_equal, A.mult, ["dn"], ["oh"])
    vtt(T.dring[:, 0:32], T.ma[:], T.mc[:], A.add, ["ma", "mc"], ["dring"])
    twice(1)
    vscan(T.ks[:], T.dring[:, 0:32], T.oh[:], 0.0, A.mult, ["dring", "oh"], ["ks"])
    vcopy(T.s0[:, 0:30], T.sti[:], ["sti"], ["s0"])
    twice(2)
    quant("qu", W0, T.ut, ["ut"], "qu")
    twice(3)
    vcopy(T.qr[:, 0:128].bitcast(dt.uint32), T.qu[:, 0:128].bitcast(dt.uint32).indirect(T.ip16[:, 0:8]), ["qu", "ip16"], ["qr"])
    twice(4)
    op("v", lambda: g.vector.reciprocal(T.rc[:, 0:2], T.ks[:, 15:17]), ["ks"], ["rc"])
    vts(sign_scale, own_scale, 2.0 ** -16, None, A.mult, None, ["rc"], ["sign_scale"])
    for k in (0, 1):
        act(T.words[:, 2 * C + 544 * k:2 * C + 544 * (k + 1)], T.one[:], ["one"], ["wordgap"])
    act(T.i5[:], T.i1[:], ["i1"], ["i5"], func=COPY, scale=2.0 ** -9, bias=(SIZE - BASE) / 512.0)
    act(T.row[:], by(T.i1[:, 0:C], T.s0, ALL), ["i1", "s0"], ["row"])
    act(T.qrs[:, 0:128], T.qus[:, 0:128].indirect(T.ip16[:, 0:8]), ["qu", "ip16"], ["qrs"])
    op("g", lambda: g.affine_select(T.eye[:], T.one[:, 0:528], [[-1, 528]], A.is_equal, 0.0, 3, 4), ["one"], ["eye"])
    repeat("g", "dring", 32, 544)
    vcopy(T.G[:, RUN:544], T.labf[:, 0:16], ["labf0"], ["Gtail"])
    def unpacker(b):
        op("v", lambda: g.vector.quantize_mx(T["qe%d" % b][:], T["qe%ds" % b][:], T.eye[:, 3 - b:515 - b]), ["eye"], ["qe%d" % b])

    later = [
        lambda: first_offsets(),
        lambda: unpacker(0),
        lambda: vts(T.F[:, 16:32], T.dm[:, 0:16], 0, None, A.not_equal, None, ["dm"], ["F1"]),
        lambda: vts(T.mb[:, 0:16], T.dm[:, 0:16], 1, BIG - 1.0, A.is_equal, A.mult, ["dm"], ["mb"]),
        lambda: unpacker(1),
        lambda: vts(T.F[:, 32:48], T.F[:, 16:32], 1.0 - BIG, BIG, A.mult, A.add, ["F1"], ["F2"]),
        lambda: vtt(T.F[:, 0:16], T.mb[:, 0:16], T.F[:, 16:32], A.add, ["mb", "F1"], ["F0"]),
        lambda: unpacker(2),
        lambda: vts(T.col[:, 3:4], T.dm[:, 0:1], 15, 16.0, A.is_equal, A.mult, ["dm"], ["col3"]),
        lambda: vts(T.km[:], T.ki[:], 15, None, A.bitwise_and, None, ["ki"], ["km"]),
        lambda: vts(T.col[:, 4:5], T.col[:, 0:1], 32.0, T.col[:, 3:4], A.mult, A.add, ["first", "col3"], ["col4"]),
        lambda: vts(T.od[:], T.km[:], T.col[:, 4:5], None, A.add, None, ["km", "col4"], ["od"]),
        lambda: unpacker(3),
        lambda: vts(last_scale, one_scale, 2.0 ** 14, None, A.mult, None, ["one_scale"], ["last_scale"]),
        lambda: vts(ring_scale, own_scale, 0.5, None, A.mult, None, ["rc"], ["ring_scale"]),
    ]

    def meanwhile():
        if later:
            later.pop(0)()

    def first_offsets():
        vts(T.s2[:, 0:L], T.sl[:, 0:L], 2.0, 0.5, A.mult, A.add, ["sl"], ["s2"])

    def half_difference():
        vts(T.hs[:, 0:30], T.hn[:, 0:30], one_scale, None, A.mult, None, ["hn", "one_scale"], ["hs"])

    def send(dst, name, land, cols, sem, reads, codes=False):
        rid, pid = topo.addr(dst)[:2]
        before("g", reads, [])
        n = len(topo.engines(core, dst))
        src, out = T[name][:, cols[0]:cols[1]], T[land][:, cols[0]:cols[1]]
        if codes:
            src, out = src.bitcast(dt.uint8), out.bitcast(dt.uint8)
        g.remote_dma(out, src, T.sem[sem], T.sem.left, pid, rid, topo.mask(core, dst))
        total["left"] = total.get("left", 0) + n
        total[sem] = total.get(sem, 0) + n

    def arrives(key, sem):
        wrote[key] = ("far", sem, total[sem], {sem: total[sem]})

    def scored(q, h, tile, reads):
        quant(q, XH[h], tile, reads, q + "h%d" % h)
        mx(h, "qr", 0, q, XH[h], ["qr", "qrs", q + "h%d" % h])
        act(T.sg[:, XH[h][0]:XH[h][1]], ps(h, XH[h]), ["ps%d" % h], ["ps%d" % h, "sg%d" % h], func=SIGN, bias=-TINY)

    def word_of(h):
        a, e = XH[h]
        op("v", lambda: g.vector.tensor_tensor_scan(T.t[:, a:e], T.i5[:, a:e], T.sg[:, a:e], 0.0, A.max, A.mult), ["sg%d" % h, "i5"], ["t%d" % h])

    def exchange(between=lambda: None):
        vscan(T.xs[:], T.d16[:, 0:C], T.sv[:], 0.0, A.mult, ["d16", "sv"], ["xs"])
        vtt(T.hn[:, 0:30], T.xs[:, 15:C:16], T.hs[:, 0:30], A.mult, ["xs", "hs"], ["hn"])
        between()
        vtt(la, T.m2[:, 0:30], T.hn[:, 0:30], A.subtract, ["m2", "hn"], ["lab"])
        vtt(lb, T.m2[:, 0:30], T.hn[:, 0:30], A.add, ["m2", "hn"], ["lab"])

    scored("q0", 0, T.xt, ["xt0"])
    scored("q0", 1, T.xt, ["xt1"])
    vscan(T.rowscan[:], T.d15[:], T.row[:], 0.0, A.mult, ["d15", "row"], ["rowscan"])
    vcopy(la, T.tai[:], ["tai"], ["lab"])
    vts(T.sl[:, 0:32], T.rowscan[:, 14:C:15], one_scale, -float(BASE), A.mult, A.add, ["rowscan", "one_scale"], ["sl"])
    vts(T.sl[:, 32:33], T.rowscan[:, 14:15], one_scale, -float(BASE), A.mult, A.add, ["rowscan", "one_scale"], ["sl"])
    vcopy(lb, T.tbi[:], ["tbi"], ["lab"])
    vset(T.G0[:, RUN:544], 0.0, ["G0tail"])
    word_of(0)

    for r, step in enumerate(STEP):
        last = r == len(STEP) - 1
        dst = T.cores[rank ^ step]
        q, ql, ll, sn, qn = "q%d" % r, "ql%d" % r, "ll%d" % r, "sn%d" % r, "q%d" % (r + 1)
        QS, TS = [q + "h0", q + "h1"], ["t0", "t1"]
        word_of(1)
        act(T.G0[:, 0:RUN], T.sg[:, 0:C].indirect(T.sl[:, 0:L]), ["sg0", "sg1", "sl", "sign_scale"], ["G0"], func=IDENT, scale=sign_scale)
        meanwhile()
        vcopy(T.words[:, DUP:WIN:2], T.t[:, 0:C].indirect(la), TS + ["lab"], ["words0"])
        act(T.words[:, DUP + 1:WIN:2], T.t[:, 0:C].indirect(lb), TS + ["lab"], ["words1"])
        gcopy(T.words[:, 2 * C - 2::-2], T.words[:, DUP:WIN:2], C, ["words0"], ["dup0"])

        def scalar_job(name):
            if name == "dup":
                act(T.words[:, 2 * C - 1::-2], T.words[:, DUP + 1:WIN:2], ["words1"], ["dup1"])
            elif name[0] == "t":
                b = int(name[2])
                k, cols = 2 + b, XH[1] if b < NE and r else ALL
                mx(k, "qe%d" % b, 0, q, cols, ["qe%d" % b] + QS)
                (vcopy if b == 3 else act)(T[name][:, cols[0]:cols[1]], ps(k, cols), ["ps%d" % k], ["ps%d" % k, name])
            elif r == 0:
                act(T.dlast[:], T.F[:, 0:48].indirect(T.od[:, 0:16]), ["F0", "F1", "F2", "od"], ["dlast"])

        vscan(T.St0[:, 0:RUN], T.dring[:, 0:RUN], T.G0[:, 1:RUN + 1], 0.0, A.mult, ["dring", "G0", "G0tail"], ["St0"])
        meanwhile()
        vtt(T.o[:, 0:L], T.St0[:, 15:RUN:16], T.s2[:, 0:L], A.add, ["St0", "s2"], ["o"])
        for k, (n, jobs) in enumerate(BESIDE[:-1]):
            win, keys = (T.words[:, DUP:WIN], []) if k == 0 else (T.words[:, 0:WIN], ["dup0", "dup1", "wordgap"])
            keys += ["o", "words0", "words1"]
            meanwhile()
            act(T.G[:, n:RUN], by(win, T.o, (n, RUN)), keys, ["Ga"], func=IDENT, scale=2.0 ** -5, bias=MID * 2.0 ** -14)
            for name in jobs:
                scalar_job(name)
            vts(T.G[:, 0:n], by(win, T.o, (0, n)), MID / 512.0, 2.0 ** -5, A.add, A.mult, keys, ["G"])
            meanwhile()
            vscan(T.St[:, 0:RUN + 2], T.dring[:, 0:RUN + 2], T.G[:, 0:RUN + 2], 0.0, A.mult, ["dring", "G", "Ga", "Gtail"], ["St"])
            meanwhile()
            vts(T.o[:, 0:L], T.St[:, 16:RUN + 1:16], pair_scale, 962.25, A.mult, A.add, ["St", "rc"], ["o"])
        far, own = T[ll], T[sn]
        SN, LL = [sn + "h0", sn + "h1"], [ll + "h0", ll + "h1"]
        keys = ["o", "words0", "words1", "dup0", "dup1", "wordgap"]
        for h, name in enumerate(("G", "Gs")):
            act(T[name][:, 0:HALF], by(T.words[:, 0:WIN], T.o, (h * HALF, (h + 1) * HALF)), keys, [name], func=ABS, scale=2.0 ** -5)
        meanwhile()
        for name in BESIDE[-1][1]:
            scalar_job(name)
        for h, name in enumerate(("G", "Gs")):
            a, e = HALF * h, HALF * (h + 1)
            vscan(T.St[:, a:e], T.dlast[:], T[name][:, 0:HALF], 0.0, A.mult, ["dlast", name], ["St%dh" % h])
            vts(own[:, 15 * h:15 * h + 15], T.St[:, a + 17:e:17], last_scale, -SIZE, A.mult, A.add, ["St%dh" % h, "last_scale"], [SN[h]])
        LL = [ll]
        send(dst, sn, ll, (0, 30), "rl%d" % r, SN)
        arrives(ll, "rl%d" % r)
        qz = "qz%d" % r
        for w in ZO.split():
            h = int(w[1])
            a, e = ZP[h]
            if w[0] == "q":
                sem = "rq%d%d" % (r, h)
                quant(qz, ZP[h], T.Zp, ["Z%d%d" % (h, b) for b in FOUR], "qz%d" % h)
                send(dst, qz, ql, ZP[h], sem, ["qz%d" % h], codes=True)
                send(dst, qz + "s", ql + "s", ZP[h], sem, ["qz%d" % h])
                arrives(ql + "_%d" % h, sem)
            else:
                b = int(w[2])
                (act if w[0] == "a" else vcopy)(T.Zp[:, 4 * a + b:4 * e:4], by(T["to%d" % b][:, 0:C], own, ZP[h]),
                                                ["to%d" % b] + (SN[0:1] if e <= ZCUT else SN), ["Z%d%d" % (h, b)])
        if not last:
            vcopy(T.Gs[:, HALF:HALF + 16], T.G[:, 0:16], ["G"], ["Gw"])
            vscan(T.St[:, 0:HALF], T.dring[:, 0:HALF], T.G[:, 0:HALF], 0.0, A.mult, ["dring", "G"], ["St"])
            vscan(T.St[:, HALF:RUN], T.dring[:, HALF:RUN], T.Gs[:, 0:HALF + 16], 0.0, A.mult, ["dring", "Gs", "Gw"], ["St"])
        if last:
            act(T.opb[:, 0:C], by(T.i1[:, 0:C], own, ALL), ["i1"] + SN, ["op0"], func=IDENT, bias=-float(BASE))
        if r == 0:
            vtt(T.labf[:, 0:30], T.tai[:], T.tbi[:], A.add, ["tai", "tbi"], ["labf0"])
            vtt(T.labf[:, 32:62], T.tbi[:], T.tai[:], A.subtract, ["tai", "tbi"], ["labf1"])
            vts(T.m2[:, 0:30], T.labf[:, 0:30], 0.5, None, A.mult, None, ["labf0"], ["m2"])
            vts(T.hn[:, 0:30], T.labf[:, 32:62], 0.5, None, A.mult, None, ["labf1"], ["hn"])
        for b in range(PLANAR, 4):
            vts(T["l%d" % b][:, 0:30], far[:, 0:30], 4, b, A.mult, A.add, LL, ["l%d" % b])
        if last:
            quant("qv", W0, T.vt, ["vt"], "qv")
        else:
            vts(T.sl[:, 0:L], T.St[:, 15:RUN:16], ring_scale, -SIZE - 0.25, A.mult, A.add, ["St", "ring_scale"], ["sl"])
        half_difference()
        if not last:
            first_offsets()
        PIECES = range(len(ZP))
        HS = ["H%d%d" % (h, b) for h in PIECES for b in FOUR]

        def answer(who, h, b):
            a, e = ZP[h]
            bank = (2 + 4 * h + b) % 8 if h < 2 else 2 + b
            k = "ps%d" % bank
            mx(bank, "wq", 128 * b, ql, ZP[h], ["wq", "wqs", ql + "_%d" % h])
            out, key = (T["hw%d" % b][:, a:e], "P%d%d" % (h, b)) if b < PLANAR else (T.H[:, 4 * a + b:4 * e:4], "H%d%d" % (h, b))
            if who == "a":
                act(out, ps(bank, ZP[h]), [k], [k, key], scale=0.03125)
            else:
                vts(out, ps(bank, ZP[h]), 0.03125, None, A.mult, None, [k], [k, key])

        def into_tile(who, h, b):
            a, e = ZP[h]
            out, in_, keys = T.H[:, 4 * a + b:4 * e:4], T["hw%d" % b][:, a:e], (["P%d%d" % (h, b)], ["H%d%d" % (h, b)])
            if who == "g":
                gcopy(out, in_, e - a, *keys)
            else:
                (act if who == "a" else vcopy)(out, in_, *keys)

        ahead = []

        def picked(h, b):
            if b < PLANAR:
                return by(T["hw%d" % b][:, 0:C], far, XH[h]), LL + ["P%d%d" % (k, b) for k in PIECES]
            return by(T.H[:, 0:4 * C], T["l%d" % b], XH[h]), HS + ["l%d" % b]

        def pick_ahead(h, b):
            (a, e), (src, keys) = XH[h], picked(h, b)
            act(T.Hp[:, 4 * a + b:4 * e:4], src, keys, ["Hp%d%d" % (h, b)])
            ahead.append((h, b))

        def state(h, b):
            a, e = XH[h]
            part, parts = (slice(4 * a, 4 * e), FOUR) if b == 4 else (slice(4 * a + b, 4 * e, 4), [b])
            src, keys = (T.Hp[:, part], ["Hp%d%d" % (h, c) for c in parts]) if b == 4 or (h, b) in ahead else picked(h, b)
            vtt(T.X[:, part], src, T.Zp[:, part], A.add, keys + ["Z%d%d" % (k, c) for k in PIECES for c in parts], ["X%d%d" % (h, c) for c in parts])

        def outputs(h, reads):
            (a, e), key = XH[h], qn + "h%d" % h
            quant(qn, XH[h], T.X, reads, key)
            dma("s", T.oc[:, 4 * a:4 * e], T[qn][:, a:e].bitcast(dt.uint8), "out", reads=[key])
            mx(h, "qv", 0, qn, XH[h], ["qv", key])
            (vcopy if h else act)(T.yb[:, a:e], ps(h, XH[h]), ["ps%d" % h], ["ps%d" % h, "y%d" % h])
            if h == 1:
                for k in FOUR:
                    dma("s", T.osc[4 * k:4 * k + 4, :], T[qn + "s"][32 * k:32 * k + 4, :], "out", reads=[qn + "h0", key])
            dma("s", T.y[:, a:e], T.yb[:, a:e], "out", reads=["y%d" % h])

        for w in (HO + " " + (XL if last else XO)).split():
            if w[0] in "av":
                answer(w[0], int(w[1]), int(w[2]))
            elif w[0] == "i":
                into_tile(w[1], int(w[2]), int(w[3]))
            elif w[0] == "p":
                pick_ahead(int(w[1]), int(w[2]))
            elif w[0] == "x":
                state(int(w[1]), int(w[2]))
            elif w == "Q":
                quant("qh", ALL, T.H, HS, "qh")
                mx(2, "qr", 0, "qh", ALL, ["qr", "qrs", "qh"])
                if r == 0:
                    gcopy(T.d16[:, 0:16], T.F[:, 0:16], 16, ["F0"], ["d16"])
                    repeat("g", "d16", 16, 512)
            elif w == "V":
                act(T.sv[:], ps(2, ALL), ["ps2"], ["ps2", "sv"], func=SIGN, bias=TINY, scale=-1.0)
            elif w[0] == "S":
                h = int(w[1])
                if last:
                    outputs(h, ["X%d%d" % (h, b) for b in FOUR])
                else:
                    scored(qn, h, T.X, ["X%d%d" % (h, b) for b in FOUR])
                    for b in range(NE if h == 0 else 0):
                        mx(3 + b, "qe%d" % b, 0, qn, XH[0], ["qe%d" % b, qn + "h0"])
                        act(T["to%d" % b][:, 0:XCUT], ps(3 + b, XH[0]), ["ps%d" % (3 + b)], ["ps%d" % (3 + b), "to%d" % b])
            elif w == "E":
                exchange((lambda: None) if last else (lambda: word_of(0)))
            elif w == "A":
                act(T.opb[:, C:2 * C], T.i1[:, 0:C].indirect(la), ["i1", "lab"], ["op1"], func=IDENT, bias=-float(BASE))
            elif w == "Av":
                vts(T.opb[:, C:2 * C], T.i1[:, 0:C].indirect(la), -float(BASE), None, A.add, None, ["i1", "lab"], ["op1"])
            else:
                act(T.opb[:, 2 * C:3 * C], T.i1[:, 0:C].indirect(lb), ["i1", "lab"], ["op2"], func=IDENT, bias=-float(BASE))
                dma("a", T.op[:], T.opb[0:128:16, :], "out", reads=["op0", "op1", "op2"])
    for s in sorted(total):
        if know["g"].get(s, 0) < total[s]:
            g.wait_ge(T.sem[s], total[s])
